import numpy as np
import ml_dtypes


def mxq(x, axis, fmt="e4m3"):
    dtype, down = {"e4m3": (ml_dtypes.float8_e4m3fn, 7), "e5m2": (ml_dtypes.float8_e5m2, 14)}[fmt]
    v = np.moveaxis(np.asarray(x, np.float32).astype(ml_dtypes.bfloat16).astype(np.float64), axis, -1)
    blocks = v.reshape(v.shape[:-1] + (-1, 32))
    amax = np.abs(blocks).max(-1, keepdims=True)
    byte = np.maximum(np.where(amax > 0, np.frexp(amax)[1] - 1 + 127, 0) - down, 1)
    scale = np.exp2(byte - 127.0)
    codes = (blocks / scale).astype(np.float32).astype(dtype).astype(np.float64)
    return np.moveaxis((codes * scale).reshape(v.shape), -1, axis)


WIDE = False


def mx_kscale(k):
    if not WIDE:
        return np.ones(k)
    levels = np.array([10, -10, 5, -5, 0])
    if k % 512:
        return np.exp2(np.random.permutation(np.resize(levels, k // 32))).repeat(32)
    a = np.empty((k // 512, 16))
    for p in range(k // 512):
        a[p, :8] = np.random.permutation(np.resize(levels, 8))
        for g in range(8):
            far = levels[np.abs(levels - a[p, g]) >= 10]
            a[p, g + 8] = far[np.random.randint(len(far))]
    return np.exp2(a.ravel()).repeat(32)


BF16 = ml_dtypes.bfloat16


def bf(x):
    return np.asarray(x, np.float32).astype(BF16)


def f64(x):
    return np.asarray(x).astype(np.float64)


E2M1 = np.array([0.0, 0.5, 1.0, 1.5, 2.0, 3.0, 4.0, 6.0, -0.0, -0.5, -1.0, -1.5, -2.0, -3.0, -4.0, -6.0])


def pack_weight(w, fmt):
    k, n = w.shape
    w = f64(bf(w)).reshape(k // 32, 32, n)
    amax = np.abs(w).max(1)
    if fmt == "e4m3":
        byte = np.frexp(amax)[1] - 1 + 127 - 7
    else:
        mant, ex = np.frexp(amax / 6.0)
        byte = np.where(mant > 0.5, ex, ex - 1) + 127
    byte = np.clip(np.where(amax > 0, byte, 1), 1, 254)
    scaled = (w * np.exp2(127.0 - byte)[:, None, :]).reshape(k, n).astype(np.float32)
    by_word = np.ascontiguousarray(scaled.reshape(k // 512, 128, 4, n).transpose(0, 1, 3, 2))
    if fmt == "e4m3":
        words = by_word.astype(ml_dtypes.float8_e4m3fn).view(np.uint8)
    else:
        c = by_word.astype(ml_dtypes.float4_e2m1fn).view(np.uint8) & 0xF
        words = c[..., 0::2] | (c[..., 1::2] << 4)
    return np.ascontiguousarray(words), np.ascontiguousarray(byte.astype(np.uint8).reshape(k // 512, 16, n))


def unpack_weight(words, scales, fmt):
    g, p, n, _ = words.shape
    if fmt == "e4m3":
        vals = np.ascontiguousarray(words).view(ml_dtypes.float8_e4m3fn).astype(np.float64)
    else:
        nib = np.empty((g, p, n, 4), np.uint8)
        nib[..., 0::2] = words & 0xF
        nib[..., 1::2] = words >> 4
        vals = E2M1[nib]
    vals = vals * np.repeat(np.exp2(scales.astype(np.float64) - 127.0), 8, axis=1)[..., None]
    return vals.transpose(0, 1, 3, 2).reshape(g * 512, n)
def pack4(w):
    words, scales = pack_weight(w, "e2m1")
    return words.reshape(words.shape[0], 128, -1), scales


def unpack4(words, scales):
    return unpack_weight(words.reshape(words.shape[0], 128, -1, 2), scales, "e2m1")


M, K, F, P, N = 1024, 1024, 1024, 3, 1024

BIAS = 0.4


def draw0():
    s, t = mx_kscale(K), mx_kscale(F)
    w = np.random.standard_normal((K, P * F)) / np.sqrt(K) / s[:, None] * np.tile(t, P)
    v = np.random.standard_normal((F, N)) / np.sqrt(F) / t[:, None]
    w_words, w_scales = pack4(w)
    v_words, v_scales = pack_weight(v, "e4m3")
    return {"x": bf(np.random.standard_normal((M, K)) * s),
            "w_words": w_words,
            "w_scales": w_scales,
            "b": bf(BIAS * np.random.standard_normal((P, F)) * t),
            "v_words": v_words,
            "v_scales": v_scales,
            "c": bf(BIAS * np.random.standard_normal(N))}


def core(x, w_words, w_scales, b, v_words, v_scales, c):
    z = mxq(f64(x), 1, "e4m3") @ unpack4(w_words, w_scales)
    z = z.reshape(M, P, F) + f64(b)
    h = z.max(axis=1)
    y = mxq(h, 1, "e4m3") @ unpack_weight(v_words, v_scales, "e4m3")
    return y + f64(c)


def e4m3fn_bytes(y):
    return np.clip(np.asarray(y, np.float64), -448.0, 448.0).astype(np.float32).astype(ml_dtypes.float8_e4m3fn).view(np.uint8)


def e4m3fn_values(b):
    return np.asarray(b, np.uint8).view(ml_dtypes.float8_e4m3fn).astype(np.float64)


def setup_inputs():
    d = draw0()
    x0 = np.asarray(d['x']).astype(np.float64)
    s = (np.max(np.abs(x0), axis=(0,), keepdims=True) / 448.0).astype(np.float32)
    out = {}
    for k, v in d.items():
        if k == 'x':
            out['x_bytes'] = e4m3fn_bytes(x0 / s.astype(np.float64))
            out['x_scale'] = s
        else:
            out[k] = v
    return out


def reference(x_bytes, x_scale, w_words, w_scales, b, v_words, v_scales, c):
    return core(e4m3fn_values(x_bytes) * x_scale.astype(np.float64), w_words, w_scales, b, v_words, v_scales, c)

@@ -1,0 +1,375 @@
+from contextlib import ExitStack
+
+import concourse.mybir as mybir
+from concourse.masks import make_identity
+
+M, K, F, PIECES, N = 1024, 1024, 1024, 3, 1024
+FLOPS = 2 * M * K * PIECES * F + 2 * M * F * N
+
+F32 = mybir.dt.float32
+BF16 = mybir.dt.bfloat16
+I32 = mybir.dt.int32
+U32 = mybir.dt.uint32
+U8 = mybir.dt.uint8
+E4M3 = mybir.dt.float8_e4m3fn
+FP8X4 = mybir.dt.float8_e4m3fn_x4
+FP4X4 = mybir.dt.float4_e2m1fn_x4
+ALU = mybir.AluOpType
+ACT = mybir.ActivationFunctionType
+
+P = 128
+ROWS = 512
+HALVES = M // ROWS
+TILES = F // P
+
+
+def tile_maxout_then_linear_f7_kernel(tc, x_bytes, x_scale, w_words, w_scales, b, v_words, v_scales, c, out):
+    nc = tc.nc
+    with ExitStack() as ctx:
+        keep = ctx.enter_context(tc.tile_pool(name="keep", bufs=1))
+        stage = ctx.enter_context(tc.tile_pool(name="stage", bufs=4))
+        deep = ctx.enter_context(tc.tile_pool(name="deep", bufs=8))
+        zpool = ctx.enter_context(tc.psum_pool(name="zpool", bufs=6))
+        tpool = ctx.enter_context(tc.psum_pool(name="tpool", bufs=2))
+        ctx.enter_context(tc.manual_schedule())
+
+        sc = keep.tile([P, 2, 2, 2], F32, name="sc")
+        nc.scalar.dma_start(
+            out=sc[:].rearrange("p g u e -> p g (u e)"), in_=x_scale.rearrange("o (g p t) -> p (o g) t", g=2, t=4)
+        )
+        ident = keep.tile([P, P], F32, name="ident")
+        make_identity(nc, ident[:])
+        braw = keep.tile([P, P], BF16, name="braw")
+        warm = keep.tile([P, 512], BF16, name="warm")
+        nc.vector.memset(warm[:], 0.0)
+        nc.gpsimd.memset(braw[:], 0.0)
+        ws = keep.tile([P, 2, PIECES * F], U8, name="ws", align_bytes=64)
+        nc.vector.memset(ws[:].rearrange("p g n -> p (g n)").bitcast(U32), 0)
+        vs = keep.tile([P, 2, N], U8, name="vs", align_bytes=64)
+        nc.gpsimd.memset(vs[:].rearrange("p g n -> p (g n)").bitcast(U32), 0)
+
+        xb4 = [keep.tile([P, 4, K], U8, name="xb%d" % i, align_bytes=64) for i in range(2)]
+        xb = [xb4[i // 4][:, i % 4] for i in range(8)]
+        wt = [keep.tile([P, 2, PIECES, 512], U8, name="wt%d" % q, align_bytes=64) for q in range(4)]
+        vt = keep.tile([P, 2, 4 * N], U8, name="vt", align_bytes=64)
+        cb = keep.tile([P, N], BF16, name="cb")
+
+        def load_x(lo, hi):
+            nc.sync.dma_start(
+                out=xb4[lo // 4][:, lo % 4 : lo % 4 + hi - lo], in_=x_bytes[lo * P : hi * P, :].rearrange("(r p) k -> p r k", p=P)
+            )
+
+        def load_w(q):
+            for g in range(2):
+                nc.sync.dma_start(
+                    out=wt[q][:, g].bitcast(I32),
+                    in_=w_words[g].rearrange("p (j n) -> p j n", j=PIECES)[:, :, q * 512 : (q + 1) * 512].bitcast(I32),
+                )
+
+        def load_scales(tile, scales):
+            for q in range(4):
+                nc.sync.dma_start(
+                    out=tile[32 * q : 32 * q + 4].bitcast(I32),
+                    in_=scales[:, 4 * q : 4 * q + 4, :].rearrange("g q n -> q g n").bitcast(I32),
+                )
+
+        load_x(0, 1)
+        load_x(1, 2)
+        load_x(2, 4)
+        load_scales(ws, w_scales)
+        load_w(0)
+        nc.sync.dma_start(out=braw[0:24, :], in_=b.rearrange("j (t p) -> (j t) p", p=P))
+        load_x(4, 6)
+        load_w(1)
+        load_x(6, 8)
+        load_w(2)
+        load_w(3)
+        for g in range(2):
+            nc.sync.dma_start(out=vt[:, g].bitcast(I32), in_=v_words[g].rearrange("p n t -> p (n t)").bitcast(I32))
+        load_scales(vs, v_scales)
+        nc.sync.dma_start(out=cb[:], in_=c.partition_broadcast(P))
+
+        xc = [keep.tile([P, 2, ROWS], U32, name="xc%d" % i, align_bytes=64) for i in range(HALVES)]
+        xcs = [keep.tile([P, 2, ROWS], U8, name="xcs%d" % i, align_bytes=64) for i in range(HALVES)]
+        hc = [keep.tile([P, 2, ROWS], U32, name="hc%d" % i, align_bytes=64) for i in range(HALVES)]
+        hcs = [keep.tile([P, 2, ROWS], U8, name="hcs%d" % i, align_bytes=64) for i in range(HALVES)]
+        hp = [[keep.tile([P, 4, ROWS], BF16, name="hp%d%d" % (i, g), align_bytes=64) for g in range(2)] for i in range(HALVES)]
+        bias = keep.tile([P, 24], F32, name="bias")
+        bf32 = keep.tile([P, P], F32, name="bf32")
+
+        xw, xt, xg = {}, {}, {}
+
+        def x_cast(i, engine):
+            w = deep.tile([P, K], BF16, name="xw", align_bytes=64)
+            if engine == "v":
+                for g in range(2):
+                    nc.vector.tensor_copy(out=w[:, g * 512 : (g + 1) * 512], in_=xb[i][:, g * 512 : (g + 1) * 512].bitcast(E4M3))
+            else:
+                nc.scalar.copy(out=w[:], in_=xb[i].bitcast(E4M3))
+            xw[i] = w
+
+        def x_turn(i):
+            words = xw[i][:].bitcast(F32)
+            t = tpool.tile([P, 2, 2, P], F32, name="xt")
+            for g in range(2):
+                for u in range(2):
+                    nc.tensor.transpose(t[:, g, u, :], words[:, 256 * g + u : 256 * (g + 1) : 2], ident[:])
+            xt[i] = t
+
+        def x_out(i, g):
+            if g == 0:
+                a = stage.tile([P, 2, P, 4], BF16, name="xg", align_bytes=64)
+                xg[i] = a
+            a = xg[i]
+            if True:
+                nc.vector.tensor_tensor(
+                    out=a[:, g].rearrange("p m (u e) -> p m u e", u=2),
+                    in0=xt[i][:, g].bitcast(BF16).rearrange("p u (m e) -> p m u e", e=2),
+                    in1=sc[:, g].unsqueeze(1).to_broadcast([P, P, 2, 2]),
+                    op=ALU.mult,
+                )
+
+        def x_quant(i, g):
+            half, r = i // 4, i % 4
+            if True:
+                nc.vector.quantize_mx(
+                    out=xc[half][:, g, r * P : (r + 1) * P].bitcast(FP8X4),
+                    scales=xcs[half][:, g, r * P : (r + 1) * P],
+                    in_=xg[i][:, g].rearrange("p m t -> p (m t)"),
+                )
+
+        zs, us, vv, hh = {}, {}, {}, {}
+
+        def z_new(s):
+            zs[s] = []
+            for j in range(PIECES):
+                z = zpool.tile([P, ROWS], F32, name="z")
+                zs[s].append(z)
+
+        def z_mul(s, lo, hi):
+            half, T = s // TILES, s % TILES
+            col = (T % 2) * 256
+            for j in range(PIECES):
+                for g in range(2):
+                    nc.tensor.matmul_mx(
+                        out=zs[s][j][:, lo:hi],
+                        lhsT=wt[T // 2][:, g, j, col : col + 256].bitcast(FP4X4),
+                        lhsT_scale=ws[:, g, j * F + T * P : j * F + (T + 1) * P],
+                        rhs=xc[half][:, g, lo:hi].bitcast(FP8X4),
+                        rhs_scale=xcs[half][:, g, lo:hi],
+                        start=(g == 0),
+                        stop=(g == 1),
+                    )
+
+        def u_out(s, pieces=2):
+            T = s % TILES
+            us[s] = []
+            for j in range(pieces):
+                u = stage.tile([P, ROWS], BF16, name="u%d" % j, align_bytes=64)
+                nc.scalar.activation(out=u[:], in_=zs[s][j][:], func=ACT.Identity, bias=bias[:, 8 * j + T : 8 * j + T + 1])
+                us[s].append(u)
+
+        def v_max(s):
+            v = stage.tile([P, ROWS], BF16, name="v", align_bytes=64)
+            nc.vector.tensor_tensor(out=v[:], in0=us[s][0][:], in1=us[s][1][:], op=ALU.max)
+            vv[s] = v
+
+        def h_max(s):
+            T = s % TILES
+            h = stage.tile([P, ROWS], BF16, name="h", align_bytes=64)
+            hh[s] = h
+            if len(us[s]) == 3:
+                nc.vector.tensor_tensor(out=h[:], in0=us[s][2][:], in1=vv[s][:], op=ALU.max)
+                return
+            nc.vector.scalar_tensor_tensor(
+                out=h[:], in0=zs[s][2][:], scalar=bias[:, 16 + T : 17 + T], in1=vv[s][:], op0=ALU.add, op1=ALU.max
+            )
+
+        def h_move(s):
+            half, T = s // TILES, s % TILES
+            g, q = T // 4, T % 4
+            for t in range(4):
+                nc.sync.dma_start(out=hp[half][g][32 * q : 32 * q + 32, t, :], in_=hh[s][t:P:4, :])
+
+        hg = {}
+
+        def h_weave(half, g, r, engine):
+            a = deep.tile([P, P, 4], BF16, name="hg", align_bytes=64)
+            src = hp[half][g][:, :, r * P : (r + 1) * P].rearrange("p t m -> p m t")
+            if engine == "v":
+                nc.vector.tensor_copy(out=a[:], in_=src)
+            else:
+                nc.scalar.copy(out=a[:], in_=src)
+            hg[(half, g, r)] = a
+
+        def h_quant(half, g, r):
+            nc.vector.quantize_mx(
+                out=hc[half][:, g, r * P : (r + 1) * P].bitcast(FP8X4),
+                scales=hcs[half][:, g, r * P : (r + 1) * P],
+                in_=hg[(half, g, r)][:].rearrange("p m t -> p (m t)"),
+            )
+
+        ys, yt = {}, {}
+
+        def y_mul(half, r, g):
+            for n in range(2):
+                if g == 0:
+                    if r == 3:
+                        y = tpool.tile([P, ROWS], F32, name="xt")
+                    else:
+                        y = zpool.tile([P, ROWS], F32, name="z")
+                    ys[(half, r, n)] = y
+                nc.tensor.matmul_mx(
+                    out=ys[(half, r, n)][:],
+                    lhsT=hc[half][:, g, r * P : (r + 1) * P].bitcast(FP8X4),
+                    lhsT_scale=hcs[half][:, g, r * P : (r + 1) * P],
+                    rhs=vt[:, g, n * 2048 : (n + 1) * 2048].bitcast(FP8X4),
+                    rhs_scale=vs[:, g, n * 512 : (n + 1) * 512],
+                    start=(g == 0),
+                    stop=(g == 1),
+                )
+
+        def y_out(half, r, n, how):
+            if n == 0:
+                o = deep.tile([P, N], F32, name="yt")
+                yt[(half, r)] = o
+            o = yt[(half, r)]
+            cols = slice(n * 512, (n + 1) * 512)
+            y = ys[(half, r, n)]
+            if how == "v":
+                nc.vector.tensor_tensor(out=o[:, cols], in0=y[:], in1=cb[:, cols], op=ALU.add)
+            else:
+                e = stage.tile([P, 512], F32, name="ye")
+                nc.scalar.copy(out=e[:], in_=y[:])
+                nc.gpsimd.tensor_tensor(out=o[:, cols], in0=e[:], in1=cb[:, cols], op=ALU.add)
+
+        def y_store(half, r, lo=0, hi=N):
+            m0 = half * ROWS + r * P
+            nc.sync.dma_start(out=out[m0 : m0 + P, lo:hi], in_=yt[(half, r)][:, lo:hi])
+
+        z_new(0)
+        z_new(1)
+
+        def head_mul(r):
+            z_mul(0, r * P, (r + 1) * P)
+            z_mul(1, r * P, (r + 1) * P)
+
+        def x_both(f, i):
+            f(i, 0)
+            f(i, 1)
+
+        def keep_warm(times):
+            for i in range(times):
+                nc.tensor.matmul(zs[1][2][:], lhsT=warm[:, 0:P], rhs=warm[:], start=True, stop=True)
+
+        keep_warm(5)
+        x_cast(0, "v")
+        x_cast(1, "s")
+        x_turn(0)
+        keep_warm(2)
+        x_cast(2, "s")
+        x_both(x_out, 0)
+        x_turn(1)
+        keep_warm(2)
+        x_both(x_quant, 0)
+        x_both(x_out, 1)
+        x_cast(3, "s")
+        x_turn(2)
+        head_mul(0)
+        x_out(2, 0)
+        x_both(x_quant, 1)
+        x_out(2, 1)
+        nc.scalar.copy(out=bf32[:], in_=braw[:])
+        x_cast(4, "s")
+        x_turn(3)
+        head_mul(1)
+        x_turn(4)
+        bps = zs[1][2][:, 3 * P : 4 * P]
+        nc.tensor.transpose(bps, bf32[:], ident[:])
+        x_out(3, 0)
+        x_cast(5, "s")
+        x_cast(6, "s")
+        nc.scalar.copy(out=bias[:], in_=bps[:, 0:24])
+        x_both(x_quant, 2)
+        x_out(3, 1)
+        head_mul(2)
+        x_both(x_quant, 3)
+        head_mul(3)
+        x_both(x_out, 4)
+        x_both(x_quant, 4)
+
+        pend = []
+        for s in range(16):
+            if s >= 2:
+                z_new(s)
+                z_mul(s, 0, ROWS)
+            u_out(s, 3 if s == 15 else 2)
+            if s == 1:
+                x_cast(7, "s")
+            ready, pend = pend, []
+            if s in (0, 1, 4):
+                x_turn((5, 6, 0, 0, 7)[s])
+            v_max(s)
+            if 1 <= s <= 6:
+                i, g = 5 + (s - 1) // 2, (s - 1) % 2
+                x_out(i, g)
+            if 8 <= s:
+                pend.append((0, (s - 8) // 4, s % 4))
+                h_weave(*pend[-1], "v")
+            if s == 14:
+                pend.append((1, 0, 0))
+                h_weave(1, 0, 0, "s")
+            h_max(s)
+            h_move(s)
+            if s < 15:
+                for q in ready:
+                    h_quant(*q)
+            if 1 <= s <= 6:
+                x_quant(i, g)
+        def y_done(half, r, n, how):
+            y_out(half, r, n, how)
+            y_store(half, r, n * 512, (n + 1) * 512)
+
+        for r in (0, 1):
+            y_mul(0, r, 0)
+            y_mul(0, r, 1)
+        y_done(0, 0, 0, "v")
+        y_done(0, 0, 1, "s")
+        h_weave(1, 0, 1, "s")
+        for r in (2, 3):
+            h_quant(0, 1, r)
+            y_mul(0, r, 0)
+            y_mul(0, r, 1)
+        h_quant(1, 0, 0)
+        y_done(0, 1, 0, "v")
+        y_done(0, 1, 1, "s")
+        h_weave(1, 0, 2, "s")
+        h_quant(1, 0, 1)
+        y_done(0, 2, 0, "v")
+        y_done(0, 2, 1, "v")
+        h_weave(1, 0, 3, "s")
+        y_done(0, 3, 0, "v")
+        h_weave(1, 1, 0, "v")
+        h_weave(1, 1, 1, "s")
+        h_quant(1, 0, 2)
+        h_quant(1, 1, 0)
+        h_weave(1, 1, 2, "s")
+        y_done(0, 3, 1, "v")
+        h_weave(1, 1, 3, "s")
+        for r in range(3):
+            y_mul(1, r, 0)
+        h_quant(1, 1, 1)
+        h_quant(1, 0, 3)
+        y_mul(1, 0, 1)
+        y_mul(1, 1, 1)
+        y_mul(1, 3, 0)
+        y_out(1, 0, 0, "v")
+        h_quant(1, 1, 2)
+        y_mul(1, 2, 1)
+        y_out(1, 0, 1, "s")
+        h_quant(1, 1, 3)
+        y_mul(1, 3, 1)
+        for r, n, how in ((1, 0, "v"), (1, 1, "s"), (2, 0, "v"), (2, 1, "v"), (3, 0, "v"), (3, 1, "v")):
+            y_out(1, r, n, how)
+        for r, n in ((0, 0), (1, 0), (0, 1), (2, 0), (2, 1), (1, 1), (3, 0), (3, 1)):
+            y_store(1, r, n * 512, (n + 1) * 512)

@@ -18,8 +18,8 @@ ALU = mybir.AluOpType
 ACT = mybir.ActivationFunctionType
 
 P = 128
-ROWS = 512
-HALVES = M // ROWS
+BANK = 512
+PAIR = 2 * P
 TILES = F // P
 
 
@@ -28,348 +28,345 @@ def tile_maxout_then_linear_f7_kernel(tc, x_bytes, x_scale, w_words, w_scales, b
     with ExitStack() as ctx:
         keep = ctx.enter_context(tc.tile_pool(name="keep", bufs=1))
         stage = ctx.enter_context(tc.tile_pool(name="stage", bufs=4))
-        deep = ctx.enter_context(tc.tile_pool(name="deep", bufs=8))
-        zpool = ctx.enter_context(tc.psum_pool(name="zpool", bufs=6))
-        tpool = ctx.enter_context(tc.psum_pool(name="tpool", bufs=2))
+        psum = ctx.enter_context(tc.psum_pool(name="psum", bufs=1))
         ctx.enter_context(tc.manual_schedule())
 
-        sc = keep.tile([P, 2, 2, 2], F32, name="sc")
-        nc.scalar.dma_start(
-            out=sc[:].rearrange("p g u e -> p g (u e)"), in_=x_scale.rearrange("o (g p t) -> p (o g) t", g=2, t=4)
-        )
+        def bank(i):
+            t = psum.tile([P, BANK], F32, name="bank%d" % i)
+            return t
+
+        sc = keep.tile([P, 2, 4], F32, name="sc")
+        ws = keep.tile([P, 2, PIECES * F], U8, name="ws", align_bytes=256)
+        vs = keep.tile([P, 2, N], U8, name="vs", align_bytes=256)
         ident = keep.tile([P, P], F32, name="ident")
-        make_identity(nc, ident[:])
         braw = keep.tile([P, P], BF16, name="braw")
-        warm = keep.tile([P, 512], BF16, name="warm")
+        xb0 = [keep.tile([P, K], U8, name="xb%d" % i, align_bytes=64) for i in range(2)]
+        xb2 = [keep.tile([P, 2, K], U8, name="xbb%d" % i, align_bytes=64) for i in range(3)]
+        xb = xb0 + [xb2[i // 2][:, i % 2] for i in range(6)]
+        wq = [keep.tile([P, 2, PIECES, 512], U8, name="wq%d" % i, align_bytes=256) for i in range(4)]
+        vt = keep.tile([P, 2, 4 * N], U8, name="vt", align_bytes=256)
+        cb = keep.tile([P, N], BF16, name="cb")
+        spread = keep.tile([P, 2, 512], F32, name="spread", align_bytes=64)
+        bias = keep.tile([P, 24], F32, name="bias")
+        bf32 = keep.tile([P, P], F32, name="bf32")
+        warm = keep.tile([P, BANK], BF16, name="warm")
+
         nc.vector.memset(warm[:], 0.0)
-        nc.gpsimd.memset(braw[:], 0.0)
-        ws = keep.tile([P, 2, PIECES * F], U8, name="ws", align_bytes=64)
         nc.vector.memset(ws[:].rearrange("p g n -> p (g n)").bitcast(U32), 0)
-        vs = keep.tile([P, 2, N], U8, name="vs", align_bytes=64)
+        make_identity(nc, ident[:])
+        nc.scalar.activation(out=braw[:], in_=ident[:], func=ACT.Identity, scale=0.0)
         nc.gpsimd.memset(vs[:].rearrange("p g n -> p (g n)").bitcast(U32), 0)
 
-        xb4 = [keep.tile([P, 4, K], U8, name="xb%d" % i, align_bytes=64) for i in range(2)]
-        xb = [xb4[i // 4][:, i % 4] for i in range(8)]
-        wt = [keep.tile([P, 2, PIECES, 512], U8, name="wt%d" % q, align_bytes=64) for q in range(4)]
-        vt = keep.tile([P, 2, 4 * N], U8, name="vt", align_bytes=64)
-        cb = keep.tile([P, N], BF16, name="cb")
+        def load_x(i):
+            nc.sync.dma_start(out=xb[i][:], in_=x_bytes[i * P : (i + 1) * P, :])
 
-        def load_x(lo, hi):
-            nc.sync.dma_start(
-                out=xb4[lo // 4][:, lo % 4 : lo % 4 + hi - lo], in_=x_bytes[lo * P : hi * P, :].rearrange("(r p) k -> p r k", p=P)
-            )
+        def load_pair(a):
+            nc.sync.dma_start(out=xb2[a - 1][:], in_=x_bytes[a * PAIR : (a + 1) * PAIR, :].rearrange("(r p) k -> p r k", p=P))
 
         def load_w(q):
             for g in range(2):
                 nc.sync.dma_start(
-                    out=wt[q][:, g].bitcast(I32),
+                    out=wq[q][:, g].bitcast(I32),
                     in_=w_words[g].rearrange("p (j n) -> p j n", j=PIECES)[:, :, q * 512 : (q + 1) * 512].bitcast(I32),
                 )
 
         def load_scales(tile, scales):
-            for q in range(4):
+            for i in range(4):
                 nc.sync.dma_start(
-                    out=tile[32 * q : 32 * q + 4].bitcast(I32),
-                    in_=scales[:, 4 * q : 4 * q + 4, :].rearrange("g q n -> q g n").bitcast(I32),
+                    out=tile[i:P:32].bitcast(I32), in_=scales[:, i:16:4, :].rearrange("g q n -> q g n").bitcast(I32)
                 )
 
-        load_x(0, 1)
-        load_x(1, 2)
-        load_x(2, 4)
+        rows = b.rearrange("j (t p) -> (j t) p", p=P)
+        load_x(0)
+        nc.sync.dma_start(out=sc[:], in_=x_scale.rearrange("o (g p t) -> p (o g) t", g=2, t=4))
+        load_x(1)
         load_scales(ws, w_scales)
         load_w(0)
-        nc.sync.dma_start(out=braw[0:24, :], in_=b.rearrange("j (t p) -> (j t) p", p=P))
-        load_x(4, 6)
+        nc.sync.dma_start(out=braw[0:16, :], in_=rows[0:16])
+        nc.sync.dma_start(out=braw[16:24, :], in_=rows[16:24])
+        load_pair(1)
         load_w(1)
-        load_x(6, 8)
+        load_pair(2)
         load_w(2)
         load_w(3)
+        load_pair(3)
+        load_scales(vs, v_scales)
         for g in range(2):
             nc.sync.dma_start(out=vt[:, g].bitcast(I32), in_=v_words[g].rearrange("p n t -> p (n t)").bitcast(I32))
-        load_scales(vs, v_scales)
         nc.sync.dma_start(out=cb[:], in_=c.partition_broadcast(P))
 
-        xc = [keep.tile([P, 2, ROWS], U32, name="xc%d" % i, align_bytes=64) for i in range(HALVES)]
-        xcs = [keep.tile([P, 2, ROWS], U8, name="xcs%d" % i, align_bytes=64) for i in range(HALVES)]
-        hc = [keep.tile([P, 2, ROWS], U32, name="hc%d" % i, align_bytes=64) for i in range(HALVES)]
-        hcs = [keep.tile([P, 2, ROWS], U8, name="hcs%d" % i, align_bytes=64) for i in range(HALVES)]
-        hp = [[keep.tile([P, 4, ROWS], BF16, name="hp%d%d" % (i, g), align_bytes=64) for g in range(2)] for i in range(HALVES)]
-        bias = keep.tile([P, 24], F32, name="bias")
-        bf32 = keep.tile([P, P], F32, name="bf32")
+        xc = [keep.tile([P, 2, n], U32, name="xc%d" % i, align_bytes=256) for i, n in enumerate((256, 512, 256))]
+        xcs = [keep.tile([P, 2, n], U8, name="xcs%d" % i, align_bytes=256) for i, n in enumerate((256, 512, 256))]
+        hc = [keep.tile([P, 2, PAIR], U32, name="hc%d" % i, align_bytes=256) for i in range(4)]
+        hcs = [keep.tile([P, 2, PAIR], U8, name="hcs%d" % i, align_bytes=256) for i in range(4)]
+        chunk_of = [(0, 0), (1, 0), (1, PAIR), (2, 0)]
 
         xw, xt, xg = {}, {}, {}
 
-        def x_cast(i, engine):
-            w = deep.tile([P, K], BF16, name="xw", align_bytes=64)
+        def spread_scales(g, where):
+            t = bank(where)
+            for e in range(4):
+                nc.tensor.transpose(t[:, e * P : (e + 1) * P], sc[:, g, e : e + 1].to_broadcast([P, P]), ident[:])
+            nc.scalar.copy(out=spread[:, g].rearrange("m (p t) -> m p t", t=4), in_=t[:].rearrange("m (t p) -> m p t", t=4))
+
+        def x_prod(i, g):
+            w = stage.tile([P, 512], BF16, name="xw", align_bytes=64, bufs=6)
+            xw[(i, g)] = w
+            nc.vector.tensor_tensor(out=w[:], in0=xb[i][:, g * 512 : (g + 1) * 512].bitcast(E4M3), in1=spread[:, g], op=ALU.mult)
+
+        def x_cast(i, g, engine):
+            w = stage.tile([P, 512], BF16, name="xw", align_bytes=64, bufs=6)
+            xw[(i, g)] = w
             if engine == "v":
-                for g in range(2):
-                    nc.vector.tensor_copy(out=w[:, g * 512 : (g + 1) * 512], in_=xb[i][:, g * 512 : (g + 1) * 512].bitcast(E4M3))
+                nc.vector.tensor_copy(out=w[:], in_=xb[i][:, g * 512 : (g + 1) * 512].bitcast(E4M3))
             else:
-                nc.scalar.copy(out=w[:], in_=xb[i].bitcast(E4M3))
-            xw[i] = w
+                nc.scalar.copy(out=w[:], in_=xb[i][:, g * 512 : (g + 1) * 512].bitcast(E4M3))
 
-        def x_turn(i):
-            words = xw[i][:].bitcast(F32)
-            t = tpool.tile([P, 2, 2, P], F32, name="xt")
-            for g in range(2):
-                for u in range(2):
-                    nc.tensor.transpose(t[:, g, u, :], words[:, 256 * g + u : 256 * (g + 1) : 2], ident[:])
-            xt[i] = t
-
-        def x_out(i, g):
+        def head_turn(i, g, where):
             if g == 0:
-                a = stage.tile([P, 2, P, 4], BF16, name="xg", align_bytes=64)
-                xg[i] = a
-            a = xg[i]
-            if True:
-                nc.vector.tensor_tensor(
-                    out=a[:, g].rearrange("p m (u e) -> p m u e", u=2),
-                    in0=xt[i][:, g].bitcast(BF16).rearrange("p u (m e) -> p m u e", e=2),
-                    in1=sc[:, g].unsqueeze(1).to_broadcast([P, P, 2, 2]),
-                    op=ALU.mult,
-                )
+                xt[i] = bank(where)
+            words = xw[(i, g)][:].bitcast(F32)
+            for u in range(2):
+                nc.tensor.transpose(xt[i][:, g * PAIR + u : (g + 1) * PAIR : 2], words[:, u:256:2], ident[:])
 
-        def x_quant(i, g):
-            half, r = i // 4, i % 4
-            if True:
-                nc.vector.quantize_mx(
-                    out=xc[half][:, g, r * P : (r + 1) * P].bitcast(FP8X4),
-                    scales=xcs[half][:, g, r * P : (r + 1) * P],
-                    in_=xg[i][:, g].rearrange("p m t -> p (m t)"),
-                )
+        def head_out(i, g):
+            t = stage.tile([P, P, 4], BF16, name="xg", align_bytes=64)
+            xg[(i, g, 0)] = t
+            nc.vector.tensor_tensor(
+                out=t[:],
+                in0=xt[i][:, g * PAIR : (g + 1) * PAIR].bitcast(BF16).rearrange("p (m t) -> p m t", t=4),
+                in1=sc[:, g].unsqueeze(1).to_broadcast([P, P, 4]),
+                op=ALU.mult,
+            )
 
-        zs, us, vv, hh = {}, {}, {}, {}
+        def head_quant(i, g):
+            nc.vector.quantize_mx(
+                out=xc[0][:, g, i * P : (i + 1) * P].bitcast(FP8X4),
+                scales=xcs[0][:, g, i * P : (i + 1) * P],
+                in_=xg[(i, g, 0)][:].rearrange("p m t -> p (m t)"),
+            )
 
-        def z_new(s):
-            zs[s] = []
-            for j in range(PIECES):
-                z = zpool.tile([P, ROWS], F32, name="z")
-                zs[s].append(z)
+        def x_turn(i, g, where):
+            a, r = i // 2, i % 2
+            if r == 0:
+                xt[(a, g)] = bank(where)
+            words = xw[(i, g)][:].bitcast(F32)
+            for u in range(2):
+                nc.tensor.transpose(xt[(a, g)][:, u * PAIR + r * P : u * PAIR + (r + 1) * P], words[:, u:256:2], ident[:])
 
-        def z_mul(s, lo, hi):
-            half, T = s // TILES, s % TILES
+        def x_out(a, g):
+            t = stage.tile([P, PAIR, 4], BF16, name="xg", align_bytes=64)
+            xg[(a, g)] = t
+            nc.scalar.copy(out=t[:].bitcast(F32), in_=xt[(a, g)][:].rearrange("p (u m) -> p m u", u=2))
+
+        def x_quant(a, g):
+            ch, at = chunk_of[a]
+            nc.vector.quantize_mx(
+                out=xc[ch][:, g, at : at + PAIR].bitcast(FP8X4),
+                scales=xcs[ch][:, g, at : at + PAIR],
+                in_=xg[(a, g)][:].rearrange("p m t -> p (m t)"),
+            )
+
+        widths = (256, 512, 256)
+        steps = [(ch, T) for ch in range(3) for T in range(TILES)]
+        zs, us, vv, hp, hg = {}, {}, {}, {}, {}
+
+        def z_pass(s, j, g, lo=0, hi=None):
+            ch, T = steps[s]
+            if g == 0 and lo == 0:
+                zs[(s, j)] = bank(3 * (s % 2) + j)
             col = (T % 2) * 256
+            cols = slice(lo, hi or widths[ch])
+            nc.tensor.matmul_mx(
+                out=zs[(s, j)][:, cols],
+                lhsT=wq[T // 2][:, g, j, col : col + 256].bitcast(FP4X4),
+                lhsT_scale=ws[:, g, j * F + T * P : j * F + (T + 1) * P],
+                rhs=xc[ch][:, g, cols].bitcast(FP8X4),
+                rhs_scale=xcs[ch][:, g, cols],
+                start=(g == 0),
+                stop=(g == 1),
+            )
+
+        def z_mul(s):
             for j in range(PIECES):
                 for g in range(2):
-                    nc.tensor.matmul_mx(
-                        out=zs[s][j][:, lo:hi],
-                        lhsT=wt[T // 2][:, g, j, col : col + 256].bitcast(FP4X4),
-                        lhsT_scale=ws[:, g, j * F + T * P : j * F + (T + 1) * P],
-                        rhs=xc[half][:, g, lo:hi].bitcast(FP8X4),
-                        rhs_scale=xcs[half][:, g, lo:hi],
-                        start=(g == 0),
-                        stop=(g == 1),
-                    )
+                    z_pass(s, j, g)
 
-        def u_out(s, pieces=2):
-            T = s % TILES
+        def u_out(s, pieces):
+            ch, T = steps[s]
+            n = widths[ch]
             us[s] = []
             for j in range(pieces):
-                u = stage.tile([P, ROWS], BF16, name="u%d" % j, align_bytes=64)
-                nc.scalar.activation(out=u[:], in_=zs[s][j][:], func=ACT.Identity, bias=bias[:, 8 * j + T : 8 * j + T + 1])
+                u = stage.tile([P, n], BF16, name="u%d" % j, align_bytes=64)
+                nc.scalar.activation(out=u[:], in_=zs[(s, j)][:, 0:n], func=ACT.Identity, bias=bias[:, 8 * j + T : 8 * j + T + 1])
                 us[s].append(u)
 
         def v_max(s):
-            v = stage.tile([P, ROWS], BF16, name="v", align_bytes=64)
+            v = stage.tile([P, widths[steps[s][0]]], BF16, name="v", align_bytes=64)
             nc.vector.tensor_tensor(out=v[:], in0=us[s][0][:], in1=us[s][1][:], op=ALU.max)
             vv[s] = v
 
         def h_max(s):
-            T = s % TILES
-            h = stage.tile([P, ROWS], BF16, name="h", align_bytes=64)
-            hh[s] = h
+            ch, T = steps[s]
+            n = widths[ch]
+            h = stage.tile([P, n], BF16, name="h", align_bytes=64, bufs=8)
             if len(us[s]) == 3:
                 nc.vector.tensor_tensor(out=h[:], in0=us[s][2][:], in1=vv[s][:], op=ALU.max)
-                return
-            nc.vector.scalar_tensor_tensor(
-                out=h[:], in0=zs[s][2][:], scalar=bias[:, 16 + T : 17 + T], in1=vv[s][:], op0=ALU.add, op1=ALU.max
-            )
-
-        def h_move(s):
-            half, T = s // TILES, s % TILES
-            g, q = T // 4, T % 4
-            for t in range(4):
-                nc.sync.dma_start(out=hp[half][g][32 * q : 32 * q + 32, t, :], in_=hh[s][t:P:4, :])
-
-        hg = {}
-
-        def h_weave(half, g, r, engine):
-            a = deep.tile([P, P, 4], BF16, name="hg", align_bytes=64)
-            src = hp[half][g][:, :, r * P : (r + 1) * P].rearrange("p t m -> p m t")
-            if engine == "v":
-                nc.vector.tensor_copy(out=a[:], in_=src)
             else:
-                nc.scalar.copy(out=a[:], in_=src)
-            hg[(half, g, r)] = a
-
-        def h_quant(half, g, r):
-            nc.vector.quantize_mx(
-                out=hc[half][:, g, r * P : (r + 1) * P].bitcast(FP8X4),
-                scales=hcs[half][:, g, r * P : (r + 1) * P],
-                in_=hg[(half, g, r)][:].rearrange("p m t -> p (m t)"),
-            )
-
-        ys, yt = {}, {}
-
-        def y_mul(half, r, g):
-            for n in range(2):
-                if g == 0:
-                    if r == 3:
-                        y = tpool.tile([P, ROWS], F32, name="xt")
-                    else:
-                        y = zpool.tile([P, ROWS], F32, name="z")
-                    ys[(half, r, n)] = y
-                nc.tensor.matmul_mx(
-                    out=ys[(half, r, n)][:],
-                    lhsT=hc[half][:, g, r * P : (r + 1) * P].bitcast(FP8X4),
-                    lhsT_scale=hcs[half][:, g, r * P : (r + 1) * P],
-                    rhs=vt[:, g, n * 2048 : (n + 1) * 2048].bitcast(FP8X4),
-                    rhs_scale=vs[:, g, n * 512 : (n + 1) * 512],
-                    start=(g == 0),
-                    stop=(g == 1),
+                nc.vector.scalar_tensor_tensor(
+                    out=h[:], in0=zs[(s, 2)][:, 0:n], scalar=bias[:, 16 + T : 17 + T], in1=vv[s][:], op0=ALU.add, op1=ALU.max
                 )
+            g, q = T // 4, T % 4
+            if q == 0:
+                planes = keep.tile([P, 4, n], BF16, name="hp%d_%d" % (ch, g), align_bytes=64)
+                hp[(ch, g)] = planes
+            nc.sync.dma_start(out=hp[(ch, g)][32 * q : 32 * q + 32].rearrange("p t m -> p (t m)"), in_=h[:])
 
-        def y_out(half, r, n, how):
-            if n == 0:
-                o = deep.tile([P, N], F32, name="yt")
-                yt[(half, r)] = o
-            o = yt[(half, r)]
-            cols = slice(n * 512, (n + 1) * 512)
-            y = ys[(half, r, n)]
-            if how == "v":
-                nc.vector.tensor_tensor(out=o[:, cols], in0=y[:], in1=cb[:, cols], op=ALU.add)
+        def h_weave(a, g, engine, lo=0, hi=PAIR):
+            ch, at = chunk_of[a]
+            t = stage.tile([P, hi - lo, 4], BF16, name="hg", align_bytes=64)
+            src = hp[(ch, g)][:, :, at + lo : at + hi].rearrange("p t (c i) -> p c t i", i=4)
+            dst = t[:].rearrange("p (c i) t -> p c t i", i=4)
+            if engine == "v":
+                nc.vector.tensor_copy(out=dst, in_=src)
             else:
-                e = stage.tile([P, 512], F32, name="ye")
-                nc.scalar.copy(out=e[:], in_=y[:])
-                nc.gpsimd.tensor_tensor(out=o[:, cols], in0=e[:], in1=cb[:, cols], op=ALU.add)
+                nc.scalar.copy(out=dst, in_=src)
+            hg[(a, g, lo)] = t
 
-        def y_store(half, r, lo=0, hi=N):
-            m0 = half * ROWS + r * P
-            nc.sync.dma_start(out=out[m0 : m0 + P, lo:hi], in_=yt[(half, r)][:, lo:hi])
+        def h_quant(a, g, lo=0, hi=PAIR):
+            nc.vector.quantize_mx(
+                out=hc[a][:, g, lo:hi].bitcast(FP8X4), scales=hcs[a][:, g, lo:hi], in_=hg[(a, g, lo)][:].rearrange("p m t -> p (m t)")
+            )
 
-        z_new(0)
-        z_new(1)
+        ys = {}
 
-        def head_mul(r):
-            z_mul(0, r * P, (r + 1) * P)
-            z_mul(1, r * P, (r + 1) * P)
+        def y_pass(r, n, g, where):
+            if g == 0:
+                ys[(r, n)] = bank(where)
+            cols = slice((r % 2) * P, (r % 2 + 1) * P)
+            nc.tensor.matmul_mx(
+                out=ys[(r, n)][:],
+                lhsT=hc[r // 2][:, g, cols].bitcast(FP8X4),
+                lhsT_scale=hcs[r // 2][:, g, cols],
+                rhs=vt[:, g, n * 2048 : (n + 1) * 2048].bitcast(FP8X4),
+                rhs_scale=vs[:, g, n * 512 : (n + 1) * 512],
+                start=(g == 0),
+                stop=(g == 1),
+            )
 
-        def x_both(f, i):
-            f(i, 0)
-            f(i, 1)
+        def y_mul(r, n, where):
+            y_pass(r, n, 0, where)
+            y_pass(r, n, 1, where)
+
+        def y_out(r, n):
+            o = stage.tile([P, BANK], F32, name="yt", bufs=6)
+            cols = slice(n * 512, (n + 1) * 512)
+            nc.vector.tensor_tensor(out=o[:], in0=ys[(r, n)][:], in1=cb[:, cols], op=ALU.add)
+            nc.sync.dma_start(out=out[r * P : (r + 1) * P, cols], in_=o[:])
+
+        spare = bank(3)
 
         def keep_warm(times):
             for i in range(times):
-                nc.tensor.matmul(zs[1][2][:], lhsT=warm[:, 0:P], rhs=warm[:], start=True, stop=True)
+                nc.tensor.matmul(spare[:], lhsT=warm[:, 0:P], rhs=warm[:], start=True, stop=True)
 
-        keep_warm(5)
-        x_cast(0, "v")
-        x_cast(1, "s")
-        x_turn(0)
+        def head_mul(i):
+            for g in range(2):
+                for s in range(2):
+                    for j in range(PIECES):
+                        z_pass(s, j, g, i * P, (i + 1) * P)
+
+        keep_warm(4)
+        x_cast(0, 0, "v")
+        x_cast(0, 1, "v")
+        x_cast(1, 0, "s")
+        x_cast(1, 1, "s")
+        head_turn(0, 0, 6)
+        head_turn(0, 1, 6)
+        spread_scales(0, 4)
+        keep_warm(1)
+        spread_scales(1, 5)
+        head_turn(1, 0, 7)
+        head_turn(1, 1, 7)
         keep_warm(2)
-        x_cast(2, "s")
-        x_both(x_out, 0)
-        x_turn(1)
-        keep_warm(2)
-        x_both(x_quant, 0)
-        x_both(x_out, 1)
-        x_cast(3, "s")
-        x_turn(2)
-        head_mul(0)
-        x_out(2, 0)
-        x_both(x_quant, 1)
-        x_out(2, 1)
+        head_out(0, 0)
+        head_out(0, 1)
+        head_quant(0, 0)
+        head_out(1, 0)
+        head_quant(0, 1)
+        head_out(1, 1)
+        head_quant(1, 0)
+        x_prod(2, 0)
+        head_quant(1, 1)
         nc.scalar.copy(out=bf32[:], in_=braw[:])
-        x_cast(4, "s")
-        x_turn(3)
+        head_mul(0)
+        turned = bank(6)
+        nc.tensor.transpose(turned[:, 0:P], bf32[:], ident[:])
+        nc.scalar.copy(out=bias[:], in_=turned[:, 0:24])
         head_mul(1)
-        x_turn(4)
-        bps = zs[1][2][:, 3 * P : 4 * P]
-        nc.tensor.transpose(bps, bf32[:], ident[:])
-        x_out(3, 0)
-        x_cast(5, "s")
-        x_cast(6, "s")
-        nc.scalar.copy(out=bias[:], in_=bps[:, 0:24])
-        x_both(x_quant, 2)
-        x_out(3, 1)
-        head_mul(2)
-        x_both(x_quant, 3)
-        head_mul(3)
-        x_both(x_out, 4)
-        x_both(x_quant, 4)
+        x_prod(3, 0)
+        x_prod(2, 1)
+        x_prod(3, 1)
 
-        pend = []
-        for s in range(16):
+        def turn_pair(a):
+            for g in range(2):
+                x_turn(2 * a, g, 6 + g)
+                x_turn(2 * a + 1, g, 6 + g)
+
+        turns = {2: 1, 5: 2, 9: 3}
+        y_tiles = {13: [(0, 0)], 15: [(0, 1)], 17: [(1, 0)], 18: [(1, 1)], 20: [(2, 0)], 21: [(2, 1)], 22: [(3, 0)], 23: [(3, 1)]}
+        before = {
+            0: [(x_prod, 4, 0)], 1: [(x_prod, 4, 1)], 3: [(x_quant, 1, 0)], 4: [(x_quant, 1, 1)], 5: [(x_prod, 6, 0)], 6: [(x_quant, 2, 0), (x_quant, 2, 1)], 7: [(x_prod, 6, 1)],
+            8: [(h_weave, 0, 0, "v")], 10: [(x_quant, 3, 0), (x_quant, 3, 1)], 11: [(h_weave, 0, 1, "v")],
+            14: [(h_weave, 1, 0, "v")], 16: [(h_weave, 2, 0, "v")], 19: [(h_quant, 1, 1, 0, P), (h_weave, 1, 1, "v", P, PAIR)],
+            20: [(h_quant, 1, 1, P, PAIR)], 21: [(h_quant, 2, 1, 0, P)], 22: [(h_quant, 2, 1, P, PAIR)], 23: [(h_quant, 3, 0, 0, P)],
+        }
+        after = {
+            0: [(x_prod, 5, 0)], 1: [(x_prod, 5, 1)], 4: [(x_prod, 7, 0)], 7: [(x_prod, 7, 1)],
+            8: [(h_quant, 0, 0)], 11: [(h_quant, 0, 1)], 14: [(h_quant, 1, 0)], 16: [(h_quant, 2, 0)],
+        }
+        on_scalar = {18: [(1, 1, "s", 0, P)], 19: [(2, 1, "s", 0, P)], 20: [(2, 1, "s", P, PAIR)], 22: [(3, 0, "s", 0, P)], 23: [(3, 0, "s", P, PAIR)]}
+        for s in range(len(steps)):
             if s >= 2:
-                z_new(s)
-                z_mul(s, 0, ROWS)
-            u_out(s, 3 if s == 15 else 2)
-            if s == 1:
-                x_cast(7, "s")
-            ready, pend = pend, []
-            if s in (0, 1, 4):
-                x_turn((5, 6, 0, 0, 7)[s])
+                z_mul(s)
+            if s in turns:
+                turn_pair(turns[s])
+            for r, n in y_tiles.get(s, []):
+                y_mul(r, n, 6 + n)
+            u_out(s, 2 if s in (3, 4, 5, 6, 7, 23) else 3)
+            if s in turns:
+                x_out(turns[s], 0)
+                x_out(turns[s], 1)
+            for job in on_scalar.get(s, []):
+                h_weave(*job)
             v_max(s)
-            if 1 <= s <= 6:
-                i, g = 5 + (s - 1) // 2, (s - 1) % 2
-                x_out(i, g)
-            if 8 <= s:
-                pend.append((0, (s - 8) // 4, s % 4))
-                h_weave(*pend[-1], "v")
-            if s == 14:
-                pend.append((1, 0, 0))
-                h_weave(1, 0, 0, "s")
+            for job in before.get(s, []):
+                job[0](*job[1:])
             h_max(s)
-            h_move(s)
-            if s < 15:
-                for q in ready:
-                    h_quant(*q)
-            if 1 <= s <= 6:
-                x_quant(i, g)
-        def y_done(half, r, n, how):
-            y_out(half, r, n, how)
-            y_store(half, r, n * 512, (n + 1) * 512)
+            for job in after.get(s, []):
+                job[0](*job[1:])
+            for r, n in y_tiles.get(s, []):
+                y_out(r, n)
 
-        for r in (0, 1):
-            y_mul(0, r, 0)
-            y_mul(0, r, 1)
-        y_done(0, 0, 0, "v")
-        y_done(0, 0, 1, "s")
-        h_weave(1, 0, 1, "s")
-        for r in (2, 3):
-            h_quant(0, 1, r)
-            y_mul(0, r, 0)
-            y_mul(0, r, 1)
-        h_quant(1, 0, 0)
-        y_done(0, 1, 0, "v")
-        y_done(0, 1, 1, "s")
-        h_weave(1, 0, 2, "s")
-        h_quant(1, 0, 1)
-        y_done(0, 2, 0, "v")
-        y_done(0, 2, 1, "v")
-        h_weave(1, 0, 3, "s")
-        y_done(0, 3, 0, "v")
-        h_weave(1, 1, 0, "v")
-        h_weave(1, 1, 1, "s")
-        h_quant(1, 0, 2)
-        h_quant(1, 1, 0)
-        h_weave(1, 1, 2, "s")
-        y_done(0, 3, 1, "v")
-        h_weave(1, 1, 3, "s")
-        for r in range(3):
-            y_mul(1, r, 0)
-        h_quant(1, 1, 1)
-        h_quant(1, 0, 3)
-        y_mul(1, 0, 1)
-        y_mul(1, 1, 1)
-        y_mul(1, 3, 0)
-        y_out(1, 0, 0, "v")
-        h_quant(1, 1, 2)
-        y_mul(1, 2, 1)
-        y_out(1, 0, 1, "s")
-        h_quant(1, 1, 3)
-        y_mul(1, 3, 1)
-        for r, n, how in ((1, 0, "v"), (1, 1, "s"), (2, 0, "v"), (2, 1, "v"), (3, 0, "v"), (3, 1, "v")):
-            y_out(1, r, n, how)
-        for r, n in ((0, 0), (1, 0), (0, 1), (2, 0), (2, 1), (1, 1), (3, 0), (3, 1)):
-            y_store(1, r, n * 512, (n + 1) * 512)
+        y_mul(4, 0, 6)
+        y_mul(4, 1, 0)
+        y_mul(5, 0, 1)
+        y_mul(5, 1, 2)
+        y_out(4, 0)
+        h_quant(3, 0, P, PAIR)
+        for r in (6, 7):
+            for n in range(2):
+                y_pass(r, n, 0, (7, 3, 4, 5)[2 * (r - 6) + n])
+        y_out(4, 1)
+        y_out(5, 0)
+        y_out(5, 1)
+        h_weave(3, 1, "s", P, PAIR)
+        h_weave(3, 1, "v", 0, P)
+        h_quant(3, 1, 0, P)
+        h_quant(3, 1, P, PAIR)
+        for r in (6, 7):
+            for n in range(2):
+                y_pass(r, n, 1, 0)
+        for r in (6, 7):
+            for n in range(2):
+                y_out(r, n)

@@ -88,18 +88,18 @@ def tile_maxout_then_linear_f7_kernel(tc, x_bytes, x_scale, w_words, w_scales, b
         load_w(1)
         load_pair(2)
         load_w(2)
-        load_w(3)
         load_pair(3)
+        load_w(3)
         load_scales(vs, v_scales)
         for g in range(2):
             nc.sync.dma_start(out=vt[:, g].bitcast(I32), in_=v_words[g].rearrange("p n t -> p (n t)").bitcast(I32))
         nc.sync.dma_start(out=cb[:], in_=c.partition_broadcast(P))
 
-        xc = [keep.tile([P, 2, n], U32, name="xc%d" % i, align_bytes=256) for i, n in enumerate((256, 512, 256))]
-        xcs = [keep.tile([P, 2, n], U8, name="xcs%d" % i, align_bytes=256) for i, n in enumerate((256, 512, 256))]
+        xc = [keep.tile([P, 2, BANK], U32, name="xc%d" % i, align_bytes=256) for i in range(2)]
+        xcs = [keep.tile([P, 2, BANK], U8, name="xcs%d" % i, align_bytes=256) for i in range(2)]
         hc = [keep.tile([P, 2, PAIR], U32, name="hc%d" % i, align_bytes=256) for i in range(4)]
         hcs = [keep.tile([P, 2, PAIR], U8, name="hcs%d" % i, align_bytes=256) for i in range(4)]
-        chunk_of = [(0, 0), (1, 0), (1, PAIR), (2, 0)]
+        chunk_of = [(0, 0), (0, PAIR), (1, 0), (1, PAIR)]
 
         xw, xt, xg = {}, {}, {}
 
@@ -167,18 +167,25 @@ def tile_maxout_then_linear_f7_kernel(tc, x_bytes, x_scale, w_words, w_scales, b
                 in_=xg[(a, g)][:].rearrange("p m t -> p (m t)"),
             )
 
-        widths = (256, 512, 256)
-        steps = [(ch, T) for ch in range(3) for T in range(TILES)]
-        zs, us, vv, hp, hg = {}, {}, {}, {}, {}
+        steps = [(a, 1, T) for a in (0, 1) for T in range(4)] + [(0, 2, T) for T in range(4, 8)]
+        steps = steps + [(2, 2, T) for T in range(4)] + [(a, 1, T) for a in (2, 3) for T in range(4, 8)]
+        zs, us, vv, hp, hg, whole = {}, {}, {}, {}, {}, {}
 
         def z_pass(s, j, g, lo=0, hi=None):
-            ch, T = steps[s]
-            if g == 0 and lo == 0:
+            a, pairs, T = steps[s]
+            ch, at = chunk_of[a]
+            if g == 0 and lo == 0 and pairs == 2:
                 zs[(s, j)] = bank(3 * (s % 2) + j)
+            elif g == 0 and lo == 0 and j != 1:
+                t = bank(2 * (s % 3) + j // 2)
+                zs[(s, j)] = t[:, 0:PAIR]
+                if j == 0:
+                    zs[(s, 1)] = t[:, PAIR:BANK]
             col = (T % 2) * 256
-            cols = slice(lo, hi or widths[ch])
+            hi = hi or pairs * PAIR
+            cols = slice(at + lo, at + hi)
             nc.tensor.matmul_mx(
-                out=zs[(s, j)][:, cols],
+                out=zs[(s, j)][:, lo:hi],
                 lhsT=wq[T // 2][:, g, j, col : col + 256].bitcast(FP4X4),
                 lhsT_scale=ws[:, g, j * F + T * P : j * F + (T + 1) * P],
                 rhs=xc[ch][:, g, cols].bitcast(FP8X4),
@@ -193,8 +200,8 @@ def tile_maxout_then_linear_f7_kernel(tc, x_bytes, x_scale, w_words, w_scales, b
                     z_pass(s, j, g)
 
         def u_out(s, pieces):
-            ch, T = steps[s]
-            n = widths[ch]
+            a, pairs, T = steps[s]
+            n = pairs * PAIR
             us[s] = []
             for j in range(pieces):
                 u = stage.tile([P, n], BF16, name="u%d" % j, align_bytes=64)
@@ -202,13 +209,13 @@ def tile_maxout_then_linear_f7_kernel(tc, x_bytes, x_scale, w_words, w_scales, b
                 us[s].append(u)
 
         def v_max(s):
-            v = stage.tile([P, widths[steps[s][0]]], BF16, name="v", align_bytes=64)
+            v = stage.tile([P, steps[s][1] * PAIR], BF16, name="v", align_bytes=64)
             nc.vector.tensor_tensor(out=v[:], in0=us[s][0][:], in1=us[s][1][:], op=ALU.max)
             vv[s] = v
 
         def h_max(s):
-            ch, T = steps[s]
-            n = widths[ch]
+            a, pairs, T = steps[s]
+            n = pairs * PAIR
             h = stage.tile([P, n], BF16, name="h", align_bytes=64, bufs=8)
             if len(us[s]) == 3:
                 nc.vector.tensor_tensor(out=h[:], in0=us[s][2][:], in1=vv[s][:], op=ALU.max)
@@ -218,14 +225,15 @@ def tile_maxout_then_linear_f7_kernel(tc, x_bytes, x_scale, w_words, w_scales, b
                 )
             g, q = T // 4, T % 4
             if q == 0:
-                planes = keep.tile([P, 4, n], BF16, name="hp%d_%d" % (ch, g), align_bytes=64)
-                hp[(ch, g)] = planes
-            nc.sync.dma_start(out=hp[(ch, g)][32 * q : 32 * q + 32].rearrange("p t m -> p (t m)"), in_=h[:])
+                planes = keep.tile([P, 4, n], BF16, name="hp%d_%d" % (a, g), align_bytes=64)
+                whole[(a, g)] = planes
+                for i in range(pairs):
+                    hp[(a + i, g)] = planes[:, :, i * PAIR : (i + 1) * PAIR]
+            nc.sync.dma_start(out=whole[(a, g)][32 * q : 32 * q + 32].rearrange("p t m -> p (t m)"), in_=h[:])
 
         def h_weave(a, g, engine, lo=0, hi=PAIR):
-            ch, at = chunk_of[a]
             t = stage.tile([P, hi - lo, 4], BF16, name="hg", align_bytes=64)
-            src = hp[(ch, g)][:, :, at + lo : at + hi].rearrange("p t (c i) -> p c t i", i=4)
+            src = hp[(a, g)][:, :, lo:hi].rearrange("p t (c i) -> p c t i", i=4)
             dst = t[:].rearrange("p (c i) t -> p c t i", i=4)
             if engine == "v":
                 nc.vector.tensor_copy(out=dst, in_=src)
@@ -258,13 +266,18 @@ def tile_maxout_then_linear_f7_kernel(tc, x_bytes, x_scale, w_words, w_scales, b
             y_pass(r, n, 0, where)
             y_pass(r, n, 1, where)
 
-        def y_out(r, n):
-            o = stage.tile([P, BANK], F32, name="yt", bufs=6)
+        def y_out(r, n, engine="v"):
+            o = stage.tile([P, BANK], F32, name="yt", bufs=8)
             cols = slice(n * 512, (n + 1) * 512)
-            nc.vector.tensor_tensor(out=o[:], in0=ys[(r, n)][:], in1=cb[:, cols], op=ALU.add)
+            if engine == "v":
+                nc.vector.tensor_tensor(out=o[:], in0=ys[(r, n)][:], in1=cb[:, cols], op=ALU.add)
+            else:
+                e = stage.tile([P, BANK], F32, name="ye")
+                nc.scalar.copy(out=e[:], in_=ys[(r, n)][:])
+                nc.gpsimd.tensor_tensor(out=o[:], in0=e[:], in1=cb[:, cols], op=ALU.add)
             nc.sync.dma_start(out=out[r * P : (r + 1) * P, cols], in_=o[:])
 
-        spare = bank(3)
+        spare = bank(2)
 
         def keep_warm(times):
             for i in range(times):
@@ -273,8 +286,11 @@ def tile_maxout_then_linear_f7_kernel(tc, x_bytes, x_scale, w_words, w_scales, b
         def head_mul(i):
             for g in range(2):
                 for s in range(2):
-                    for j in range(PIECES):
+                    for j in (0, 2):
                         z_pass(s, j, g, i * P, (i + 1) * P)
+            for s in range(2):
+                for g in range(2):
+                    z_pass(s, 1, g, i * P, (i + 1) * P)
 
         keep_warm(4)
         x_cast(0, 0, "v")
@@ -313,60 +329,59 @@ def tile_maxout_then_linear_f7_kernel(tc, x_bytes, x_scale, w_words, w_scales, b
                 x_turn(2 * a, g, 6 + g)
                 x_turn(2 * a + 1, g, 6 + g)
 
-        turns = {2: 1, 5: 2, 9: 3}
-        y_tiles = {13: [(0, 0)], 15: [(0, 1)], 17: [(1, 0)], 18: [(1, 1)], 20: [(2, 0)], 21: [(2, 1)], 22: [(3, 0)], 23: [(3, 1)]}
+        def y_step(r, n):
+            y_mul(r, n, 6 + n)
+
+        on_tensor = {2: [(turn_pair, 1)], 7: [(turn_pair, 2)], 10: [(turn_pair, 3)], 15: [(y_step, 0, 0)], 16: [(y_step, 0, 1)], 17: [(y_step, 1, 0)], 19: [(y_step, 1, 1)], 20: [(y_step, 2, 0)], 21: [(y_step, 2, 1)]}
+        on_scalar = {2: [(x_out, 1, 0), (x_out, 1, 1)], 7: [(x_out, 2, 0), (x_out, 2, 1)], 10: [(x_out, 3, 0), (x_out, 3, 1)], 19: [(h_weave, 3, 0, "s", 0, P)], 20: [(h_weave, 3, 0, "s", P, PAIR)]}
         before = {
-            0: [(x_prod, 4, 0)], 1: [(x_prod, 4, 1)], 3: [(x_quant, 1, 0)], 4: [(x_quant, 1, 1)], 5: [(x_prod, 6, 0)], 6: [(x_quant, 2, 0), (x_quant, 2, 1)], 7: [(x_prod, 6, 1)],
-            8: [(h_weave, 0, 0, "v")], 10: [(x_quant, 3, 0), (x_quant, 3, 1)], 11: [(h_weave, 0, 1, "v")],
-            14: [(h_weave, 1, 0, "v")], 16: [(h_weave, 2, 0, "v")], 19: [(h_quant, 1, 1, 0, P), (h_weave, 1, 1, "v", P, PAIR)],
-            20: [(h_quant, 1, 1, P, PAIR)], 21: [(h_quant, 2, 1, 0, P)], 22: [(h_quant, 2, 1, P, PAIR)], 23: [(h_quant, 3, 0, 0, P)],
+            0: [(x_prod, 4, 0)], 2: [(x_quant, 1, 0), (x_quant, 1, 1)], 3: [(x_prod, 5, 0)], 4: [(x_prod, 4, 1)], 5: [(x_prod, 5, 1)], 6: [(x_prod, 6, 0)], 8: [(x_quant, 2, 0)], 9: [(x_quant, 2, 1)], 10: [(h_quant, 0, 0)], 12: [(h_quant, 1, 0)], 14: [(h_quant, 0, 1)], 16: [(h_quant, 1, 1)],
+            19: [(h_quant, 2, 0)], 21: [(h_quant, 3, 0, 0, P)], 22: [(h_quant, 3, 0, P, PAIR)],
         }
         after = {
-            0: [(x_prod, 5, 0)], 1: [(x_prod, 5, 1)], 4: [(x_prod, 7, 0)], 7: [(x_prod, 7, 1)],
-            8: [(h_quant, 0, 0)], 11: [(h_quant, 0, 1)], 14: [(h_quant, 1, 0)], 16: [(h_quant, 2, 0)],
+            7: [(x_prod, 7, 0), (x_prod, 6, 1)], 8: [(x_prod, 7, 1)],
+            9: [(h_weave, 0, 0, "v")], 10: [(x_quant, 3, 0), (x_quant, 3, 1)], 11: [(h_weave, 1, 0, "v")], 13: [(h_weave, 0, 1, "v")], 14: [(h_weave, 1, 1, "v")],
+            15: [(y_out, 0, 0)], 16: [(y_out, 0, 1)], 17: [(y_out, 1, 0)], 18: [(h_weave, 2, 0, "v")], 19: [(y_out, 1, 1)], 20: [(y_out, 2, 0)], 21: [(y_out, 2, 1)],
         }
-        on_scalar = {18: [(1, 1, "s", 0, P)], 19: [(2, 1, "s", 0, P)], 20: [(2, 1, "s", P, PAIR)], 22: [(3, 0, "s", 0, P)], 23: [(3, 0, "s", P, PAIR)]}
         for s in range(len(steps)):
             if s >= 2:
                 z_mul(s)
-            if s in turns:
-                turn_pair(turns[s])
-            for r, n in y_tiles.get(s, []):
-                y_mul(r, n, 6 + n)
-            u_out(s, 2 if s in (3, 4, 5, 6, 7, 23) else 3)
-            if s in turns:
-                x_out(turns[s], 0)
-                x_out(turns[s], 1)
+            for job in on_tensor.get(s, []):
+                job[0](*job[1:])
+            u_out(s, 2 if s in (0, 1, 2, 3, 7, 11, 15, 19, 22, 23) else 3)
             for job in on_scalar.get(s, []):
-                h_weave(*job)
+                job[0](*job[1:])
             v_max(s)
             for job in before.get(s, []):
                 job[0](*job[1:])
             h_max(s)
             for job in after.get(s, []):
                 job[0](*job[1:])
-            for r, n in y_tiles.get(s, []):
-                y_out(r, n)
 
-        y_mul(4, 0, 6)
-        y_mul(4, 1, 0)
-        y_mul(5, 0, 1)
-        y_mul(5, 1, 2)
-        y_out(4, 0)
-        h_quant(3, 0, P, PAIR)
-        for r in (6, 7):
-            for n in range(2):
-                y_pass(r, n, 0, (7, 3, 4, 5)[2 * (r - 6) + n])
-        y_out(4, 1)
-        y_out(5, 0)
-        y_out(5, 1)
+        held = [(r, n) for r in (3, 4, 5) for n in range(2)]
+        free = [0, 1, 2, 3, 6, 7, 4, 5]
+        last = [(r, n) for r in (6, 7) for n in range(2)]
+        y_mul(3, 0, free[0])
+        y_mul(3, 1, free[1])
+        h_weave(2, 1, "s", 0, P)
+        h_weave(2, 1, "s", P, PAIR)
+        h_quant(2, 1, 0, P)
+        y_out(3, 0, "v")
+        h_quant(2, 1, P, PAIR)
+        for i in range(2, 6):
+            y_mul(*held[i], free[i])
+        y_out(3, 1, "v")
+        y_out(4, 0, "v")
+        for i, tile in enumerate(last):
+            y_pass(*tile, 0, free[(6 + i) % 8])
+        y_out(4, 1, "v")
+        y_out(5, 0, "v")
+        h_weave(3, 1, "s", 0, P)
         h_weave(3, 1, "s", P, PAIR)
-        h_weave(3, 1, "v", 0, P)
         h_quant(3, 1, 0, P)
+        y_out(5, 1)
         h_quant(3, 1, P, PAIR)
-        for r in (6, 7):
-            for n in range(2):
-                y_pass(r, n, 1, 0)
-        for r in (6, 7):
-            for n in range(2):
-                y_out(r, n)
+        for tile in last:
+            y_pass(*tile, 1, 0)
+        for tile in last:
+            y_out(*tile)

@@ -51,6 +51,7 @@ def tile_maxout_then_linear_f7_kernel(tc, x_bytes, x_scale, w_words, w_scales, b
         bf32 = keep.tile([P, P], F32, name="bf32")
         warm = keep.tile([P, BANK], BF16, name="warm")
 
+        nc.scalar.dma_start(out=sc[:], in_=x_scale.rearrange("o (g p t) -> p (o g) t", g=2, t=4))
         nc.vector.memset(warm[:], 0.0)
         nc.vector.memset(ws[:].rearrange("p g n -> p (g n)").bitcast(U32), 0)
         make_identity(nc, ident[:])
@@ -78,13 +79,12 @@ def tile_maxout_then_linear_f7_kernel(tc, x_bytes, x_scale, w_words, w_scales, b
 
         rows = b.rearrange("j (t p) -> (j t) p", p=P)
         load_x(0)
-        nc.sync.dma_start(out=sc[:], in_=x_scale.rearrange("o (g p t) -> p (o g) t", g=2, t=4))
         load_x(1)
+        load_pair(1)
         load_scales(ws, w_scales)
         load_w(0)
         nc.sync.dma_start(out=braw[0:16, :], in_=rows[0:16])
         nc.sync.dma_start(out=braw[16:24, :], in_=rows[16:24])
-        load_pair(1)
         load_w(1)
         load_pair(2)
         load_w(2)
@@ -103,19 +103,23 @@ def tile_maxout_then_linear_f7_kernel(tc, x_bytes, x_scale, w_words, w_scales, b
 
         xw, xt, xg = {}, {}, {}
 
-        def spread_scales(g, where):
+        def spread_turn(g, where):
             t = bank(where)
+            xt[("spread", g)] = t
             for e in range(4):
                 nc.tensor.transpose(t[:, e * P : (e + 1) * P], sc[:, g, e : e + 1].to_broadcast([P, P]), ident[:])
+
+        def spread_out(g):
+            t = xt[("spread", g)]
             nc.scalar.copy(out=spread[:, g].rearrange("m (p t) -> m p t", t=4), in_=t[:].rearrange("m (t p) -> m p t", t=4))
 
         def x_prod(i, g):
-            w = stage.tile([P, 512], BF16, name="xw", align_bytes=64, bufs=6)
+            w = stage.tile([P, 512], BF16, name="xw", align_bytes=64, bufs=8)
             xw[(i, g)] = w
             nc.vector.tensor_tensor(out=w[:], in0=xb[i][:, g * 512 : (g + 1) * 512].bitcast(E4M3), in1=spread[:, g], op=ALU.mult)
 
         def x_cast(i, g, engine):
-            w = stage.tile([P, 512], BF16, name="xw", align_bytes=64, bufs=6)
+            w = stage.tile([P, 512], BF16, name="xw", align_bytes=64, bufs=8)
             xw[(i, g)] = w
             if engine == "v":
                 nc.vector.tensor_copy(out=w[:], in_=xb[i][:, g * 512 : (g + 1) * 512].bitcast(E4M3))
@@ -277,34 +281,26 @@ def tile_maxout_then_linear_f7_kernel(tc, x_bytes, x_scale, w_words, w_scales, b
                 nc.gpsimd.tensor_tensor(out=o[:], in0=e[:], in1=cb[:, cols], op=ALU.add)
             nc.sync.dma_start(out=out[r * P : (r + 1) * P, cols], in_=o[:])
 
-        spare = bank(2)
+        spare = bank(4)
 
         def keep_warm(times):
             for i in range(times):
                 nc.tensor.matmul(spare[:], lhsT=warm[:, 0:P], rhs=warm[:], start=True, stop=True)
 
-        def head_mul(i):
-            for g in range(2):
-                for s in range(2):
-                    for j in (0, 2):
-                        z_pass(s, j, g, i * P, (i + 1) * P)
-            for s in range(2):
-                for g in range(2):
-                    z_pass(s, 1, g, i * P, (i + 1) * P)
-
-        keep_warm(4)
-        x_cast(0, 0, "v")
-        x_cast(0, 1, "v")
-        x_cast(1, 0, "s")
-        x_cast(1, 1, "s")
-        head_turn(0, 0, 6)
-        head_turn(0, 1, 6)
-        spread_scales(0, 4)
-        keep_warm(1)
-        spread_scales(1, 5)
-        head_turn(1, 0, 7)
-        head_turn(1, 1, 7)
-        keep_warm(2)
+        keep_warm(3)
+        spread_turn(0, 2)
+        spread_turn(1, 3)
+        for i in range(2):
+            x_cast(i, 0, "v")
+            x_cast(i, 1, "v")
+        for g in range(2):
+            spread_out(g)
+            x_cast(2 + g, 0, "s")
+            x_cast(2 + g, 1, "s")
+        for i, where in enumerate((6, 7, 5)):
+            head_turn(i, 0, where)
+            head_turn(i, 1, where)
+            keep_warm(1)
         head_out(0, 0)
         head_out(0, 1)
         head_quant(0, 0)
@@ -312,17 +308,31 @@ def tile_maxout_then_linear_f7_kernel(tc, x_bytes, x_scale, w_words, w_scales, b
         head_quant(0, 1)
         head_out(1, 1)
         head_quant(1, 0)
-        x_prod(2, 0)
+        head_out(2, 0)
         head_quant(1, 1)
         nc.scalar.copy(out=bf32[:], in_=braw[:])
-        head_mul(0)
-        turned = bank(6)
+        for g in range(2):
+            for s in range(2):
+                for j in (0, 2):
+                    z_pass(s, j, g, 0, P)
+        for s in range(2):
+            for g in range(2):
+                z_pass(s, 1, g, 0, P)
+        head_turn(3, 0, 6)
+        head_turn(3, 1, 6)
+        turned = bank(7)
         nc.tensor.transpose(turned[:, 0:P], bf32[:], ident[:])
         nc.scalar.copy(out=bias[:], in_=turned[:, 0:24])
-        head_mul(1)
-        x_prod(3, 0)
-        x_prod(2, 1)
-        x_prod(3, 1)
+        for s in range(2):
+            for j in range(PIECES):
+                for g in range(2):
+                    z_pass(s, j, g, P, PAIR)
+        head_out(2, 1)
+        head_quant(2, 0)
+        head_out(3, 0)
+        head_quant(2, 1)
+        head_out(3, 1)
+        head_quant(3, 0)
 
         def turn_pair(a):
             for g in range(2):
@@ -332,10 +342,10 @@ def tile_maxout_then_linear_f7_kernel(tc, x_bytes, x_scale, w_words, w_scales, b
         def y_step(r, n):
             y_mul(r, n, 6 + n)
 
-        on_tensor = {2: [(turn_pair, 1)], 7: [(turn_pair, 2)], 10: [(turn_pair, 3)], 15: [(y_step, 0, 0)], 16: [(y_step, 0, 1)], 17: [(y_step, 1, 0)], 19: [(y_step, 1, 1)], 20: [(y_step, 2, 0)], 21: [(y_step, 2, 1)]}
-        on_scalar = {2: [(x_out, 1, 0), (x_out, 1, 1)], 7: [(x_out, 2, 0), (x_out, 2, 1)], 10: [(x_out, 3, 0), (x_out, 3, 1)], 19: [(h_weave, 3, 0, "s", 0, P)], 20: [(h_weave, 3, 0, "s", P, PAIR)]}
+        on_tensor = {7: [(turn_pair, 2)], 10: [(turn_pair, 3)], 15: [(y_step, 0, 0)], 16: [(y_step, 0, 1)], 17: [(y_step, 1, 0)], 19: [(y_step, 1, 1)], 20: [(y_step, 2, 0)], 21: [(y_step, 2, 1)]}
+        on_scalar = {7: [(x_out, 2, 0), (x_out, 2, 1)], 10: [(x_out, 3, 0), (x_out, 3, 1)], 19: [(h_weave, 3, 0, "s", 0, P)], 20: [(h_weave, 3, 0, "s", P, PAIR)]}
         before = {
-            0: [(x_prod, 4, 0)], 2: [(x_quant, 1, 0), (x_quant, 1, 1)], 3: [(x_prod, 5, 0)], 4: [(x_prod, 4, 1)], 5: [(x_prod, 5, 1)], 6: [(x_prod, 6, 0)], 8: [(x_quant, 2, 0)], 9: [(x_quant, 2, 1)], 10: [(h_quant, 0, 0)], 12: [(h_quant, 1, 0)], 14: [(h_quant, 0, 1)], 16: [(h_quant, 1, 1)],
+            0: [(head_quant, 3, 1)], 1: [(x_prod, 4, 0)], 2: [(x_prod, 5, 0)], 4: [(x_prod, 4, 1)], 5: [(x_prod, 5, 1)], 6: [(x_prod, 6, 0)], 8: [(x_quant, 2, 0)], 9: [(x_quant, 2, 1)], 10: [(h_quant, 0, 0)], 12: [(h_quant, 1, 0)], 14: [(h_quant, 0, 1)], 16: [(h_quant, 1, 1)],
             19: [(h_quant, 2, 0)], 21: [(h_quant, 3, 0, 0, P)], 22: [(h_quant, 3, 0, P, PAIR)],
         }
         after = {
@@ -348,7 +358,7 @@ def tile_maxout_then_linear_f7_kernel(tc, x_bytes, x_scale, w_words, w_scales, b
                 z_mul(s)
             for job in on_tensor.get(s, []):
                 job[0](*job[1:])
-            u_out(s, 2 if s in (0, 1, 2, 3, 7, 11, 15, 19, 22, 23) else 3)
+            u_out(s, 2 if s in (3, 7, 11, 15, 19, 22, 23) else 3)
             for job in on_scalar.get(s, []):
                 job[0](*job[1:])
             v_max(s)

@@ -21,6 +21,7 @@ P = 128
 BANK = 512
 PAIR = 2 * P
 TILES = F // P
+EARLY = 6
 
 
 def tile_maxout_then_linear_f7_kernel(tc, x_bytes, x_scale, w_words, w_scales, b, v_words, v_scales, c, out):
@@ -43,7 +44,10 @@ def tile_maxout_then_linear_f7_kernel(tc, x_bytes, x_scale, w_words, w_scales, b
         xb0 = [keep.tile([P, K], U8, name="xb%d" % i, align_bytes=64) for i in range(2)]
         xb2 = [keep.tile([P, 2, K], U8, name="xbb%d" % i, align_bytes=64) for i in range(3)]
         xb = xb0 + [xb2[i // 2][:, i % 2] for i in range(6)]
-        wq = [keep.tile([P, 2, PIECES, 512], U8, name="wq%d" % i, align_bytes=256) for i in range(4)]
+        wa = keep.tile([P, 2, 2 * EARLY * P], U8, name="wa", align_bytes=256)
+        wb = keep.tile([P, 2, 2, 1024], U8, name="wb", align_bytes=256)
+        wc = keep.tile([P, 2, 2 * (TILES - EARLY) * P], U8, name="wc", align_bytes=256)
+        wd = keep.tile([P, 2, 2, 1024], U8, name="wd", align_bytes=256)
         vt = keep.tile([P, 2, 4 * N], U8, name="vt", align_bytes=256)
         cb = keep.tile([P, N], BF16, name="cb")
         spread = keep.tile([P, 2, 512], F32, name="spread", align_bytes=64)
@@ -64,33 +68,34 @@ def tile_maxout_then_linear_f7_kernel(tc, x_bytes, x_scale, w_words, w_scales, b
         def load_pair(a):
             nc.sync.dma_start(out=xb2[a - 1][:], in_=x_bytes[a * PAIR : (a + 1) * PAIR, :].rearrange("(r p) k -> p r k", p=P))
 
-        def load_w(q):
+        def load_w(tile, pieces, lo, hi):
             for g in range(2):
                 nc.sync.dma_start(
-                    out=wq[q][:, g].bitcast(I32),
-                    in_=w_words[g].rearrange("p (j n) -> p j n", j=PIECES)[:, :, q * 512 : (q + 1) * 512].bitcast(I32),
+                    out=tile[:, g].bitcast(I32),
+                    in_=w_words[g].rearrange("p (j n) -> p j n", j=PIECES)[:, pieces, 2 * lo : 2 * hi].bitcast(I32),
                 )
 
-        def load_scales(tile, scales):
+        def load_scales(tile, scales, lo, hi):
             for i in range(4):
                 nc.sync.dma_start(
-                    out=tile[i:P:32].bitcast(I32), in_=scales[:, i:16:4, :].rearrange("g q n -> q g n").bitcast(I32)
+                    out=tile[i:P:32, :, lo:hi].bitcast(I32), in_=scales[:, i:16:4, lo:hi].rearrange("g q n -> q g n").bitcast(I32)
                 )
 
         rows = b.rearrange("j (t p) -> (j t) p", p=P)
         load_x(0)
         load_x(1)
         load_pair(1)
-        load_scales(ws, w_scales)
-        load_w(0)
+        load_scales(ws, w_scales, 0, EARLY * P)
+        load_w(wa, 0, 0, EARLY * P)
         nc.sync.dma_start(out=braw[0:16, :], in_=rows[0:16])
         nc.sync.dma_start(out=braw[16:24, :], in_=rows[16:24])
-        load_w(1)
+        load_scales(ws, w_scales, EARLY * P, PIECES * F)
+        load_w(wb, slice(1, 3), 0, 512)
         load_pair(2)
-        load_w(2)
+        load_w(wd, slice(1, 3), 512, F)
         load_pair(3)
-        load_w(3)
-        load_scales(vs, v_scales)
+        load_w(wc, 0, EARLY * P, F)
+        load_scales(vs, v_scales, 0, N)
         for g in range(2):
             nc.sync.dma_start(out=vt[:, g].bitcast(I32), in_=v_words[g].rearrange("p n t -> p (n t)").bitcast(I32))
         nc.sync.dma_start(out=cb[:], in_=c.partition_broadcast(P))
@@ -174,58 +179,87 @@ def tile_maxout_then_linear_f7_kernel(tc, x_bytes, x_scale, w_words, w_scales, b
         steps = [(a, 1, T) for a in (0, 1) for T in range(4)] + [(0, 2, T) for T in range(4, 8)]
         steps = steps + [(2, 2, T) for T in range(4)] + [(a, 1, T) for a in (2, 3) for T in range(4, 8)]
         zs, us, vv, hp, hg, whole = {}, {}, {}, {}, {}, {}
+        early = [keep.tile([P, PAIR if T < 4 else BANK], BF16, name="early%d" % T, align_bytes=64) for T in range(EARLY)]
 
-        def z_pass(s, j, g, lo=0, hi=None):
-            a, pairs, T = steps[s]
-            ch, at = chunk_of[a]
-            if g == 0 and lo == 0 and pairs == 2:
-                zs[(s, j)] = bank(3 * (s % 2) + j)
-            elif g == 0 and lo == 0 and j != 1:
-                t = bank(2 * (s % 3) + j // 2)
-                zs[(s, j)] = t[:, 0:PAIR]
-                if j == 0:
-                    zs[(s, 1)] = t[:, PAIR:BANK]
-            col = (T % 2) * 256
-            hi = hi or pairs * PAIR
-            cols = slice(at + lo, at + hi)
+        turn = [0]
+
+        def next_bank():
+            turn[0] = (turn[0] + 1) % 6
+            return bank((turn[0] - 1) % 6)
+
+        def w_tile(T, j, g):
+            if j == 0:
+                return wa[:, g, 256 * T : 256 * (T + 1)] if T < EARLY else wc[:, g, 256 * (T - EARLY) : 256 * (T - EARLY + 1)]
+            return (wb if T < 4 else wd)[:, g, j - 1, 256 * (T % 4) : 256 * (T % 4 + 1)]
+
+        def z_pass(dst, T, j, g, first, n):
+            half, at = first // BANK, first % BANK
             nc.tensor.matmul_mx(
-                out=zs[(s, j)][:, lo:hi],
-                lhsT=wq[T // 2][:, g, j, col : col + 256].bitcast(FP4X4),
+                out=dst,
+                lhsT=w_tile(T, j, g).bitcast(FP4X4),
                 lhsT_scale=ws[:, g, j * F + T * P : j * F + (T + 1) * P],
-                rhs=xc[ch][:, g, cols].bitcast(FP8X4),
-                rhs_scale=xcs[ch][:, g, cols],
+                rhs=xc[half][:, g, at : at + n].bitcast(FP8X4),
+                rhs_scale=xcs[half][:, g, at : at + n],
                 start=(g == 0),
                 stop=(g == 1),
             )
 
         def z_mul(s):
+            a, pairs, T = steps[s]
+            done = a == 0 and T < EARLY
+            shared = None
             for j in range(PIECES):
+                first, n = a * PAIR, pairs * PAIR
+                if j == 0 and done:
+                    if pairs == 1:
+                        continue
+                    first, n = PAIR, PAIR
+                if pairs == 2 or s == len(steps) - 1:
+                    dst = next_bank()[:, 0:n]
+                elif shared is None:
+                    shared = next_bank()
+                    dst = shared[:, 0:n]
+                else:
+                    dst = shared[:, PAIR:BANK]
+                    shared = None
+                zs[(s, j)] = dst
                 for g in range(2):
-                    z_pass(s, j, g)
+                    z_pass(dst, T, j, g, first, n)
+
+        def u_piece(dst, src, T, j):
+            nc.scalar.activation(out=dst, in_=src, func=ACT.Identity, bias=bias[:, 8 * j + T : 8 * j + T + 1])
 
         def u_out(s, pieces):
             a, pairs, T = steps[s]
-            n = pairs * PAIR
             us[s] = []
             for j in range(pieces):
-                u = stage.tile([P, n], BF16, name="u%d" % j, align_bytes=64)
-                nc.scalar.activation(out=u[:], in_=zs[(s, j)][:, 0:n], func=ACT.Identity, bias=bias[:, 8 * j + T : 8 * j + T + 1])
+                if j == 0 and a == 0 and T < EARLY:
+                    u = early[T]
+                    if pairs == 2:
+                        u_piece(u[:, PAIR:BANK], zs[(s, j)], T, j)
+                else:
+                    u = stage.tile([P, pairs * PAIR], BF16, name="u%d" % j, align_bytes=64)
+                    u_piece(u[:], zs[(s, j)], T, j)
                 us[s].append(u)
 
-        def v_max(s):
-            v = stage.tile([P, steps[s][1] * PAIR], BF16, name="v", align_bytes=64)
-            nc.vector.tensor_tensor(out=v[:], in0=us[s][0][:], in1=us[s][1][:], op=ALU.max)
-            vv[s] = v
+        def v_max(s, lo=0, hi=None):
+            n = steps[s][1] * PAIR
+            if lo == 0:
+                v = stage.tile([P, n], BF16, name="v", align_bytes=64)
+                vv[s] = v
+            cols = slice(lo, hi or n)
+            nc.vector.tensor_tensor(out=vv[s][:, cols], in0=us[s][0][:, cols], in1=us[s][1][:, cols], op=ALU.max)
 
-        def h_max(s):
+        def h_max(s, lo=0, hi=None):
             a, pairs, T = steps[s]
             n = pairs * PAIR
-            h = stage.tile([P, n], BF16, name="h", align_bytes=64, bufs=8)
+            cols = slice(lo, hi or n)
+            h = stage.tile([P, cols.stop - lo], BF16, name="h", align_bytes=64, bufs=8)
             if len(us[s]) == 3:
-                nc.vector.tensor_tensor(out=h[:], in0=us[s][2][:], in1=vv[s][:], op=ALU.max)
+                nc.vector.tensor_tensor(out=h[:], in0=us[s][2][:, cols], in1=vv[s][:, cols], op=ALU.max)
             else:
                 nc.vector.scalar_tensor_tensor(
-                    out=h[:], in0=zs[(s, 2)][:, 0:n], scalar=bias[:, 16 + T : 17 + T], in1=vv[s][:], op0=ALU.add, op1=ALU.max
+                    out=h[:], in0=zs[(s, 2)][:, cols], scalar=bias[:, 16 + T : 17 + T], in1=vv[s][:, cols], op0=ALU.add, op1=ALU.max
                 )
             g, q = T // 4, T % 4
             if q == 0:
@@ -233,7 +267,7 @@ def tile_maxout_then_linear_f7_kernel(tc, x_bytes, x_scale, w_words, w_scales, b
                 whole[(a, g)] = planes
                 for i in range(pairs):
                     hp[(a + i, g)] = planes[:, :, i * PAIR : (i + 1) * PAIR]
-            nc.sync.dma_start(out=whole[(a, g)][32 * q : 32 * q + 32].rearrange("p t m -> p (t m)"), in_=h[:])
+            nc.sync.dma_start(out=whole[(a, g)][32 * q : 32 * q + 32, :, cols], in_=h[:])
 
         def h_weave(a, g, engine, lo=0, hi=PAIR):
             t = stage.tile([P, hi - lo, 4], BF16, name="hg", align_bytes=64)
@@ -281,15 +315,15 @@ def tile_maxout_then_linear_f7_kernel(tc, x_bytes, x_scale, w_words, w_scales, b
                 nc.gpsimd.tensor_tensor(out=o[:], in0=e[:], in1=cb[:, cols], op=ALU.add)
             nc.sync.dma_start(out=out[r * P : (r + 1) * P, cols], in_=o[:])
 
-        spare = bank(4)
+        spare = bank(0)
 
         def keep_warm(times):
             for i in range(times):
                 nc.tensor.matmul(spare[:], lhsT=warm[:, 0:P], rhs=warm[:], start=True, stop=True)
 
         keep_warm(3)
-        spread_turn(0, 2)
-        spread_turn(1, 3)
+        spread_turn(0, 3)
+        spread_turn(1, 4)
         for i in range(2):
             x_cast(i, 0, "v")
             x_cast(i, 1, "v")
@@ -304,35 +338,37 @@ def tile_maxout_then_linear_f7_kernel(tc, x_bytes, x_scale, w_words, w_scales, b
         head_out(0, 0)
         head_out(0, 1)
         head_quant(0, 0)
-        head_out(1, 0)
         head_quant(0, 1)
+        head_out(1, 0)
         head_out(1, 1)
         head_quant(1, 0)
         head_out(2, 0)
         head_quant(1, 1)
         nc.scalar.copy(out=bf32[:], in_=braw[:])
-        for g in range(2):
-            for s in range(2):
-                for j in (0, 2):
-                    z_pass(s, j, g, 0, P)
-        for s in range(2):
+        first = [next_bank() for i in range(EARLY // 2)]
+        for odd in range(2):
             for g in range(2):
-                z_pass(s, 1, g, 0, P)
+                for i in range(EARLY // 2):
+                    z_pass(first[i][:, odd * PAIR : odd * PAIR + P], 2 * i + odd, 0, g, 0, P)
         head_turn(3, 0, 6)
         head_turn(3, 1, 6)
         turned = bank(7)
         nc.tensor.transpose(turned[:, 0:P], bf32[:], ident[:])
         nc.scalar.copy(out=bias[:], in_=turned[:, 0:24])
-        for s in range(2):
-            for j in range(PIECES):
-                for g in range(2):
-                    z_pass(s, j, g, P, PAIR)
+        for T in range(EARLY):
+            for g in range(2):
+                z_pass(first[T // 2][:, (T % 2) * PAIR + P : (T % 2 + 1) * PAIR], T, 0, g, P, P)
+        for T in range(EARLY):
+            u_piece(early[T][:, 0:PAIR], first[T // 2][:, (T % 2) * PAIR : (T % 2 + 1) * PAIR], T, 0)
         head_out(2, 1)
         head_quant(2, 0)
         head_out(3, 0)
         head_quant(2, 1)
         head_out(3, 1)
         head_quant(3, 0)
+        x_prod(4, 0)
+        head_quant(3, 1)
+        x_prod(5, 0)
 
         def turn_pair(a):
             for g in range(2):
@@ -345,22 +381,23 @@ def tile_maxout_then_linear_f7_kernel(tc, x_bytes, x_scale, w_words, w_scales, b
         on_tensor = {7: [(turn_pair, 2)], 10: [(turn_pair, 3)], 15: [(y_step, 0, 0)], 16: [(y_step, 0, 1)], 17: [(y_step, 1, 0)], 19: [(y_step, 1, 1)], 20: [(y_step, 2, 0)], 21: [(y_step, 2, 1)]}
         on_scalar = {7: [(x_out, 2, 0), (x_out, 2, 1)], 10: [(x_out, 3, 0), (x_out, 3, 1)], 19: [(h_weave, 3, 0, "s", 0, P)], 20: [(h_weave, 3, 0, "s", P, PAIR)]}
         before = {
-            0: [(head_quant, 3, 1)], 1: [(x_prod, 4, 0)], 2: [(x_prod, 5, 0)], 4: [(x_prod, 4, 1)], 5: [(x_prod, 5, 1)], 6: [(x_prod, 6, 0)], 8: [(x_quant, 2, 0)], 9: [(x_quant, 2, 1)], 10: [(h_quant, 0, 0)], 12: [(h_quant, 1, 0)], 14: [(h_quant, 0, 1)], 16: [(h_quant, 1, 1)],
+            1: [(x_prod, 4, 1)], 4: [(x_prod, 5, 1)], 5: [(x_prod, 6, 0)], 6: [(x_prod, 7, 0)], 8: [(x_quant, 2, 0)], 9: [(x_quant, 2, 1)], 10: [(h_quant, 0, 0)], 12: [(h_quant, 1, 0)], 14: [(h_quant, 0, 1)], 16: [(h_quant, 1, 1)],
             19: [(h_quant, 2, 0)], 21: [(h_quant, 3, 0, 0, P)], 22: [(h_quant, 3, 0, P, PAIR)],
         }
         after = {
-            7: [(x_prod, 7, 0), (x_prod, 6, 1)], 8: [(x_prod, 7, 1)],
+            7: [(x_prod, 6, 1)], 8: [(x_prod, 7, 1)],
             9: [(h_weave, 0, 0, "v")], 10: [(x_quant, 3, 0), (x_quant, 3, 1)], 11: [(h_weave, 1, 0, "v")], 13: [(h_weave, 0, 1, "v")], 14: [(h_weave, 1, 1, "v")],
             15: [(y_out, 0, 0)], 16: [(y_out, 0, 1)], 17: [(y_out, 1, 0)], 18: [(h_weave, 2, 0, "v")], 19: [(y_out, 1, 1)], 20: [(y_out, 2, 0)], 21: [(y_out, 2, 1)],
         }
         for s in range(len(steps)):
-            if s >= 2:
-                z_mul(s)
+            z_mul(s)
             for job in on_tensor.get(s, []):
                 job[0](*job[1:])
-            u_out(s, 2 if s in (3, 7, 11, 15, 19, 22, 23) else 3)
+            u_out(s, 2 if s in (7, 11, 15, 19, 22, 23) else 3)
             for job in on_scalar.get(s, []):
                 job[0](*job[1:])
+            if s == len(steps) - 1:
+                break
             v_max(s)
             for job in before.get(s, []):
                 job[0](*job[1:])
@@ -369,23 +406,27 @@ def tile_maxout_then_linear_f7_kernel(tc, x_bytes, x_scale, w_words, w_scales, b
                 job[0](*job[1:])
 
         held = [(r, n) for r in (3, 4, 5) for n in range(2)]
-        free = [0, 1, 2, 3, 6, 7, 4, 5]
+        free = [2, 6, 7, 3, 4, 5, 0, 1]
         last = [(r, n) for r in (6, 7) for n in range(2)]
+        for lo in (0, P):
+            v_max(s, lo, lo + P)
+        for lo in (0, P):
+            h_max(s, lo, lo + P)
         y_mul(3, 0, free[0])
         y_mul(3, 1, free[1])
         h_weave(2, 1, "s", 0, P)
         h_weave(2, 1, "s", P, PAIR)
         h_quant(2, 1, 0, P)
-        y_out(3, 0, "v")
+        y_out(3, 0)
         h_quant(2, 1, P, PAIR)
         for i in range(2, 6):
             y_mul(*held[i], free[i])
-        y_out(3, 1, "v")
-        y_out(4, 0, "v")
+        y_out(3, 1)
+        y_out(4, 0)
         for i, tile in enumerate(last):
             y_pass(*tile, 0, free[(6 + i) % 8])
-        y_out(4, 1, "v")
-        y_out(5, 0, "v")
+        y_out(4, 1)
+        y_out(5, 0)
         h_weave(3, 1, "s", 0, P)
         h_weave(3, 1, "s", P, PAIR)
         h_quant(3, 1, 0, P)

@@ -18,10 +18,22 @@ ALU = mybir.AluOpType
 ACT = mybir.ActivationFunctionType
 
 P = 128
+PASS = 512
 BANK = 512
 PAIR = 2 * P
 TILES = F // P
+GROUP = 4
+W_TILE = 2 * P
+SUM_BANKS = 6
 EARLY = 6
+
+STEPS = (
+    [(a, 1, T) for a in (0, 1) for T in range(GROUP)]
+    + [(0, 2, T) for T in range(GROUP, TILES)]
+    + [(2, 2, T) for T in range(GROUP)]
+    + [(a, 1, T) for a in (2, 3) for T in range(GROUP, TILES)]
+)
+LAST = len(STEPS) - 1
 
 
 def tile_maxout_then_linear_f7_kernel(tc, x_bytes, x_scale, w_words, w_scales, b, v_words, v_scales, c, out):
@@ -36,43 +48,46 @@ def tile_maxout_then_linear_f7_kernel(tc, x_bytes, x_scale, w_words, w_scales, b
             t = psum.tile([P, BANK], F32, name="bank%d" % i)
             return t
 
-        sc = keep.tile([P, 2, 4], F32, name="sc")
-        ws = keep.tile([P, 2, PIECES * F], U8, name="ws", align_bytes=256)
-        vs = keep.tile([P, 2, N], U8, name="vs", align_bytes=256)
+        taken = []
+
+        def next_sum_bank():
+            taken.append(bank(len(taken) % SUM_BANKS))
+            return taken[-1]
+
+        scale_cols = keep.tile([P, 2, 4], F32, name="scale_cols")
+        w_sc = keep.tile([P, 2, PIECES * F], U8, name="w_sc", align_bytes=256)
+        v_sc = keep.tile([P, 2, N], U8, name="v_sc", align_bytes=256)
         ident = keep.tile([P, P], F32, name="ident")
-        braw = keep.tile([P, P], BF16, name="braw")
-        xb0 = [keep.tile([P, K], U8, name="xb%d" % i, align_bytes=64) for i in range(2)]
-        xb2 = [keep.tile([P, 2, K], U8, name="xbb%d" % i, align_bytes=64) for i in range(3)]
-        xb = xb0 + [xb2[i // 2][:, i % 2] for i in range(6)]
-        wa = keep.tile([P, 2, 2 * EARLY * P], U8, name="wa", align_bytes=256)
-        wb = keep.tile([P, 2, 2, 1024], U8, name="wb", align_bytes=256)
-        wc = keep.tile([P, 2, 2 * (TILES - EARLY) * P], U8, name="wc", align_bytes=256)
-        wd = keep.tile([P, 2, 2, 1024], U8, name="wd", align_bytes=256)
-        vt = keep.tile([P, 2, 4 * N], U8, name="vt", align_bytes=256)
-        cb = keep.tile([P, N], BF16, name="cb")
-        spread = keep.tile([P, 2, 512], F32, name="spread", align_bytes=64)
-        bias = keep.tile([P, 24], F32, name="bias")
-        bf32 = keep.tile([P, P], F32, name="bf32")
-        warm = keep.tile([P, BANK], BF16, name="warm")
+        b_rows = keep.tile([P, P], BF16, name="b_rows")
+        x_single = [keep.tile([P, K], U8, name="x_single%d" % i, align_bytes=64) for i in range(2)]
+        x_pair = [keep.tile([P, 2, K], U8, name="x_pair%d" % i, align_bytes=64) for i in range(3)]
+        x_rows = x_single + [x_pair[i // 2][:, i % 2] for i in range(6)]
+        w_early = keep.tile([P, 2, EARLY * W_TILE], U8, name="w_early", align_bytes=256)
+        w_low = keep.tile([P, 2, 2, GROUP * W_TILE], U8, name="w_low", align_bytes=256)
+        w_rest = keep.tile([P, 2, (TILES - EARLY) * W_TILE], U8, name="w_rest", align_bytes=256)
+        w_high = keep.tile([P, 2, 2, GROUP * W_TILE], U8, name="w_high", align_bytes=256)
+        v_w = keep.tile([P, 2, 4 * N], U8, name="v_w", align_bytes=256)
+        c_all = keep.tile([P, N], BF16, name="c_all")
+        scale_all = keep.tile([P, 2, PASS], F32, name="scale_all", align_bytes=64)
+        bias = keep.tile([P, PIECES * TILES], F32, name="bias")
+        b_f32 = keep.tile([P, P], F32, name="b_f32")
+        zeros = keep.tile([P, BANK], BF16, name="zeros")
 
-        nc.scalar.dma_start(out=sc[:], in_=x_scale.rearrange("o (g p t) -> p (o g) t", g=2, t=4))
-        nc.vector.memset(warm[:], 0.0)
-        nc.vector.memset(ws[:].rearrange("p g n -> p (g n)").bitcast(U32), 0)
+        nc.scalar.dma_start(out=scale_cols[:], in_=x_scale.rearrange("o (g p t) -> p (o g) t", g=2, t=4))
+        nc.vector.memset(zeros[:], 0.0)
+        nc.vector.memset(w_sc[:].rearrange("p g n -> p (g n)").bitcast(U32), 0)
         make_identity(nc, ident[:])
-        nc.scalar.activation(out=braw[:], in_=ident[:], func=ACT.Identity, scale=0.0)
-        nc.gpsimd.memset(vs[:].rearrange("p g n -> p (g n)").bitcast(U32), 0)
-
-        def load_x(i):
-            nc.sync.dma_start(out=xb[i][:], in_=x_bytes[i * P : (i + 1) * P, :])
+        nc.scalar.activation(out=b_rows[:], in_=ident[:], func=ACT.Identity, scale=0.0)
+        nc.gpsimd.memset(v_sc[:].rearrange("p g n -> p (g n)").bitcast(U32), 0)
 
         def load_pair(a):
-            nc.sync.dma_start(out=xb2[a - 1][:], in_=x_bytes[a * PAIR : (a + 1) * PAIR, :].rearrange("(r p) k -> p r k", p=P))
+            nc.sync.dma_start(out=x_pair[a - 1][:], in_=x_bytes[a * PAIR : (a + 1) * PAIR, :].rearrange("(r p) k -> p r k", p=P))
 
         def load_w(tile, pieces, lo, hi):
             for g in range(2):
                 nc.sync.dma_start(
                     out=tile[:, g].bitcast(I32),
-                    in_=w_words[g].rearrange("p (j n) -> p j n", j=PIECES)[:, pieces, 2 * lo : 2 * hi].bitcast(I32),
+                    in_=w_words[g].rearrange("p (j n) -> p j n", j=PIECES)[:, pieces, lo * W_TILE : hi * W_TILE].bitcast(I32),
                 )
 
         def load_scales(tile, scales, lo, hi):
@@ -81,358 +96,345 @@ def tile_maxout_then_linear_f7_kernel(tc, x_bytes, x_scale, w_words, w_scales, b
                     out=tile[i:P:32, :, lo:hi].bitcast(I32), in_=scales[:, i:16:4, lo:hi].rearrange("g q n -> q g n").bitcast(I32)
                 )
 
-        rows = b.rearrange("j (t p) -> (j t) p", p=P)
-        load_x(0)
-        load_x(1)
+        for i in range(2):
+            nc.sync.dma_start(out=x_single[i][:], in_=x_bytes[i * P : (i + 1) * P, :])
         load_pair(1)
-        load_scales(ws, w_scales, 0, EARLY * P)
-        load_w(wa, 0, 0, EARLY * P)
-        nc.sync.dma_start(out=braw[0:16, :], in_=rows[0:16])
-        nc.sync.dma_start(out=braw[16:24, :], in_=rows[16:24])
-        load_scales(ws, w_scales, EARLY * P, PIECES * F)
-        load_w(wb, slice(1, 3), 0, 512)
+        load_scales(w_sc, w_scales, 0, EARLY * P)
+        load_w(w_early, 0, 0, EARLY)
+        for lo, hi in ((0, 16), (16, 24)):
+            nc.sync.dma_start(out=b_rows[lo:hi, :], in_=b.rearrange("j (t p) -> (j t) p", p=P)[lo:hi])
+        load_scales(w_sc, w_scales, EARLY * P, PIECES * F)
+        load_w(w_low, slice(1, PIECES), 0, GROUP)
         load_pair(2)
-        load_w(wd, slice(1, 3), 512, F)
+        load_w(w_high, slice(1, PIECES), GROUP, TILES)
         load_pair(3)
-        load_w(wc, 0, EARLY * P, F)
-        load_scales(vs, v_scales, 0, N)
+        load_w(w_rest, 0, EARLY, TILES)
+        load_scales(v_sc, v_scales, 0, N)
         for g in range(2):
-            nc.sync.dma_start(out=vt[:, g].bitcast(I32), in_=v_words[g].rearrange("p n t -> p (n t)").bitcast(I32))
-        nc.sync.dma_start(out=cb[:], in_=c.partition_broadcast(P))
+            nc.sync.dma_start(out=v_w[:, g].bitcast(I32), in_=v_words[g].rearrange("p n t -> p (n t)").bitcast(I32))
+        nc.sync.dma_start(out=c_all[:], in_=c.partition_broadcast(P))
 
-        xc = [keep.tile([P, 2, BANK], U32, name="xc%d" % i, align_bytes=256) for i in range(2)]
-        xcs = [keep.tile([P, 2, BANK], U8, name="xcs%d" % i, align_bytes=256) for i in range(2)]
-        hc = [keep.tile([P, 2, PAIR], U32, name="hc%d" % i, align_bytes=256) for i in range(4)]
-        hcs = [keep.tile([P, 2, PAIR], U8, name="hcs%d" % i, align_bytes=256) for i in range(4)]
-        chunk_of = [(0, 0), (0, PAIR), (1, 0), (1, PAIR)]
+        x_codes = [keep.tile([P, 2, BANK], U32, name="x_codes%d" % i, align_bytes=256) for i in range(2)]
+        x_sc = [keep.tile([P, 2, BANK], U8, name="x_sc%d" % i, align_bytes=256) for i in range(2)]
+        h_codes = [keep.tile([P, 2, PAIR], U32, name="h_codes%d" % i, align_bytes=256) for i in range(4)]
+        h_sc = [keep.tile([P, 2, PAIR], U8, name="h_sc%d" % i, align_bytes=256) for i in range(4)]
 
-        xw, xt, xg = {}, {}, {}
+        wide, turned, grouped, spread = {}, {}, {}, {}
 
         def spread_turn(g, where):
-            t = bank(where)
-            xt[("spread", g)] = t
-            for e in range(4):
-                nc.tensor.transpose(t[:, e * P : (e + 1) * P], sc[:, g, e : e + 1].to_broadcast([P, P]), ident[:])
+            spread[g] = bank(where)
+            for t in range(4):
+                nc.tensor.transpose(spread[g][:, t * P : (t + 1) * P], scale_cols[:, g, t : t + 1].to_broadcast([P, P]), ident[:])
 
         def spread_out(g):
-            t = xt[("spread", g)]
-            nc.scalar.copy(out=spread[:, g].rearrange("m (p t) -> m p t", t=4), in_=t[:].rearrange("m (t p) -> m p t", t=4))
+            nc.scalar.copy(out=scale_all[:, g].rearrange("m (p t) -> m p t", t=4), in_=spread[g][:].rearrange("m (t p) -> m p t", t=4))
 
-        def x_prod(i, g):
-            w = stage.tile([P, 512], BF16, name="xw", align_bytes=64, bufs=8)
-            xw[(i, g)] = w
-            nc.vector.tensor_tensor(out=w[:], in0=xb[i][:, g * 512 : (g + 1) * 512].bitcast(E4M3), in1=spread[:, g], op=ALU.mult)
+        def x_fp8(i, g):
+            return x_rows[i][:, g * PASS : (g + 1) * PASS].bitcast(E4M3)
 
-        def x_cast(i, g, engine):
-            w = stage.tile([P, 512], BF16, name="xw", align_bytes=64, bufs=8)
-            xw[(i, g)] = w
-            if engine == "v":
-                nc.vector.tensor_copy(out=w[:], in_=xb[i][:, g * 512 : (g + 1) * 512].bitcast(E4M3))
-            else:
-                nc.scalar.copy(out=w[:], in_=xb[i][:, g * 512 : (g + 1) * 512].bitcast(E4M3))
+        def wide_tile(i, g):
+            w = stage.tile([P, PASS], BF16, name="wide", align_bytes=64, bufs=8)
+            wide[(i, g)] = w
+            return w
 
-        def head_turn(i, g, where):
-            if g == 0:
-                xt[i] = bank(where)
-            words = xw[(i, g)][:].bitcast(F32)
+        def x_cast(i, g, copy):
+            copy(out=wide_tile(i, g)[:], in_=x_fp8(i, g))
+
+        def x_product(i, g):
+            nc.vector.tensor_tensor(out=wide_tile(i, g)[:], in0=x_fp8(i, g), in1=scale_all[:, g], op=ALU.mult)
+
+        def row_turn(i, g, where):
+            turned[(i, g)] = where[:, g * PAIR : (g + 1) * PAIR]
+            words = wide[(i, g)][:].bitcast(F32)
             for u in range(2):
-                nc.tensor.transpose(xt[i][:, g * PAIR + u : (g + 1) * PAIR : 2], words[:, u:256:2], ident[:])
+                nc.tensor.transpose(where[:, g * PAIR + u : (g + 1) * PAIR : 2], words[:, u:PAIR:2], ident[:])
 
-        def head_out(i, g):
-            t = stage.tile([P, P, 4], BF16, name="xg", align_bytes=64)
-            xg[(i, g, 0)] = t
+        def row_out(i, g):
+            t = stage.tile([P, P, 4], BF16, name="grouped", align_bytes=64)
+            grouped[(i, g)] = t
             nc.vector.tensor_tensor(
                 out=t[:],
-                in0=xt[i][:, g * PAIR : (g + 1) * PAIR].bitcast(BF16).rearrange("p (m t) -> p m t", t=4),
-                in1=sc[:, g].unsqueeze(1).to_broadcast([P, P, 4]),
+                in0=turned[(i, g)].bitcast(BF16).rearrange("p (m t) -> p m t", t=4),
+                in1=scale_cols[:, g].unsqueeze(1).to_broadcast([P, P, 4]),
                 op=ALU.mult,
             )
 
-        def head_quant(i, g):
+        def x_quant(i, g):
+            t = grouped[(i, g)]
+            cols = slice((i % 4) * P, (i % 4) * P + t.shape[1])
             nc.vector.quantize_mx(
-                out=xc[0][:, g, i * P : (i + 1) * P].bitcast(FP8X4),
-                scales=xcs[0][:, g, i * P : (i + 1) * P],
-                in_=xg[(i, g, 0)][:].rearrange("p m t -> p (m t)"),
+                out=x_codes[i // 4][:, g, cols].bitcast(FP8X4), scales=x_sc[i // 4][:, g, cols], in_=t[:].rearrange("p m t -> p (m t)")
             )
 
-        def x_turn(i, g, where):
-            a, r = i // 2, i % 2
-            if r == 0:
-                xt[(a, g)] = bank(where)
-            words = xw[(i, g)][:].bitcast(F32)
-            for u in range(2):
-                nc.tensor.transpose(xt[(a, g)][:, u * PAIR + r * P : u * PAIR + (r + 1) * P], words[:, u:256:2], ident[:])
+        def pair_turn(a):
+            for g in range(2):
+                turned[(2 * a, g)] = bank(SUM_BANKS + g)
+                for r in range(2):
+                    words = wide[(2 * a + r, g)][:].bitcast(F32)
+                    for u in range(2):
+                        at = u * PAIR + r * P
+                        nc.tensor.transpose(turned[(2 * a, g)][:, at : at + P], words[:, u:PAIR:2], ident[:])
 
-        def x_out(a, g):
-            t = stage.tile([P, PAIR, 4], BF16, name="xg", align_bytes=64)
-            xg[(a, g)] = t
-            nc.scalar.copy(out=t[:].bitcast(F32), in_=xt[(a, g)][:].rearrange("p (u m) -> p m u", u=2))
+        def pair_out(a):
+            for g in range(2):
+                t = stage.tile([P, PAIR, 4], BF16, name="grouped", align_bytes=64)
+                grouped[(2 * a, g)] = t
+                nc.scalar.copy(out=t[:].bitcast(F32), in_=turned[(2 * a, g)][:].rearrange("p (u m) -> p m u", u=2))
 
-        def x_quant(a, g):
-            ch, at = chunk_of[a]
-            nc.vector.quantize_mx(
-                out=xc[ch][:, g, at : at + PAIR].bitcast(FP8X4),
-                scales=xcs[ch][:, g, at : at + PAIR],
-                in_=xg[(a, g)][:].rearrange("p m t -> p (m t)"),
-            )
-
-        steps = [(a, 1, T) for a in (0, 1) for T in range(4)] + [(0, 2, T) for T in range(4, 8)]
-        steps = steps + [(2, 2, T) for T in range(4)] + [(a, 1, T) for a in (2, 3) for T in range(4, 8)]
-        zs, us, vv, hp, hg, whole = {}, {}, {}, {}, {}, {}
-        early = [keep.tile([P, PAIR if T < 4 else BANK], BF16, name="early%d" % T, align_bytes=64) for T in range(EARLY)]
-
-        turn = [0]
-
-        def next_bank():
-            turn[0] = (turn[0] + 1) % 6
-            return bank((turn[0] - 1) % 6)
+        sums, pieces_of, upper, folded, folds, woven = {}, {}, {}, {}, {}, {}
+        early = [keep.tile([P, PAIR if T < GROUP else BANK], BF16, name="early%d" % T, align_bytes=64) for T in range(EARLY)]
 
         def w_tile(T, j, g):
-            if j == 0:
-                return wa[:, g, 256 * T : 256 * (T + 1)] if T < EARLY else wc[:, g, 256 * (T - EARLY) : 256 * (T - EARLY + 1)]
-            return (wb if T < 4 else wd)[:, g, j - 1, 256 * (T % 4) : 256 * (T % 4 + 1)]
+            if j > 0:
+                tile, at = (w_low if T < GROUP else w_high)[:, g, j - 1], T % GROUP
+            elif T < EARLY:
+                tile, at = w_early[:, g], T
+            else:
+                tile, at = w_rest[:, g], T - EARLY
+            return tile[:, at * W_TILE : (at + 1) * W_TILE]
 
         def z_pass(dst, T, j, g, first, n):
             half, at = first // BANK, first % BANK
             nc.tensor.matmul_mx(
                 out=dst,
                 lhsT=w_tile(T, j, g).bitcast(FP4X4),
-                lhsT_scale=ws[:, g, j * F + T * P : j * F + (T + 1) * P],
-                rhs=xc[half][:, g, at : at + n].bitcast(FP8X4),
-                rhs_scale=xcs[half][:, g, at : at + n],
+                lhsT_scale=w_sc[:, g, j * F + T * P : j * F + (T + 1) * P],
+                rhs=x_codes[half][:, g, at : at + n].bitcast(FP8X4),
+                rhs_scale=x_sc[half][:, g, at : at + n],
                 start=(g == 0),
                 stop=(g == 1),
             )
 
-        def z_mul(s):
-            a, pairs, T = steps[s]
-            done = a == 0 and T < EARLY
+        def z_step(s):
+            a, pairs, T = STEPS[s]
             shared = None
             for j in range(PIECES):
                 first, n = a * PAIR, pairs * PAIR
-                if j == 0 and done:
+                if j == 0 and a == 0 and T < EARLY:
                     if pairs == 1:
                         continue
                     first, n = PAIR, PAIR
-                if pairs == 2 or s == len(steps) - 1:
-                    dst = next_bank()[:, 0:n]
+                if pairs == 2 or s == LAST:
+                    dst = next_sum_bank()[:, 0:n]
                 elif shared is None:
-                    shared = next_bank()
+                    shared = next_sum_bank()
                     dst = shared[:, 0:n]
                 else:
                     dst = shared[:, PAIR:BANK]
                     shared = None
-                zs[(s, j)] = dst
+                sums[(s, j)] = dst
                 for g in range(2):
                     z_pass(dst, T, j, g, first, n)
 
-        def u_piece(dst, src, T, j):
-            nc.scalar.activation(out=dst, in_=src, func=ACT.Identity, bias=bias[:, 8 * j + T : 8 * j + T + 1])
+        def piece_out(dst, src, T, j):
+            col = TILES * j + T
+            nc.scalar.activation(out=dst, in_=src, func=ACT.Identity, bias=bias[:, col : col + 1])
 
-        def u_out(s, pieces):
-            a, pairs, T = steps[s]
-            us[s] = []
-            for j in range(pieces):
+        def pieces_out(s, count):
+            a, pairs, T = STEPS[s]
+            pieces_of[s] = []
+            for j in range(count):
                 if j == 0 and a == 0 and T < EARLY:
                     u = early[T]
                     if pairs == 2:
-                        u_piece(u[:, PAIR:BANK], zs[(s, j)], T, j)
+                        piece_out(u[:, PAIR:BANK], sums[(s, j)], T, j)
                 else:
-                    u = stage.tile([P, pairs * PAIR], BF16, name="u%d" % j, align_bytes=64)
-                    u_piece(u[:], zs[(s, j)], T, j)
-                us[s].append(u)
+                    u = stage.tile([P, pairs * PAIR], BF16, name="piece%d" % j, align_bytes=64)
+                    piece_out(u[:], sums[(s, j)], T, j)
+                pieces_of[s].append(u)
 
-        def v_max(s, lo=0, hi=None):
-            n = steps[s][1] * PAIR
+        def first_max(s, lo, hi):
             if lo == 0:
-                v = stage.tile([P, n], BF16, name="v", align_bytes=64)
-                vv[s] = v
-            cols = slice(lo, hi or n)
-            nc.vector.tensor_tensor(out=vv[s][:, cols], in0=us[s][0][:, cols], in1=us[s][1][:, cols], op=ALU.max)
+                v = stage.tile([P, STEPS[s][1] * PAIR], BF16, name="upper", align_bytes=64)
+                upper[s] = v
+            nc.vector.tensor_tensor(out=upper[s][:, lo:hi], in0=pieces_of[s][0][:, lo:hi], in1=pieces_of[s][1][:, lo:hi], op=ALU.max)
 
-        def h_max(s, lo=0, hi=None):
-            a, pairs, T = steps[s]
-            n = pairs * PAIR
-            cols = slice(lo, hi or n)
-            h = stage.tile([P, cols.stop - lo], BF16, name="h", align_bytes=64, bufs=8)
-            if len(us[s]) == 3:
-                nc.vector.tensor_tensor(out=h[:], in0=us[s][2][:, cols], in1=vv[s][:, cols], op=ALU.max)
+        def second_max(s, lo, hi):
+            a, pairs, T = STEPS[s]
+            h = stage.tile([P, hi - lo], BF16, name="h", align_bytes=64, bufs=8)
+            if len(pieces_of[s]) == PIECES:
+                nc.vector.tensor_tensor(out=h[:], in0=pieces_of[s][2][:, lo:hi], in1=upper[s][:, lo:hi], op=ALU.max)
             else:
+                col = 2 * TILES + T
                 nc.vector.scalar_tensor_tensor(
-                    out=h[:], in0=zs[(s, 2)][:, cols], scalar=bias[:, 16 + T : 17 + T], in1=vv[s][:, cols], op0=ALU.add, op1=ALU.max
+                    out=h[:], in0=sums[(s, 2)][:, lo:hi], scalar=bias[:, col : col + 1], in1=upper[s][:, lo:hi], op0=ALU.add, op1=ALU.max
                 )
-            g, q = T // 4, T % 4
+            g, q = T // GROUP, T % GROUP
             if q == 0:
-                planes = keep.tile([P, 4, n], BF16, name="hp%d_%d" % (a, g), align_bytes=64)
-                whole[(a, g)] = planes
+                fold = keep.tile([P, 4, pairs * PAIR], BF16, name="fold%d_%d" % (a, g), align_bytes=64)
+                folds[(a, g)] = fold
                 for i in range(pairs):
-                    hp[(a + i, g)] = planes[:, :, i * PAIR : (i + 1) * PAIR]
-            nc.sync.dma_start(out=whole[(a, g)][32 * q : 32 * q + 32, :, cols], in_=h[:])
+                    folded[(a + i, g)] = fold[:, :, i * PAIR : (i + 1) * PAIR]
+            nc.sync.dma_start(out=folds[(a, g)][32 * q : 32 * q + 32, :, lo:hi], in_=h[:])
 
-        def h_weave(a, g, engine, lo=0, hi=PAIR):
-            t = stage.tile([P, hi - lo, 4], BF16, name="hg", align_bytes=64)
-            src = hp[(a, g)][:, :, lo:hi].rearrange("p t (c i) -> p c t i", i=4)
-            dst = t[:].rearrange("p (c i) t -> p c t i", i=4)
-            if engine == "v":
-                nc.vector.tensor_copy(out=dst, in_=src)
-            else:
-                nc.scalar.copy(out=dst, in_=src)
-            hg[(a, g, lo)] = t
+        def h_weave(a, g, lo, hi, copy):
+            t = stage.tile([P, hi - lo, 4], BF16, name="woven", align_bytes=64)
+            woven[(a, g, lo)] = t
+            copy(out=t[:].rearrange("p (c i) t -> p c t i", i=4), in_=folded[(a, g)][:, :, lo:hi].rearrange("p t (c i) -> p c t i", i=4))
 
-        def h_quant(a, g, lo=0, hi=PAIR):
+        def h_quant(a, g, lo, hi):
             nc.vector.quantize_mx(
-                out=hc[a][:, g, lo:hi].bitcast(FP8X4), scales=hcs[a][:, g, lo:hi], in_=hg[(a, g, lo)][:].rearrange("p m t -> p (m t)")
+                out=h_codes[a][:, g, lo:hi].bitcast(FP8X4), scales=h_sc[a][:, g, lo:hi], in_=woven[(a, g, lo)][:].rearrange("p m t -> p (m t)")
             )
 
-        ys = {}
+        y_sums = {}
 
-        def y_pass(r, n, g, where):
-            if g == 0:
-                ys[(r, n)] = bank(where)
-            cols = slice((r % 2) * P, (r % 2 + 1) * P)
+        def y_pass(r, n, g):
+            rows = slice((r % 2) * P, (r % 2 + 1) * P)
             nc.tensor.matmul_mx(
-                out=ys[(r, n)][:],
-                lhsT=hc[r // 2][:, g, cols].bitcast(FP8X4),
-                lhsT_scale=hcs[r // 2][:, g, cols],
-                rhs=vt[:, g, n * 2048 : (n + 1) * 2048].bitcast(FP8X4),
-                rhs_scale=vs[:, g, n * 512 : (n + 1) * 512],
+                out=y_sums[(r, n)][:],
+                lhsT=h_codes[r // 2][:, g, rows].bitcast(FP8X4),
+                lhsT_scale=h_sc[r // 2][:, g, rows],
+                rhs=v_w[:, g, 4 * n * BANK : 4 * (n + 1) * BANK].bitcast(FP8X4),
+                rhs_scale=v_sc[:, g, n * BANK : (n + 1) * BANK],
                 start=(g == 0),
                 stop=(g == 1),
             )
 
-        def y_mul(r, n, where):
-            y_pass(r, n, 0, where)
-            y_pass(r, n, 1, where)
+        def y_open(r, n, where):
+            y_sums[(r, n)] = bank(where)
+            y_pass(r, n, 0)
 
-        def y_out(r, n, engine="v"):
-            o = stage.tile([P, BANK], F32, name="yt", bufs=8)
-            cols = slice(n * 512, (n + 1) * 512)
-            if engine == "v":
-                nc.vector.tensor_tensor(out=o[:], in0=ys[(r, n)][:], in1=cb[:, cols], op=ALU.add)
-            else:
-                e = stage.tile([P, BANK], F32, name="ye")
-                nc.scalar.copy(out=e[:], in_=ys[(r, n)][:])
-                nc.gpsimd.tensor_tensor(out=o[:], in0=e[:], in1=cb[:, cols], op=ALU.add)
+        def y_mul(r, n, where):
+            y_open(r, n, where)
+            y_pass(r, n, 1)
+
+        def y_out(r, n):
+            o = stage.tile([P, BANK], F32, name="y", bufs=8)
+            cols = slice(n * BANK, (n + 1) * BANK)
+            nc.vector.tensor_tensor(out=o[:], in0=y_sums[(r, n)][:], in1=c_all[:, cols], op=ALU.add)
             nc.sync.dma_start(out=out[r * P : (r + 1) * P, cols], in_=o[:])
 
-        spare = bank(0)
+        idle_bank = bank(0)
 
-        def keep_warm(times):
+        def warm_up(times):
             for i in range(times):
-                nc.tensor.matmul(spare[:], lhsT=warm[:, 0:P], rhs=warm[:], start=True, stop=True)
+                nc.tensor.matmul(idle_bank[:], lhsT=zeros[:, 0:P], rhs=zeros[:], start=True, stop=True)
 
-        keep_warm(3)
+        on_vector, on_scalar = nc.vector.tensor_copy, nc.scalar.copy
+        warm_up(3)
         spread_turn(0, 3)
         spread_turn(1, 4)
+        warm_up(1)
+        halves = [(i, g) for i in range(4) for g in range(2)]
+        for i, g in halves[:3]:
+            x_cast(i, g, on_vector)
+        for i, g in halves[3:]:
+            x_cast(i, g, on_scalar)
+        row_turn(0, 0, bank(1))
+        row_turn(0, 1, bank(6))
+        for i, where in ((1, 7), (2, 5)):
+            warm_up(1)
+            both = bank(where)
+            row_turn(i, 0, both)
+            row_turn(i, 1, both)
         for i in range(2):
-            x_cast(i, 0, "v")
-            x_cast(i, 1, "v")
-        for g in range(2):
-            spread_out(g)
-            x_cast(2 + g, 0, "s")
-            x_cast(2 + g, 1, "s")
-        for i, where in enumerate((6, 7, 5)):
-            head_turn(i, 0, where)
-            head_turn(i, 1, where)
-            keep_warm(1)
-        head_out(0, 0)
-        head_out(0, 1)
-        head_quant(0, 0)
-        head_quant(0, 1)
-        head_out(1, 0)
-        head_out(1, 1)
-        head_quant(1, 0)
-        head_out(2, 0)
-        head_quant(1, 1)
-        nc.scalar.copy(out=bf32[:], in_=braw[:])
-        first = [next_bank() for i in range(EARLY // 2)]
+            row_out(i, 0)
+            row_out(i, 1)
+            x_quant(i, 0)
+            x_quant(i, 1)
+        row_out(2, 0)
+        nc.scalar.copy(out=b_f32[:], in_=b_rows[:])
+        spread_out(0)
+        spread_out(1)
+        start_banks = [next_sum_bank() for i in range(EARLY // 2)]
+
+        def start_sum(T, lo, hi):
+            return start_banks[T // 2][:, (T % 2) * PAIR + lo : (T % 2) * PAIR + hi]
+
         for odd in range(2):
             for g in range(2):
-                for i in range(EARLY // 2):
-                    z_pass(first[i][:, odd * PAIR : odd * PAIR + P], 2 * i + odd, 0, g, 0, P)
-        head_turn(3, 0, 6)
-        head_turn(3, 1, 6)
-        turned = bank(7)
-        nc.tensor.transpose(turned[:, 0:P], bf32[:], ident[:])
-        nc.scalar.copy(out=bias[:], in_=turned[:, 0:24])
+                for T in range(odd, EARLY, 2):
+                    z_pass(start_sum(T, 0, P), T, 0, g, 0, P)
+        both = bank(6)
+        row_turn(3, 0, both)
+        row_turn(3, 1, both)
+        b_turned = bank(7)
+        nc.tensor.transpose(b_turned[:, 0:P], b_f32[:], ident[:])
+        nc.scalar.copy(out=bias[:], in_=b_turned[:, 0 : PIECES * TILES])
         for T in range(EARLY):
             for g in range(2):
-                z_pass(first[T // 2][:, (T % 2) * PAIR + P : (T % 2 + 1) * PAIR], T, 0, g, P, P)
+                z_pass(start_sum(T, P, PAIR), T, 0, g, P, P)
         for T in range(EARLY):
-            u_piece(early[T][:, 0:PAIR], first[T // 2][:, (T % 2) * PAIR : (T % 2 + 1) * PAIR], T, 0)
-        head_out(2, 1)
-        head_quant(2, 0)
-        head_out(3, 0)
-        head_quant(2, 1)
-        head_out(3, 1)
-        head_quant(3, 0)
-        x_prod(4, 0)
-        head_quant(3, 1)
-        x_prod(5, 0)
+            piece_out(early[T][:, 0:PAIR], start_sum(T, 0, PAIR), T, 0)
+        row_out(2, 1)
+        x_quant(2, 0)
+        row_out(3, 0)
+        x_quant(2, 1)
+        row_out(3, 1)
+        x_quant(3, 0)
+        x_product(4, 0)
+        x_quant(3, 1)
+        x_product(5, 0)
 
-        def turn_pair(a):
-            for g in range(2):
-                x_turn(2 * a, g, 6 + g)
-                x_turn(2 * a + 1, g, 6 + g)
+        between, behind, tensor_after, scalar_after = {}, {}, {}, {}
 
-        def y_step(r, n):
-            y_mul(r, n, 6 + n)
+        def place(table, s, job, *args):
+            table.setdefault(s, []).append((job, args))
 
-        on_tensor = {7: [(turn_pair, 2)], 10: [(turn_pair, 3)], 15: [(y_step, 0, 0)], 16: [(y_step, 0, 1)], 17: [(y_step, 1, 0)], 19: [(y_step, 1, 1)], 20: [(y_step, 2, 0)], 21: [(y_step, 2, 1)]}
-        on_scalar = {7: [(x_out, 2, 0), (x_out, 2, 1)], 10: [(x_out, 3, 0), (x_out, 3, 1)], 19: [(h_weave, 3, 0, "s", 0, P)], 20: [(h_weave, 3, 0, "s", P, PAIR)]}
-        before = {
-            1: [(x_prod, 4, 1)], 4: [(x_prod, 5, 1)], 5: [(x_prod, 6, 0)], 6: [(x_prod, 7, 0)], 8: [(x_quant, 2, 0)], 9: [(x_quant, 2, 1)], 10: [(h_quant, 0, 0)], 12: [(h_quant, 1, 0)], 14: [(h_quant, 0, 1)], 16: [(h_quant, 1, 1)],
-            19: [(h_quant, 2, 0)], 21: [(h_quant, 3, 0, 0, P)], 22: [(h_quant, 3, 0, P, PAIR)],
-        }
-        after = {
-            7: [(x_prod, 6, 1)], 8: [(x_prod, 7, 1)],
-            9: [(h_weave, 0, 0, "v")], 10: [(x_quant, 3, 0), (x_quant, 3, 1)], 11: [(h_weave, 1, 0, "v")], 13: [(h_weave, 0, 1, "v")], 14: [(h_weave, 1, 1, "v")],
-            15: [(y_out, 0, 0)], 16: [(y_out, 0, 1)], 17: [(y_out, 1, 0)], 18: [(h_weave, 2, 0, "v")], 19: [(y_out, 1, 1)], 20: [(y_out, 2, 0)], 21: [(y_out, 2, 1)],
-        }
-        for s in range(len(steps)):
-            z_mul(s)
-            for job in on_tensor.get(s, []):
-                job[0](*job[1:])
-            u_out(s, 2 if s in (7, 11, 15, 19, 22, 23) else 3)
-            for job in on_scalar.get(s, []):
-                job[0](*job[1:])
-            if s == len(steps) - 1:
-                break
-            v_max(s)
-            for job in before.get(s, []):
-                job[0](*job[1:])
-            h_max(s)
-            for job in after.get(s, []):
-                job[0](*job[1:])
+        def run(table, s):
+            for job, args in table.get(s, []):
+                job(*args)
 
+        for i, (r, g) in enumerate([(4, 1), (5, 1), (6, 0), (7, 0), (6, 1), (7, 1)]):
+            place(between, 2 + i, x_product, r, g)
+        for a, s in ((2, 7), (3, 10)):
+            place(tensor_after, s, pair_turn, a)
+            place(scalar_after, s, pair_out, a)
+        for g in range(2):
+            place(between, 8 + g, x_quant, 4, g)
+            place(behind, 10, x_quant, 6, g)
+        for s, a, g in ((9, 0, 0), (11, 1, 0), (13, 0, 1), (14, 1, 1), (18, 2, 0)):
+            place(behind, s, h_weave, a, g, 0, PAIR, on_vector)
+            place(between, s + 1, h_quant, a, g, 0, PAIR)
+        for r in range(2):
+            place(scalar_after, 19 + r, h_weave, 3, 0, r * P, (r + 1) * P, on_scalar)
+            place(between, 21 + r, h_quant, 3, 0, r * P, (r + 1) * P)
+        for i, s in enumerate((15, 16, 17, 19, 20, 21)):
+            place(tensor_after, s, y_mul, i // 2, i % 2, SUM_BANKS + i % 2)
+            place(behind, s, y_out, i // 2, i % 2)
+        vector_empties = [s for s in range(7, LAST + 1) if s <= 9 or STEPS[s][2] % GROUP == GROUP - 1 or s >= LAST - 1]
+
+        for s in range(LAST + 1):
+            z_step(s)
+            run(tensor_after, s)
+            pieces_out(s, 2 if s in vector_empties else PIECES)
+            run(scalar_after, s)
+            if s < LAST:
+                first_max(s, 0, STEPS[s][1] * PAIR)
+                run(between, s)
+                second_max(s, 0, STEPS[s][1] * PAIR)
+                run(behind, s)
+
+        row_tiles = ((0, P), (P, PAIR))
         held = [(r, n) for r in (3, 4, 5) for n in range(2)]
-        free = [2, 6, 7, 3, 4, 5, 0, 1]
-        last = [(r, n) for r in (6, 7) for n in range(2)]
-        for lo in (0, P):
-            v_max(s, lo, lo + P)
-        for lo in (0, P):
-            h_max(s, lo, lo + P)
-        y_mul(3, 0, free[0])
-        y_mul(3, 1, free[1])
-        h_weave(2, 1, "s", 0, P)
-        h_weave(2, 1, "s", P, PAIR)
+        final = [(r, n) for r in (6, 7) for n in range(2)]
+        free_banks = [2, 6, 7, 3, 4, 5, 0, 1]
+        for lo, hi in row_tiles:
+            first_max(LAST, lo, hi)
+        for lo, hi in row_tiles:
+            second_max(LAST, lo, hi)
+        for i in range(2):
+            y_mul(*held[i], free_banks[i])
+        for lo, hi in row_tiles:
+            h_weave(2, 1, lo, hi, on_scalar)
         h_quant(2, 1, 0, P)
-        y_out(3, 0)
+        y_out(*held[0])
         h_quant(2, 1, P, PAIR)
-        for i in range(2, 6):
-            y_mul(*held[i], free[i])
-        y_out(3, 1)
-        y_out(4, 0)
-        for i, tile in enumerate(last):
-            y_pass(*tile, 0, free[(6 + i) % 8])
-        y_out(4, 1)
-        y_out(5, 0)
-        h_weave(3, 1, "s", 0, P)
-        h_weave(3, 1, "s", P, PAIR)
+        for i in range(2, len(held)):
+            y_mul(*held[i], free_banks[i])
+        for tile in held[1:3]:
+            y_out(*tile)
+        for i, tile in enumerate(final):
+            y_open(*tile, free_banks[(len(held) + i) % 8])
+        for tile in held[3:5]:
+            y_out(*tile)
+        for lo, hi in row_tiles:
+            h_weave(3, 1, lo, hi, on_scalar)
         h_quant(3, 1, 0, P)
-        y_out(5, 1)
+        y_out(*held[5])
         h_quant(3, 1, P, PAIR)
-        for tile in last:
-            y_pass(*tile, 1, 0)
-        for tile in last:
+        for tile in final:
+            y_pass(*tile, 1)
+        for tile in final:
             y_out(*tile)

@@ -99,20 +99,23 @@ def tile_maxout_then_linear_f7_kernel(tc, x_bytes, x_scale, w_words, w_scales, b
         for i in range(2):
             nc.sync.dma_start(out=x_single[i][:], in_=x_bytes[i * P : (i + 1) * P, :])
         load_pair(1)
-        load_scales(w_sc, w_scales, 0, EARLY * P)
+        load_scales(w_sc, w_scales, 0, F)
         load_w(w_early, 0, 0, EARLY)
         for lo, hi in ((0, 16), (16, 24)):
             nc.sync.dma_start(out=b_rows[lo:hi, :], in_=b.rearrange("j (t p) -> (j t) p", p=P)[lo:hi])
-        load_scales(w_sc, w_scales, EARLY * P, PIECES * F)
+        load_scales(w_sc, w_scales, F, 2 * F + GROUP * P)
         load_w(w_low, slice(1, PIECES), 0, GROUP)
         load_pair(2)
+        load_scales(w_sc, w_scales, 2 * F + GROUP * P, PIECES * F)
         load_w(w_high, slice(1, PIECES), GROUP, TILES)
         load_pair(3)
         load_w(w_rest, 0, EARLY, TILES)
         load_scales(v_sc, v_scales, 0, N)
         for g in range(2):
             nc.sync.dma_start(out=v_w[:, g].bitcast(I32), in_=v_words[g].rearrange("p n t -> p (n t)").bitcast(I32))
-        nc.sync.dma_start(out=c_all[:], in_=c.partition_broadcast(P))
+
+        def load_c():
+            nc.sync.dma_start(out=c_all[:], in_=c.partition_broadcast(P))
 
         x_codes = [keep.tile([P, 2, BANK], U32, name="x_codes%d" % i, align_bytes=256) for i in range(2)]
         x_sc = [keep.tile([P, 2, BANK], U8, name="x_sc%d" % i, align_bytes=256) for i in range(2)]
@@ -377,14 +380,15 @@ def tile_maxout_then_linear_f7_kernel(tc, x_bytes, x_scale, w_words, w_scales, b
                 job(*args)
 
         for i, (r, g) in enumerate([(4, 1), (5, 1), (6, 0), (7, 0), (6, 1), (7, 1)]):
-            place(between, 2 + i, x_product, r, g)
-        for a, s in ((2, 7), (3, 10)):
+            place(between, 3 + i, x_product, r, g)
+        for a, s in ((2, 8), (3, 10)):
             place(tensor_after, s, pair_turn, a)
             place(scalar_after, s, pair_out, a)
         for g in range(2):
-            place(between, 8 + g, x_quant, 4, g)
+            place(between, 9 + g, x_quant, 4, g)
             place(behind, 10, x_quant, 6, g)
-        for s, a, g in ((9, 0, 0), (11, 1, 0), (13, 0, 1), (14, 1, 1), (18, 2, 0)):
+        place(behind, 7, load_c)
+        for s, a, g in ((10, 0, 0), (11, 1, 0), (13, 0, 1), (14, 1, 1), (18, 2, 0)):
             place(behind, s, h_weave, a, g, 0, PAIR, on_vector)
             place(between, s + 1, h_quant, a, g, 0, PAIR)
         for r in range(2):
@@ -395,6 +399,7 @@ def tile_maxout_then_linear_f7_kernel(tc, x_bytes, x_scale, w_words, w_scales, b
             place(behind, s, y_out, i // 2, i % 2)
         vector_empties = [s for s in range(7, LAST + 1) if s <= 9 or STEPS[s][2] % GROUP == GROUP - 1 or s >= LAST - 1]
 
+        lagging = [s for s in range(LAST) if STEPS[s][1] == 1 and s not in between and s not in vector_empties]
         for s in range(LAST + 1):
             z_step(s)
             run(tensor_after, s)
@@ -402,8 +407,11 @@ def tile_maxout_then_linear_f7_kernel(tc, x_bytes, x_scale, w_words, w_scales, b
             run(scalar_after, s)
             if s < LAST:
                 first_max(s, 0, STEPS[s][1] * PAIR)
+                if s - 1 in lagging:
+                    second_max(s - 1, 0, PAIR)
                 run(between, s)
-                second_max(s, 0, STEPS[s][1] * PAIR)
+                if s not in lagging:
+                    second_max(s, 0, STEPS[s][1] * PAIR)
                 run(behind, s)
 
         row_tiles = ((0, P), (P, PAIR))

@@ -122,7 +122,7 @@ def tile_maxout_then_linear_f7_kernel(tc, x_bytes, x_scale, w_words, w_scales, b
         h_codes = [keep.tile([P, 2, PAIR], U32, name="h_codes%d" % i, align_bytes=256) for i in range(4)]
         h_sc = [keep.tile([P, 2, PAIR], U8, name="h_sc%d" % i, align_bytes=256) for i in range(4)]
 
-        wide, turned, grouped, spread = {}, {}, {}, {}
+        wide, turned, grouped, spread, by_parity = {}, {}, {}, {}, {}
 
         def spread_turn(g, where):
             spread[g] = bank(where)
@@ -145,6 +145,11 @@ def tile_maxout_then_linear_f7_kernel(tc, x_bytes, x_scale, w_words, w_scales, b
 
         def x_product(i, g):
             nc.vector.tensor_tensor(out=wide_tile(i, g)[:], in0=x_fp8(i, g), in1=scale_all[:, g], op=ALU.mult)
+
+        def x_sort(i, g):
+            t = stage.tile([P, 2, P], F32, name="sorted", align_bytes=64, bufs=8)
+            nc.vector.tensor_copy(out=t[:], in_=wide[(i, g)][:].bitcast(F32).rearrange("m (p u) -> m u p", u=2))
+            by_parity[(i, g)] = t
 
         def row_turn(i, g, where):
             turned[(i, g)] = where[:, g * PAIR : (g + 1) * PAIR]
@@ -173,10 +178,9 @@ def tile_maxout_then_linear_f7_kernel(tc, x_bytes, x_scale, w_words, w_scales, b
             for g in range(2):
                 turned[(2 * a, g)] = bank(SUM_BANKS + g)
                 for r in range(2):
-                    words = wide[(2 * a + r, g)][:].bitcast(F32)
                     for u in range(2):
                         at = u * PAIR + r * P
-                        nc.tensor.transpose(turned[(2 * a, g)][:, at : at + P], words[:, u:PAIR:2], ident[:])
+                        nc.tensor.transpose(turned[(2 * a, g)][:, at : at + P], by_parity[(2 * a + r, g)][:, u], ident[:])
 
         def pair_out(a):
             for g in range(2):
@@ -242,13 +246,13 @@ def tile_maxout_then_linear_f7_kernel(tc, x_bytes, x_scale, w_words, w_scales, b
                     if pairs == 2:
                         piece_out(u[:, PAIR:BANK], sums[(s, j)], T, j)
                 else:
-                    u = stage.tile([P, pairs * PAIR], BF16, name="piece%d" % j, align_bytes=64)
+                    u = stage.tile([P, pairs * PAIR], BF16, name="piece%d" % j, align_bytes=64, bufs=8)
                     piece_out(u[:], sums[(s, j)], T, j)
                 pieces_of[s].append(u)
 
         def first_max(s, lo, hi):
             if lo == 0:
-                v = stage.tile([P, STEPS[s][1] * PAIR], BF16, name="upper", align_bytes=64)
+                v = stage.tile([P, STEPS[s][1] * PAIR], BF16, name="upper", align_bytes=64, bufs=8)
                 upper[s] = v
             nc.vector.tensor_tensor(out=upper[s][:, lo:hi], in0=pieces_of[s][0][:, lo:hi], in1=pieces_of[s][1][:, lo:hi], op=ALU.max)
 
@@ -379,16 +383,19 @@ def tile_maxout_then_linear_f7_kernel(tc, x_bytes, x_scale, w_words, w_scales, b
             for job, args in table.get(s, []):
                 job(*args)
 
-        for i, (r, g) in enumerate([(4, 1), (5, 1), (6, 0), (7, 0), (6, 1), (7, 1)]):
-            place(between, 3 + i, x_product, r, g)
-        for a, s in ((2, 8), (3, 10)):
+        for r in range(2):
+            place(behind, 0, x_sort, 4 + r, 0)
+        for s, (r, g) in zip((0, 0, 1, 1, 2, 2), [(4, 1), (5, 1), (6, 0), (7, 0), (6, 1), (7, 1)]):
+            place(between, s, x_product, r, g)
+            place(behind, s, x_sort, r, g)
+        for a, s in ((2, 7), (3, 9)):
             place(tensor_after, s, pair_turn, a)
             place(scalar_after, s, pair_out, a)
         for g in range(2):
-            place(between, 9 + g, x_quant, 4, g)
-            place(behind, 10, x_quant, 6, g)
+            place(between, 8 + g, x_quant, 4, g)
+            place(behind, 9, x_quant, 6, g)
         place(behind, 7, load_c)
-        for s, a, g in ((10, 0, 0), (11, 1, 0), (13, 0, 1), (14, 1, 1), (18, 2, 0)):
+        for s, a, g in ((11, 0, 0), (12, 1, 0), (13, 0, 1), (14, 1, 1), (18, 2, 0)):
             place(behind, s, h_weave, a, g, 0, PAIR, on_vector)
             place(between, s + 1, h_quant, a, g, 0, PAIR)
         for r in range(2):
@@ -397,7 +404,7 @@ def tile_maxout_then_linear_f7_kernel(tc, x_bytes, x_scale, w_words, w_scales, b
         for i, s in enumerate((15, 16, 17, 19, 20, 21)):
             place(tensor_after, s, y_mul, i // 2, i % 2, SUM_BANKS + i % 2)
             place(behind, s, y_out, i // 2, i % 2)
-        vector_empties = [s for s in range(7, LAST + 1) if s <= 9 or STEPS[s][2] % GROUP == GROUP - 1 or s >= LAST - 1]
+        vector_empties = (8, 9, 10, 11, 15, 19, 22, 23)
 
         lagging = [s for s in range(LAST) if STEPS[s][1] == 1 and s not in between and s not in vector_empties]
         for s in range(LAST + 1):

@@ -113,16 +113,14 @@ def tile_maxout_then_linear_f7_kernel(tc, x_bytes, x_scale, w_words, w_scales, b
         load_scales(v_sc, v_scales, 0, N)
         for g in range(2):
             nc.sync.dma_start(out=v_w[:, g].bitcast(I32), in_=v_words[g].rearrange("p n t -> p (n t)").bitcast(I32))
-
-        def load_c():
-            nc.sync.dma_start(out=c_all[:], in_=c.partition_broadcast(P))
+        nc.sync.dma_start(out=c_all[:], in_=c.partition_broadcast(P))
 
         x_codes = [keep.tile([P, 2, BANK], U32, name="x_codes%d" % i, align_bytes=256) for i in range(2)]
         x_sc = [keep.tile([P, 2, BANK], U8, name="x_sc%d" % i, align_bytes=256) for i in range(2)]
         h_codes = [keep.tile([P, 2, PAIR], U32, name="h_codes%d" % i, align_bytes=256) for i in range(4)]
         h_sc = [keep.tile([P, 2, PAIR], U8, name="h_sc%d" % i, align_bytes=256) for i in range(4)]
 
-        wide, turned, grouped, spread, by_parity = {}, {}, {}, {}, {}
+        wide, turned, grouped, spread, scaled, by_parity = {}, {}, {}, {}, {}, {}
 
         def spread_turn(g, where):
             spread[g] = bank(where)
@@ -132,24 +130,20 @@ def tile_maxout_then_linear_f7_kernel(tc, x_bytes, x_scale, w_words, w_scales, b
         def spread_out(g):
             nc.scalar.copy(out=scale_all[:, g].rearrange("m (p t) -> m p t", t=4), in_=spread[g][:].rearrange("m (t p) -> m p t", t=4))
 
-        def x_fp8(i, g):
-            return x_rows[i][:, g * PASS : (g + 1) * PASS].bitcast(E4M3)
-
-        def wide_tile(i, g):
+        def x_cast(i, g, copy):
             w = stage.tile([P, PASS], BF16, name="wide", align_bytes=64, bufs=8)
             wide[(i, g)] = w
-            return w
+            copy(out=w[:], in_=x_rows[i][:, g * PASS : (g + 1) * PASS].bitcast(E4M3))
 
-        def x_cast(i, g, copy):
-            copy(out=wide_tile(i, g)[:], in_=x_fp8(i, g))
+        def x_product(i):
+            t = stage.tile([P, K], BF16, name="scaled", align_bytes=64)
+            scaled[i] = t
+            nc.vector.tensor_tensor(out=t[:], in0=x_rows[i].bitcast(E4M3), in1=scale_all[:].rearrange("m g k -> m (g k)"), op=ALU.mult)
 
-        def x_product(i, g):
-            nc.vector.tensor_tensor(out=wide_tile(i, g)[:], in0=x_fp8(i, g), in1=scale_all[:, g], op=ALU.mult)
-
-        def x_sort(i, g):
-            t = stage.tile([P, 2, P], F32, name="sorted", align_bytes=64, bufs=8)
-            nc.vector.tensor_copy(out=t[:], in_=wide[(i, g)][:].bitcast(F32).rearrange("m (p u) -> m u p", u=2))
-            by_parity[(i, g)] = t
+        def x_sort(i):
+            t = stage.tile([P, 2, 2, P], F32, name="by_parity", align_bytes=64)
+            by_parity[i] = t
+            nc.vector.tensor_copy(out=t[:], in_=scaled[i][:].bitcast(F32).rearrange("m (g p u) -> m g u p", g=2, u=2))
 
         def row_turn(i, g, where):
             turned[(i, g)] = where[:, g * PAIR : (g + 1) * PAIR]
@@ -180,16 +174,21 @@ def tile_maxout_then_linear_f7_kernel(tc, x_bytes, x_scale, w_words, w_scales, b
                 for r in range(2):
                     for u in range(2):
                         at = u * PAIR + r * P
-                        nc.tensor.transpose(turned[(2 * a, g)][:, at : at + P], by_parity[(2 * a + r, g)][:, u], ident[:])
+                        nc.tensor.transpose(turned[(2 * a, g)][:, at : at + P], by_parity[2 * a + r][:, g, u], ident[:])
 
-        def pair_out(a):
-            for g in range(2):
-                t = stage.tile([P, PAIR, 4], BF16, name="grouped", align_bytes=64)
-                grouped[(2 * a, g)] = t
-                nc.scalar.copy(out=t[:].bitcast(F32), in_=turned[(2 * a, g)][:].rearrange("p (u m) -> p m u", u=2))
+        def pair_out(a, g, copy):
+            t = stage.tile([P, PAIR, 4], BF16, name="grouped", align_bytes=64)
+            grouped[(2 * a, g)] = t
+            copy(out=t[:].bitcast(F32), in_=turned[(2 * a, g)][:].rearrange("p (u m) -> p m u", u=2))
 
         sums, pieces_of, upper, folded, folds, woven = {}, {}, {}, {}, {}, {}
-        early = [keep.tile([P, PAIR if T < GROUP else BANK], BF16, name="early%d" % T, align_bytes=64) for T in range(EARLY)]
+        first_half = {}
+
+        def half_piece(T, j):
+            if (T, j) not in first_half:
+                t = keep.tile([P, BANK], BF16, name="half%d_%d" % (T, j), align_bytes=64)
+                first_half[(T, j)] = t
+            return first_half[(T, j)]
 
         def w_tile(T, j, g):
             if j > 0:
@@ -241,23 +240,30 @@ def tile_maxout_then_linear_f7_kernel(tc, x_bytes, x_scale, w_words, w_scales, b
             a, pairs, T = STEPS[s]
             pieces_of[s] = []
             for j in range(count):
-                if j == 0 and a == 0 and T < EARLY:
-                    u = early[T]
-                    if pairs == 2:
-                        piece_out(u[:, PAIR:BANK], sums[(s, j)], T, j)
+                if a < 2 and (pairs == 1 or (j == 0 and T < EARLY)):
+                    u = half_piece(T, j)
+                    if (s, j) in sums:
+                        second = a == 1 or pairs == 2
+                        piece_out(u[:, PAIR:BANK] if second else u[:, 0:PAIR], sums[(s, j)], T, j)
                 else:
-                    u = stage.tile([P, pairs * PAIR], BF16, name="piece%d" % j, align_bytes=64, bufs=8)
+                    u = stage.tile([P, pairs * PAIR], BF16, name="piece%d" % j, align_bytes=64)
                     piece_out(u[:], sums[(s, j)], T, j)
                 pieces_of[s].append(u)
 
+        def max_width(s):
+            a, pairs, T = STEPS[s]
+            return 0 if (a, pairs) == (0, 1) else (BANK if a < 2 else pairs * PAIR)
+
         def first_max(s, lo, hi):
             if lo == 0:
-                v = stage.tile([P, STEPS[s][1] * PAIR], BF16, name="upper", align_bytes=64, bufs=8)
+                v = stage.tile([P, max_width(s)], BF16, name="upper", align_bytes=64)
                 upper[s] = v
             nc.vector.tensor_tensor(out=upper[s][:, lo:hi], in0=pieces_of[s][0][:, lo:hi], in1=pieces_of[s][1][:, lo:hi], op=ALU.max)
 
         def second_max(s, lo, hi):
             a, pairs, T = STEPS[s]
+            if a == 1:
+                a, pairs = 0, 2
             h = stage.tile([P, hi - lo], BF16, name="h", align_bytes=64, bufs=8)
             if len(pieces_of[s]) == PIECES:
                 nc.vector.tensor_tensor(out=h[:], in0=pieces_of[s][2][:, lo:hi], in1=upper[s][:, lo:hi], op=ALU.max)
@@ -363,18 +369,17 @@ def tile_maxout_then_linear_f7_kernel(tc, x_bytes, x_scale, w_words, w_scales, b
             for g in range(2):
                 z_pass(start_sum(T, P, PAIR), T, 0, g, P, P)
         for T in range(EARLY):
-            piece_out(early[T][:, 0:PAIR], start_sum(T, 0, PAIR), T, 0)
-        row_out(2, 1)
-        x_quant(2, 0)
-        row_out(3, 0)
-        x_quant(2, 1)
-        row_out(3, 1)
-        x_quant(3, 0)
-        x_product(4, 0)
-        x_quant(3, 1)
-        x_product(5, 0)
+            piece_out(half_piece(T, 0)[:, 0:PAIR], start_sum(T, 0, PAIR), T, 0)
+        for fed, (i, g) in zip(halves[4:7], halves[5:]):
+            row_out(i, g)
+            x_quant(*fed)
+        x_quant(*halves[7])
+        for a in (2, 3):
+            for job in (x_product, x_sort):
+                job(2 * a)
+                job(2 * a + 1)
 
-        between, behind, tensor_after, scalar_after = {}, {}, {}, {}
+        ahead, between, behind, tensor_after, scalar_after = {}, {}, {}, {}, {}
 
         def place(table, s, job, *args):
             table.setdefault(s, []).append((job, args))
@@ -383,18 +388,14 @@ def tile_maxout_then_linear_f7_kernel(tc, x_bytes, x_scale, w_words, w_scales, b
             for job, args in table.get(s, []):
                 job(*args)
 
-        for r in range(2):
-            place(behind, 0, x_sort, 4 + r, 0)
-        for s, (r, g) in zip((0, 0, 1, 1, 2, 2), [(4, 1), (5, 1), (6, 0), (7, 0), (6, 1), (7, 1)]):
-            place(between, s, x_product, r, g)
-            place(behind, s, x_sort, r, g)
         for a, s in ((2, 7), (3, 9)):
             place(tensor_after, s, pair_turn, a)
-            place(scalar_after, s, pair_out, a)
+            place(scalar_after, s, pair_out, a, 0, on_scalar)
+        place(ahead, 7, pair_out, 2, 1, on_vector)
+        place(scalar_after, 9, pair_out, 3, 1, on_scalar)
         for g in range(2):
             place(between, 8 + g, x_quant, 4, g)
             place(behind, 9, x_quant, 6, g)
-        place(behind, 7, load_c)
         for s, a, g in ((11, 0, 0), (12, 1, 0), (13, 0, 1), (14, 1, 1), (18, 2, 0)):
             place(behind, s, h_weave, a, g, 0, PAIR, on_vector)
             place(between, s + 1, h_quant, a, g, 0, PAIR)
@@ -404,22 +405,29 @@ def tile_maxout_then_linear_f7_kernel(tc, x_bytes, x_scale, w_words, w_scales, b
         for i, s in enumerate((15, 16, 17, 19, 20, 21)):
             place(tensor_after, s, y_mul, i // 2, i % 2, SUM_BANKS + i % 2)
             place(behind, s, y_out, i // 2, i % 2)
-        vector_empties = (8, 9, 10, 11, 15, 19, 22, 23)
+        vector_empties = [s for s in range(9, LAST + 1) if s <= 10 or STEPS[s][2] % GROUP == GROUP - 1 or s >= LAST - 1]
 
-        lagging = [s for s in range(LAST) if STEPS[s][1] == 1 and s not in between and s not in vector_empties]
+        lagging = [s for s in range(LAST) if STEPS[s][1] == 1 and max_width(s) and s not in between and s not in vector_empties]
+
+        def vector_steps(s):
+            if s < 7 or s == LAST:
+                return []
+            return range(4, 8) if s == 7 else [s]
+
         for s in range(LAST + 1):
             z_step(s)
             run(tensor_after, s)
             pieces_out(s, 2 if s in vector_empties else PIECES)
             run(scalar_after, s)
-            if s < LAST:
-                first_max(s, 0, STEPS[s][1] * PAIR)
-                if s - 1 in lagging:
-                    second_max(s - 1, 0, PAIR)
-                run(between, s)
-                if s not in lagging:
-                    second_max(s, 0, STEPS[s][1] * PAIR)
-                run(behind, s)
+            run(ahead, s)
+            for r in vector_steps(s):
+                first_max(r, 0, max_width(r))
+                if r - 1 in lagging:
+                    second_max(r - 1, 0, max_width(r - 1))
+                run(between, r)
+                if r not in lagging:
+                    second_max(r, 0, max_width(r))
+                run(behind, r)
 
         row_tiles = ((0, P), (P, PAIR))
         held = [(r, n) for r in (3, 4, 5) for n in range(2)]

@@ -34,6 +34,9 @@ STEPS = (
     + [(a, 1, T) for a in (2, 3) for T in range(GROUP, TILES)]
 )
 LAST = len(STEPS) - 1
+TURN_AFTER = {2: 7, 3: 9}
+FOLD_STEPS = {2: 2, 1: 3}
+HELD = 6
 
 
 def tile_maxout_then_linear_f7_kernel(tc, x_bytes, x_scale, w_words, w_scales, b, v_words, v_scales, c, out):
@@ -312,11 +315,11 @@ def tile_maxout_then_linear_f7_kernel(tc, x_bytes, x_scale, w_words, w_scales, b
             y_open(r, n, where)
             y_pass(r, n, 1)
 
-        def y_out(r, n):
+        def y_out(r, n, queue=nc.sync):
             o = stage.tile([P, BANK], F32, name="y", bufs=8)
             cols = slice(n * BANK, (n + 1) * BANK)
             nc.vector.tensor_tensor(out=o[:], in0=y_sums[(r, n)][:], in1=c_all[:, cols], op=ALU.add)
-            nc.sync.dma_start(out=out[r * P : (r + 1) * P, cols], in_=o[:])
+            queue.dma_start(out=out[r * P : (r + 1) * P, cols], in_=o[:])
 
         idle_bank = bank(0)
 
@@ -388,31 +391,44 @@ def tile_maxout_then_linear_f7_kernel(tc, x_bytes, x_scale, w_words, w_scales, b
             for job, args in table.get(s, []):
                 job(*args)
 
-        for a, s in ((2, 7), (3, 9)):
+        def fold_arrives(a, g):
+            done = max(s for s, (first, pairs, T) in enumerate(STEPS) if first <= a < first + pairs and T // GROUP == g)
+            return done + FOLD_STEPS[STEPS[done + 1][1]]
+
+        turn_2, turn_3 = TURN_AFTER[2], TURN_AFTER[3]
+        for a, s in TURN_AFTER.items():
             place(tensor_after, s, pair_turn, a)
             place(scalar_after, s, pair_out, a, 0, on_scalar)
-        place(ahead, 7, pair_out, 2, 1, on_vector)
-        place(scalar_after, 9, pair_out, 3, 1, on_scalar)
+        place(ahead, turn_2, pair_out, 2, 1, on_vector)
+        place(scalar_after, turn_3, pair_out, 3, 1, on_scalar)
         for g in range(2):
-            place(between, 8 + g, x_quant, 4, g)
-            place(behind, 9, x_quant, 6, g)
-        for s, a, g in ((11, 0, 0), (12, 1, 0), (13, 0, 1), (14, 1, 1), (18, 2, 0)):
+            place(between, turn_2 + 1 + g, x_quant, 4, g)
+            place(behind, turn_3, x_quant, 6, g)
+        vector_empties = [
+            s for s in range(turn_3, LAST + 1) if s <= turn_3 + 1 or STEPS[s][2] % GROUP == GROUP - 1 or s >= LAST - 1
+        ]
+        s = turn_3 + 1
+        for a, g in ((0, 0), (1, 0), (0, 1), (1, 1), (2, 0)):
+            s = max(s + 1, fold_arrives(a, g))
             place(behind, s, h_weave, a, g, 0, PAIR, on_vector)
             place(between, s + 1, h_quant, a, g, 0, PAIR)
         for r in range(2):
-            place(scalar_after, 19 + r, h_weave, 3, 0, r * P, (r + 1) * P, on_scalar)
-            place(between, 21 + r, h_quant, 3, 0, r * P, (r + 1) * P)
-        for i, s in enumerate((15, 16, 17, 19, 20, 21)):
-            place(tensor_after, s, y_mul, i // 2, i % 2, SUM_BANKS + i % 2)
-            place(behind, s, y_out, i // 2, i % 2)
-        vector_empties = [s for s in range(9, LAST + 1) if s <= 10 or STEPS[s][2] % GROUP == GROUP - 1 or s >= LAST - 1]
+            place(scalar_after, s + 1 + r, h_weave, 3, 0, r * P, (r + 1) * P, on_scalar)
+            place(between, s + 3 + r, h_quant, 3, 0, r * P, (r + 1) * P)
+        tiles = [(r, n) for r in range(M // P) for n in range(2)]
+        final = tiles[-4:]
+        held = tiles[-4 - HELD : -4]
+        free_steps = [s for s in range(fold_arrives(0, 1) + 1, LAST) if s not in behind]
+        for s, (r, n) in zip(free_steps, tiles[: -4 - HELD]):
+            place(tensor_after, s, y_mul, r, n, SUM_BANKS + n)
+            place(behind, s, y_out, r, n)
 
         lagging = [s for s in range(LAST) if STEPS[s][1] == 1 and max_width(s) and s not in between and s not in vector_empties]
 
         def vector_steps(s):
-            if s < 7 or s == LAST:
+            if s < turn_2 or s == LAST:
                 return []
-            return range(4, 8) if s == 7 else [s]
+            return range(GROUP, s + 1) if s == turn_2 else [s]
 
         for s in range(LAST + 1):
             z_step(s)
@@ -430,8 +446,6 @@ def tile_maxout_then_linear_f7_kernel(tc, x_bytes, x_scale, w_words, w_scales, b
                 run(behind, r)
 
         row_tiles = ((0, P), (P, PAIR))
-        held = [(r, n) for r in (3, 4, 5) for n in range(2)]
-        final = [(r, n) for r in (6, 7) for n in range(2)]
         free_banks = [2, 6, 7, 3, 4, 5, 0, 1]
         for lo, hi in row_tiles:
             first_max(LAST, lo, hi)
@@ -455,9 +469,9 @@ def tile_maxout_then_linear_f7_kernel(tc, x_bytes, x_scale, w_words, w_scales, b
         for lo, hi in row_tiles:
             h_weave(3, 1, lo, hi, on_scalar)
         h_quant(3, 1, 0, P)
-        y_out(*held[5])
+        y_out(*held[5], nc.scalar)
         h_quant(3, 1, P, PAIR)
         for tile in final:
             y_pass(*tile, 1)
-        for tile in final:
-            y_out(*tile)
+        for r, n in final:
+            y_out(r, n, (nc.sync, nc.scalar)[n])

@@ -152,15 +152,15 @@ def tile_maxout_then_linear_f7_kernel(tc, x_bytes, x_scale, w_words, w_scales, b
             turned[(i, g)] = where[:, g * PAIR : (g + 1) * PAIR]
             words = wide[(i, g)][:].bitcast(F32)
             for u in range(2):
-                nc.tensor.transpose(where[:, g * PAIR + u : (g + 1) * PAIR : 2], words[:, u:PAIR:2], ident[:])
+                nc.tensor.transpose(where[:, g * PAIR + u * P : g * PAIR + (u + 1) * P], words[:, u:PAIR:2], ident[:])
 
         def row_out(i, g):
             t = stage.tile([P, P, 4], BF16, name="grouped", align_bytes=64)
             grouped[(i, g)] = t
             nc.vector.tensor_tensor(
-                out=t[:],
-                in0=turned[(i, g)].bitcast(BF16).rearrange("p (m t) -> p m t", t=4),
-                in1=scale_cols[:, g].unsqueeze(1).to_broadcast([P, P, 4]),
+                out=t[:].rearrange("p m (u e) -> p m u e", u=2),
+                in0=turned[(i, g)].bitcast(BF16).rearrange("p (u m e) -> p m u e", u=2, e=2),
+                in1=scale_cols[:, g].rearrange("p (u e) -> p u e", u=2).unsqueeze(1).to_broadcast([P, P, 2, 2]),
                 op=ALU.mult,
             )
 

@@ -23,20 +23,10 @@ BANK = 512
 PAIR = 2 * P
 TILES = F // P
 GROUP = 4
-W_TILE = 2 * P
 SUM_BANKS = 6
-EARLY = 6
-
-STEPS = (
-    [(a, 1, T) for a in (0, 1) for T in range(GROUP)]
-    + [(0, 2, T) for T in range(GROUP, TILES)]
-    + [(2, 2, T) for T in range(GROUP)]
-    + [(a, 1, T) for a in (2, 3) for T in range(GROUP, TILES)]
-)
-LAST = len(STEPS) - 1
-TURN_AFTER = {2: 7, 3: 9}
-FOLD_STEPS = {2: 2, 1: 3}
-HELD = 6
+EARLY = 10
+FIRST = 4
+LATE = 20
 
 
 def tile_maxout_then_linear_f7_kernel(tc, x_bytes, x_scale, w_words, w_scales, b, v_words, v_scales, c, out):
@@ -51,68 +41,68 @@ def tile_maxout_then_linear_f7_kernel(tc, x_bytes, x_scale, w_words, w_scales, b
             t = psum.tile([P, BANK], F32, name="bank%d" % i)
             return t
 
-        taken = []
-
-        def next_sum_bank():
-            taken.append(bank(len(taken) % SUM_BANKS))
-            return taken[-1]
-
+        parts = ((0, EARLY), (EARLY, LATE), (LATE, PIECES * TILES))
         scale_cols = keep.tile([P, 2, 4], F32, name="scale_cols")
-        w_sc = keep.tile([P, 2, PIECES * F], U8, name="w_sc", align_bytes=256)
+        w_w = [keep.tile([P, 2, (hi - lo) * 2 * P], U8, name="w_w%d" % lo, align_bytes=256) for lo, hi in parts]
+        w_sc = [keep.tile([P, 2, (hi - lo) * P], U8, name="w_sc%d" % lo, align_bytes=256) for lo, hi in parts]
+        v_w = keep.tile([P, 2, 4 * N], U8, name="v_w", align_bytes=256)
         v_sc = keep.tile([P, 2, N], U8, name="v_sc", align_bytes=256)
         ident = keep.tile([P, P], F32, name="ident")
-        b_rows = keep.tile([P, P], BF16, name="b_rows")
-        x_single = [keep.tile([P, K], U8, name="x_single%d" % i, align_bytes=64) for i in range(2)]
-        x_pair = [keep.tile([P, 2, K], U8, name="x_pair%d" % i, align_bytes=64) for i in range(3)]
-        x_rows = x_single + [x_pair[i // 2][:, i % 2] for i in range(6)]
-        w_early = keep.tile([P, 2, EARLY * W_TILE], U8, name="w_early", align_bytes=256)
-        w_low = keep.tile([P, 2, 2, GROUP * W_TILE], U8, name="w_low", align_bytes=256)
-        w_rest = keep.tile([P, 2, (TILES - EARLY) * W_TILE], U8, name="w_rest", align_bytes=256)
-        w_high = keep.tile([P, 2, 2, GROUP * W_TILE], U8, name="w_high", align_bytes=256)
-        v_w = keep.tile([P, 2, 4 * N], U8, name="v_w", align_bytes=256)
-        c_all = keep.tile([P, N], BF16, name="c_all")
-        scale_all = keep.tile([P, 2, PASS], F32, name="scale_all", align_bytes=64)
+        pick = keep.tile([P, TILES], BF16, name="pick")
+        one = keep.tile([P, 1], F32, name="one")
+        b_rows = keep.tile([P, PIECES, P], BF16, name="b_rows")
         bias = keep.tile([P, PIECES * TILES], F32, name="bias")
-        b_f32 = keep.tile([P, P], F32, name="b_f32")
+        x_start = [keep.tile([P, PASS], U8, name="x_start%d" % i, align_bytes=64) for i in range(2)]
+        x_next = keep.tile([P, 2, PASS], U8, name="x_next", align_bytes=64)
+        x_pair = [keep.tile([P, 2, K], U8, name="x_pair%d" % a, align_bytes=64) for a in range(1, 4)]
+        c_all = keep.tile([P, N], BF16, name="c_all")
         zeros = keep.tile([P, BANK], BF16, name="zeros")
 
         nc.scalar.dma_start(out=scale_cols[:], in_=x_scale.rearrange("o (g p t) -> p (o g) t", g=2, t=4))
+        nc.vector.memset(b_rows[:], 0.0)
         nc.vector.memset(zeros[:], 0.0)
-        nc.vector.memset(w_sc[:].rearrange("p g n -> p (g n)").bitcast(U32), 0)
+        for tile in (w_sc[0], w_sc[1], w_sc[2], v_sc):
+            nc.vector.memset(tile[:].rearrange("p g n -> p (g n)").bitcast(U32), 0)
+        nc.vector.memset(one[:], 1.0)
         make_identity(nc, ident[:])
-        nc.scalar.activation(out=b_rows[:], in_=ident[:], func=ACT.Identity, scale=0.0)
-        nc.gpsimd.memset(v_sc[:].rearrange("p g n -> p (g n)").bitcast(U32), 0)
 
         def load_pair(a):
             nc.sync.dma_start(out=x_pair[a - 1][:], in_=x_bytes[a * PAIR : (a + 1) * PAIR, :].rearrange("(r p) k -> p r k", p=P))
 
-        def load_w(tile, pieces, lo, hi):
-            for g in range(2):
-                nc.sync.dma_start(
-                    out=tile[:, g].bitcast(I32),
-                    in_=w_words[g].rearrange("p (j n) -> p j n", j=PIECES)[:, pieces, lo * W_TILE : hi * W_TILE].bitcast(I32),
-                )
+        def load_w(part, g, lo=None, hi=None):
+            base = parts[part][0]
+            if lo is None:
+                lo, hi = parts[part]
+            nc.sync.dma_start(
+                out=w_w[part][:, g, (lo - base) * 2 * P : (hi - base) * 2 * P].bitcast(I32),
+                in_=w_words[g][:, lo * 2 * P : hi * 2 * P].bitcast(I32),
+            )
 
         def load_scales(tile, scales, lo, hi):
             for i in range(4):
-                nc.sync.dma_start(
-                    out=tile[i:P:32, :, lo:hi].bitcast(I32), in_=scales[:, i:16:4, lo:hi].rearrange("g q n -> q g n").bitcast(I32)
-                )
+                nc.sync.dma_start(out=tile[i:P:32].bitcast(I32), in_=scales[:, i:16:4, lo:hi].rearrange("g q n -> q g n").bitcast(I32))
+
+        def load_w_scales(part):
+            load_scales(w_sc[part], w_scales, parts[part][0] * P, parts[part][1] * P)
 
         for i in range(2):
-            nc.sync.dma_start(out=x_single[i][:], in_=x_bytes[i * P : (i + 1) * P, :])
+            nc.sync.dma_start(out=x_start[i][:], in_=x_bytes[i * P : (i + 1) * P, 0:PASS])
+        nc.sync.dma_start(out=x_next[:], in_=x_bytes[0:PAIR, PASS:K].rearrange("(r p) k -> p r k", p=P))
         load_pair(1)
-        load_scales(w_sc, w_scales, 0, F)
-        load_w(w_early, 0, 0, EARLY)
-        for lo, hi in ((0, 16), (16, 24)):
-            nc.sync.dma_start(out=b_rows[lo:hi, :], in_=b.rearrange("j (t p) -> (j t) p", p=P)[lo:hi])
-        load_scales(w_sc, w_scales, F, 2 * F + GROUP * P)
-        load_w(w_low, slice(1, PIECES), 0, GROUP)
+        nc.scalar.dma_start(out=b_rows[0:TILES], in_=b.rearrange("j (t p) -> t j p", p=P))
+        nc.scalar.activation(out=pick[:], in_=ident[:, 0:TILES], func=ACT.Identity)
+        load_w_scales(0)
+        load_w(0, 0, 0, FIRST)
+        load_w(0, 0, FIRST, EARLY)
+        load_w(0, 1)
         load_pair(2)
-        load_scales(w_sc, w_scales, 2 * F + GROUP * P, PIECES * F)
-        load_w(w_high, slice(1, PIECES), GROUP, TILES)
+        load_w_scales(1)
+        load_w(1, 0)
+        load_w(1, 1)
         load_pair(3)
-        load_w(w_rest, 0, EARLY, TILES)
+        load_w_scales(2)
+        load_w(2, 0)
+        load_w(2, 1)
         load_scales(v_sc, v_scales, 0, N)
         for g in range(2):
             nc.sync.dma_start(out=v_w[:, g].bitcast(I32), in_=v_words[g].rearrange("p n t -> p (n t)").bitcast(I32))
@@ -123,44 +113,55 @@ def tile_maxout_then_linear_f7_kernel(tc, x_bytes, x_scale, w_words, w_scales, b
         h_codes = [keep.tile([P, 2, PAIR], U32, name="h_codes%d" % i, align_bytes=256) for i in range(4)]
         h_sc = [keep.tile([P, 2, PAIR], U8, name="h_sc%d" % i, align_bytes=256) for i in range(4)]
 
-        wide, turned, grouped, spread, scaled, by_parity = {}, {}, {}, {}, {}, {}
+        plain, words, turned, grouped = {}, {}, {}, {}
 
-        def spread_turn(g, where):
-            spread[g] = bank(where)
-            for t in range(4):
-                nc.tensor.transpose(spread[g][:, t * P : (t + 1) * P], scale_cols[:, g, t : t + 1].to_broadcast([P, P]), ident[:])
+        def x_row(i, passes):
+            if i >= 2:
+                return x_pair[i // 2 - 1][:, i % 2, passes[0] * PASS : (passes[-1] + 1) * PASS].bitcast(E4M3)
+            return (x_start[i][:] if passes[0] == 0 else x_next[:, i]).bitcast(E4M3)
 
-        def spread_out(g):
-            nc.scalar.copy(out=scale_all[:, g].rearrange("m (p t) -> m p t", t=4), in_=spread[g][:].rearrange("m (t p) -> m p t", t=4))
-
-        def x_cast(i, g, copy):
-            w = stage.tile([P, PASS], BF16, name="wide", align_bytes=64, bufs=8)
-            wide[(i, g)] = w
-            copy(out=w[:], in_=x_rows[i][:, g * PASS : (g + 1) * PASS].bitcast(E4M3))
-
-        def x_product(i):
-            t = stage.tile([P, K], BF16, name="scaled", align_bytes=64)
-            scaled[i] = t
-            nc.vector.tensor_tensor(out=t[:], in0=x_rows[i].bitcast(E4M3), in1=scale_all[:].rearrange("m g k -> m (g k)"), op=ALU.mult)
-
-        def x_sort(i):
-            t = stage.tile([P, 2, 2, P], F32, name="by_parity", align_bytes=64)
-            by_parity[i] = t
-            nc.vector.tensor_copy(out=t[:], in_=scaled[i][:].bitcast(F32).rearrange("m (g p u) -> m g u p", g=2, u=2))
-
-        def row_turn(i, g, where):
-            turned[(i, g)] = where[:, g * PAIR : (g + 1) * PAIR]
-            words = wide[(i, g)][:].bitcast(F32)
+        def x_cast(i, g):
+            t = stage.tile([P, PASS], BF16, name="plain", align_bytes=64, bufs=5)
+            plain[(i, g)] = t
+            nc.scalar.copy(out=t[:], in_=x_row(i, [g]))
             for u in range(2):
-                nc.tensor.transpose(where[:, g * PAIR + u * P : g * PAIR + (u + 1) * P], words[:, u:PAIR:2], ident[:])
+                words[(i, g, u)] = t[:].bitcast(F32)[:, u:PAIR:2]
 
-        def row_out(i, g):
-            t = stage.tile([P, P, 4], BF16, name="grouped", align_bytes=64)
+        def x_resort(i, g):
+            t = stage.tile([P, 2, P], F32, name="resorted", align_bytes=64)
+            nc.scalar.copy(out=t[:], in_=plain[(i, g)][:].bitcast(F32).rearrange("m (w u) -> m u w", u=2))
+            for u in range(2):
+                words[(i, g, u)] = t[:, u]
+
+        def x_sort(i, passes):
+            t = stage.tile([P, 2, len(passes) * P, 2], BF16, name="sorted", align_bytes=64)
+            nc.vector.tensor_scalar(
+                out=t[:].rearrange("m u w e -> m w u e"),
+                in0=x_row(i, passes).rearrange("m (w u e) -> m w u e", u=2, e=2),
+                scalar1=one[:],
+                scalar2=None,
+                op0=ALU.mult,
+            )
+            for n, g in enumerate(passes):
+                for u in range(2):
+                    words[(i, g, u)] = t[:].rearrange("m u w e -> m u (w e)").bitcast(F32)[:, u, n * P : (n + 1) * P]
+
+        def x_turn(rows, g, where):
+            t = bank(where)
+            for i in rows:
+                turned[(i, g)] = t
+                for u in range(2):
+                    at = u * PAIR + (i % 2) * P
+                    nc.tensor.transpose(t[:, at : at + P], words[(i, g, u)], ident[:])
+
+        def x_out(i, rows, g):
+            t = stage.tile([P, rows * P, 4], BF16, name="grouped", align_bytes=64)
             grouped[(i, g)] = t
+            lo = (i % 2) * P
             nc.vector.tensor_tensor(
                 out=t[:].rearrange("p m (u e) -> p m u e", u=2),
-                in0=turned[(i, g)].bitcast(BF16).rearrange("p (u m e) -> p m u e", u=2, e=2),
-                in1=scale_cols[:, g].rearrange("p (u e) -> p u e", u=2).unsqueeze(1).to_broadcast([P, P, 2, 2]),
+                in0=turned[(i, g)][:].bitcast(BF16).rearrange("p (u m e) -> p m u e", u=2, e=2)[:, lo : lo + rows * P],
+                in1=scale_cols[:, g].rearrange("p (u e) -> p u e", u=2).unsqueeze(1).to_broadcast([P, rows * P, 2, 2]),
                 op=ALU.mult,
             )
 
@@ -171,129 +172,96 @@ def tile_maxout_then_linear_f7_kernel(tc, x_bytes, x_scale, w_words, w_scales, b
                 out=x_codes[i // 4][:, g, cols].bitcast(FP8X4), scales=x_sc[i // 4][:, g, cols], in_=t[:].rearrange("p m t -> p (m t)")
             )
 
-        def pair_turn(a):
-            for g in range(2):
-                turned[(2 * a, g)] = bank(SUM_BANKS + g)
-                for r in range(2):
-                    for u in range(2):
-                        at = u * PAIR + r * P
-                        nc.tensor.transpose(turned[(2 * a, g)][:, at : at + P], by_parity[2 * a + r][:, g, u], ident[:])
+        sums, pieces, upper, folds, woven = {}, {}, {}, {}, {}
 
-        def pair_out(a, g, copy):
-            t = stage.tile([P, PAIR, 4], BF16, name="grouped", align_bytes=64)
-            grouped[(2 * a, g)] = t
-            copy(out=t[:].bitcast(F32), in_=turned[(2 * a, g)][:].rearrange("p (u m) -> p m u", u=2))
-
-        sums, pieces_of, upper, folded, folds, woven = {}, {}, {}, {}, {}, {}
-        first_half = {}
-
-        def half_piece(T, j):
-            if (T, j) not in first_half:
-                t = keep.tile([P, BANK], BF16, name="half%d_%d" % (T, j), align_bytes=64)
-                first_half[(T, j)] = t
-            return first_half[(T, j)]
-
-        def w_tile(T, j, g):
-            if j > 0:
-                tile, at = (w_low if T < GROUP else w_high)[:, g, j - 1], T % GROUP
-            elif T < EARLY:
-                tile, at = w_early[:, g], T
-            else:
-                tile, at = w_rest[:, g], T - EARLY
-            return tile[:, at * W_TILE : (at + 1) * W_TILE]
-
-        def z_pass(dst, T, j, g, first, n):
-            half, at = first // BANK, first % BANK
+        def z_pass(dst, j, T, first, n, g, start, stop):
+            col = TILES * j + T
+            part = [lo <= col < hi for lo, hi in parts].index(True)
+            col -= parts[part][0]
+            half, cols = first // BANK, slice(first % BANK, first % BANK + n)
             nc.tensor.matmul_mx(
                 out=dst,
-                lhsT=w_tile(T, j, g).bitcast(FP4X4),
-                lhsT_scale=w_sc[:, g, j * F + T * P : j * F + (T + 1) * P],
-                rhs=x_codes[half][:, g, at : at + n].bitcast(FP8X4),
-                rhs_scale=x_sc[half][:, g, at : at + n],
-                start=(g == 0),
-                stop=(g == 1),
+                lhsT=w_w[part][:, g, col * 2 * P : (col + 1) * 2 * P].bitcast(FP4X4),
+                lhsT_scale=w_sc[part][:, g, col * P : (col + 1) * P],
+                rhs=x_codes[half][:, g, cols].bitcast(FP8X4),
+                rhs_scale=x_sc[half][:, g, cols],
+                start=start,
+                stop=stop,
             )
 
-        def z_step(s):
-            a, pairs, T = STEPS[s]
-            shared = None
-            for j in range(PIECES):
-                first, n = a * PAIR, pairs * PAIR
-                if j == 0 and a == 0 and T < EARLY:
-                    if pairs == 1:
-                        continue
-                    first, n = PAIR, PAIR
-                if pairs == 2 or s == LAST:
-                    dst = next_sum_bank()[:, 0:n]
-                elif shared is None:
-                    shared = next_sum_bank()
-                    dst = shared[:, 0:n]
-                else:
-                    dst = shared[:, PAIR:BANK]
-                    shared = None
-                sums[(s, j)] = dst
+        def z_bank(where, *todo):
+            t = bank(where)
+            for n, s in enumerate(todo):
+                sums[s] = t[:, n * PAIR : n * PAIR + s[3]]
                 for g in range(2):
-                    z_pass(dst, T, j, g, first, n)
+                    z_pass(sums[s], *s, g, g == 0, g == 1)
 
-        def piece_out(dst, src, T, j):
+        def piece_out(j, T, first, n):
+            half, lo = first // BANK, first % BANK
+            if (j, T, half) not in pieces:
+                t = keep.tile([P, BANK], BF16, name="piece%d_%d_%d" % (j, T, half), align_bytes=64)
+                pieces[(j, T, half)] = t
             col = TILES * j + T
-            nc.scalar.activation(out=dst, in_=src, func=ACT.Identity, bias=bias[:, col : col + 1])
-
-        def pieces_out(s, count):
-            a, pairs, T = STEPS[s]
-            pieces_of[s] = []
-            for j in range(count):
-                if a < 2 and (pairs == 1 or (j == 0 and T < EARLY)):
-                    u = half_piece(T, j)
-                    if (s, j) in sums:
-                        second = a == 1 or pairs == 2
-                        piece_out(u[:, PAIR:BANK] if second else u[:, 0:PAIR], sums[(s, j)], T, j)
-                else:
-                    u = stage.tile([P, pairs * PAIR], BF16, name="piece%d" % j, align_bytes=64)
-                    piece_out(u[:], sums[(s, j)], T, j)
-                pieces_of[s].append(u)
-
-        def max_width(s):
-            a, pairs, T = STEPS[s]
-            return 0 if (a, pairs) == (0, 1) else (BANK if a < 2 else pairs * PAIR)
-
-        def first_max(s, lo, hi):
-            if lo == 0:
-                v = stage.tile([P, max_width(s)], BF16, name="upper", align_bytes=64)
-                upper[s] = v
-            nc.vector.tensor_tensor(out=upper[s][:, lo:hi], in0=pieces_of[s][0][:, lo:hi], in1=pieces_of[s][1][:, lo:hi], op=ALU.max)
-
-        def second_max(s, lo, hi):
-            a, pairs, T = STEPS[s]
-            if a == 1:
-                a, pairs = 0, 2
-            h = stage.tile([P, hi - lo], BF16, name="h", align_bytes=64, bufs=8)
-            if len(pieces_of[s]) == PIECES:
-                nc.vector.tensor_tensor(out=h[:], in0=pieces_of[s][2][:, lo:hi], in1=upper[s][:, lo:hi], op=ALU.max)
-            else:
-                col = 2 * TILES + T
-                nc.vector.scalar_tensor_tensor(
-                    out=h[:], in0=sums[(s, 2)][:, lo:hi], scalar=bias[:, col : col + 1], in1=upper[s][:, lo:hi], op0=ALU.add, op1=ALU.max
-                )
-            g, q = T // GROUP, T % GROUP
-            if q == 0:
-                fold = keep.tile([P, 4, pairs * PAIR], BF16, name="fold%d_%d" % (a, g), align_bytes=64)
-                folds[(a, g)] = fold
-                for i in range(pairs):
-                    folded[(a + i, g)] = fold[:, :, i * PAIR : (i + 1) * PAIR]
-            nc.sync.dma_start(out=folds[(a, g)][32 * q : 32 * q + 32, :, lo:hi], in_=h[:])
-
-        def h_weave(a, g, lo, hi, copy):
-            t = stage.tile([P, hi - lo, 4], BF16, name="woven", align_bytes=64)
-            woven[(a, g, lo)] = t
-            copy(out=t[:].rearrange("p (c i) t -> p c t i", i=4), in_=folded[(a, g)][:, :, lo:hi].rearrange("p t (c i) -> p c t i", i=4))
-
-        def h_quant(a, g, lo, hi):
-            nc.vector.quantize_mx(
-                out=h_codes[a][:, g, lo:hi].bitcast(FP8X4), scales=h_sc[a][:, g, lo:hi], in_=woven[(a, g, lo)][:].rearrange("p m t -> p (m t)")
+            nc.scalar.activation(
+                out=pieces[(j, T, half)][:, lo : lo + n],
+                in_=sums[(j, T, first, n)],
+                func=ACT.Identity,
+                bias=bias[:, col : col + 1],
             )
 
-        y_sums = {}
+        def first_max(T, first, n):
+            half, lo = first // BANK, first % BANK
+            t = stage.tile([P, n], BF16, name="upper", align_bytes=64)
+            upper[(T, first)] = t
+            nc.vector.tensor_tensor(out=t[:], in0=pieces[(0, T, half)][:, lo : lo + n], in1=pieces[(1, T, half)][:, lo : lo + n], op=ALU.max)
+
+        def fold(h, T, first, n):
+            g, q = T // GROUP, T % GROUP
+            wide = first < BANK or g == 0
+            key = (first // BANK * 2 if wide else first // PAIR, g)
+            if key not in folds:
+                t = keep.tile([P, 4, BANK if wide else PAIR], BF16, name="fold%d_%d" % key, align_bytes=64)
+                folds[key] = t
+            lo = first - key[0] * PAIR
+            nc.sync.dma_start(out=folds[key][32 * q : 32 * q + 32, :, lo : lo + n], in_=h[:])
+
+        def second_max(T, first, n):
+            half, lo = first // BANK, first % BANK
+            h = stage.tile([P, n], BF16, name="h", align_bytes=64, bufs=8)
+            nc.vector.tensor_tensor(out=h[:], in0=pieces[(2, T, half)][:, lo : lo + n], in1=upper[(T, first)][:], op=ALU.max)
+            fold(h, T, first, n)
+
+        def out_max(dst, j, T, first, n, other):
+            col = TILES * j + T
+            nc.vector.scalar_tensor_tensor(
+                out=dst, in0=sums[(j, T, first, n)], scalar=bias[:, col : col + 1], in1=other, op0=ALU.add, op1=ALU.max
+            )
+
+        def first_out_max(T, first, n):
+            t = stage.tile([P, n], BF16, name="upper", align_bytes=64)
+            upper[(T, first)] = t
+            out_max(t[:], 1, T, first, n, pieces[(0, T, first // BANK)][:, first % BANK : first % BANK + n])
+
+        def second_out_max(T, first, n):
+            h = stage.tile([P, n], BF16, name="h", align_bytes=64, bufs=8)
+            out_max(h[:], 2, T, first, n, upper[(T, first)][:])
+            fold(h, T, first, n)
+
+        def h_weave(first, n, g, copy):
+            key = (first // PAIR, g) if (first // PAIR, g) in folds else (first // BANK * 2, g)
+            lo = first - key[0] * PAIR
+            t = stage.tile([P, n, 4], BF16, name="woven", align_bytes=64)
+            woven[(first, g)] = t
+            copy(out=t[:].rearrange("p (c i) t -> p c t i", i=4), in_=folds[key][:, :, lo : lo + n].rearrange("p t (c i) -> p c t i", i=4))
+
+        def h_quant(first, g):
+            t = woven[(first, g)]
+            a, cols = first // PAIR, slice(first % PAIR, first % PAIR + t.shape[1])
+            nc.vector.quantize_mx(
+                out=h_codes[a][:, g, cols].bitcast(FP8X4), scales=h_sc[a][:, g, cols], in_=t[:].rearrange("p m t -> p (m t)")
+            )
+
+        y_sums, y_rows = {}, {}
 
         def y_pass(r, n, g):
             rows = slice((r % 2) * P, (r % 2 + 1) * P)
@@ -315,11 +283,20 @@ def tile_maxout_then_linear_f7_kernel(tc, x_bytes, x_scale, w_words, w_scales, b
             y_open(r, n, where)
             y_pass(r, n, 1)
 
-        def y_out(r, n, queue=nc.sync):
-            o = stage.tile([P, BANK], F32, name="y", bufs=8)
-            cols = slice(n * BANK, (n + 1) * BANK)
-            nc.vector.tensor_tensor(out=o[:], in0=y_sums[(r, n)][:], in1=c_all[:, cols], op=ALU.add)
+        def y_out(r, n, queue=nc.sync, lo=0, hi=BANK):
+            o = stage.tile([P, hi - lo], F32, name="y", bufs=8)
+            cols = slice(n * BANK + lo, n * BANK + hi)
+            nc.vector.tensor_tensor(out=o[:], in0=y_sums[(r, n)][:, lo:hi], in1=c_all[:, cols], op=ALU.add)
             queue.dma_start(out=out[r * P : (r + 1) * P, cols], in_=o[:])
+
+        def y_row_out(r, n, queue=nc.sync):
+            if n == 0:
+                o = stage.tile([P, N], F32, name="y_row", bufs=4)
+                y_rows[r] = o
+            cols = slice(n * BANK, (n + 1) * BANK)
+            nc.vector.tensor_tensor(out=y_rows[r][:, cols], in0=y_sums[(r, n)][:], in1=c_all[:, cols], op=ALU.add)
+            if n == 1:
+                queue.dma_start(out=out[r * P : (r + 1) * P, :], in_=y_rows[r][:])
 
         idle_bank = bank(0)
 
@@ -329,149 +306,193 @@ def tile_maxout_then_linear_f7_kernel(tc, x_bytes, x_scale, w_words, w_scales, b
 
         on_vector, on_scalar = nc.vector.tensor_copy, nc.scalar.copy
         warm_up(3)
-        spread_turn(0, 3)
-        spread_turn(1, 4)
-        warm_up(1)
-        halves = [(i, g) for i in range(4) for g in range(2)]
-        for i, g in halves[:3]:
-            x_cast(i, g, on_vector)
-        for i, g in halves[3:]:
-            x_cast(i, g, on_scalar)
-        row_turn(0, 0, bank(1))
-        row_turn(0, 1, bank(6))
-        for i, where in ((1, 7), (2, 5)):
-            warm_up(1)
-            both = bank(where)
-            row_turn(i, 0, both)
-            row_turn(i, 1, both)
-        for i in range(2):
-            row_out(i, 0)
-            row_out(i, 1)
-            x_quant(i, 0)
-            x_quant(i, 1)
-        row_out(2, 0)
-        nc.scalar.copy(out=b_f32[:], in_=b_rows[:])
-        spread_out(0)
-        spread_out(1)
-        start_banks = [next_sum_bank() for i in range(EARLY // 2)]
-
-        def start_sum(T, lo, hi):
-            return start_banks[T // 2][:, (T % 2) * PAIR + lo : (T % 2) * PAIR + hi]
-
-        for odd in range(2):
-            for g in range(2):
-                for T in range(odd, EARLY, 2):
-                    z_pass(start_sum(T, 0, P), T, 0, g, 0, P)
-        both = bank(6)
-        row_turn(3, 0, both)
-        row_turn(3, 1, both)
-        b_turned = bank(7)
-        nc.tensor.transpose(b_turned[:, 0:P], b_f32[:], ident[:])
+        for i, g in ((0, 0), (1, 0), (0, 1)):
+            x_sort(i, [g])
+        for i, g in ((1, 1), (2, 0), (3, 0)):
+            x_cast(i, g)
+        x_turn([0], 0, 6)
+        x_turn([1], 0, 7)
+        x_turn([0, 1], 1, 4)
+        b_turned = bank(3)
+        for j in range(PIECES):
+            nc.tensor.matmul(b_turned[:, j * TILES : (j + 1) * TILES], lhsT=b_rows[:, j], rhs=pick[:], start=True, stop=True)
         nc.scalar.copy(out=bias[:], in_=b_turned[:, 0 : PIECES * TILES])
-        for T in range(EARLY):
-            for g in range(2):
-                z_pass(start_sum(T, P, PAIR), T, 0, g, P, P)
-        for T in range(EARLY):
-            piece_out(half_piece(T, 0)[:, 0:PAIR], start_sum(T, 0, PAIR), T, 0)
-        for fed, (i, g) in zip(halves[4:7], halves[5:]):
-            row_out(i, g)
-            x_quant(*fed)
-        x_quant(*halves[7])
-        for a in (2, 3):
-            for job in (x_product, x_sort):
-                job(2 * a)
-                job(2 * a + 1)
+        for job in (x_cast, x_resort):
+            for i in (2, 3):
+                job(i, 1)
+        warm_up(2)
+        x_turn([2, 3], 0, 5)
+        for job in (x_out, x_quant):
+            for i in (0, 1):
+                job(*((i, 1, 0) if job is x_out else (i, 0)))
+        early = [(col // TILES, col % TILES, 0, PAIR) for col in range(EARLY)]
+        early_banks = [bank(i) for i in (6, 0, 1, 2, 3)]
+        for n, s in enumerate(early):
+            sums[s] = early_banks[n // 2][:, (n % 2) * PAIR : (n % 2 + 1) * PAIR]
+            z_pass(sums[s], *s, 0, n % 2 == 0, False)
+        for i in (0, 1):
+            x_out(i, 1, 1)
+        for i in (0, 1):
+            x_quant(i, 1)
+        for n, s in enumerate(early):
+            z_pass(sums[s], *s, 1, False, n % 2 == 1)
+        for s in early:
+            piece_out(*s)
+        for i in (2, 3):
+            x_out(i, 1, 0)
+        for i in (2, 3):
+            x_quant(i, 0)
 
-        ahead, between, behind, tensor_after, scalar_after = {}, {}, {}, {}, {}
+        low = [(j, T) for T in range(GROUP) for j in range(PIECES)]
+        high = [(j, T) for T in range(GROUP, TILES) for j in range(PIECES)]
+        rest_0 = [(j, T, 0, PAIR) for j, T in sorted(low) if (j, T, 0, PAIR) not in early]
+        pair_1 = [(j, T, PAIR, PAIR) for j, T in low + high if j == 0 or T < GROUP]
 
-        def place(table, s, job, *args):
-            table.setdefault(s, []).append((job, args))
+        last_rows = (3 * PAIR, 3 * PAIR + P)
 
-        def run(table, s):
-            for job, args in table.get(s, []):
+        def by_two(todo):
+            return [todo[i : i + 2] for i in range(0, len(todo), 2)]
+
+        slots = (
+            by_two(rest_0)
+            + by_two(pair_1)
+            + [[(j, T, 0, BANK)] for j, T in high if j > 0]
+            + [[(j, T, BANK, BANK)] for j, T in low]
+            + by_two([(j, T, BANK, PAIR) for j, T in high])
+            + by_two([(j, T, 3 * PAIR, PAIR) for j, T in high[:-4] + [high[-3], high[-4]]])
+            + [[(j, TILES - 1, first, P)] for first in last_rows for j in (1, 2)]
+        )
+        at = {s: n for n, todo in enumerate(slots) for s in todo}
+        tensor_after, scalar_after, vector_after = {}, {}, {}
+
+        def place(table, n, job, *args):
+            table.setdefault(n, []).append((job, args))
+
+        def run(table, n):
+            for job, args in table.get(n, []):
                 job(*args)
 
-        def fold_arrives(a, g):
-            done = max(s for s, (first, pairs, T) in enumerate(STEPS) if first <= a < first + pairs and T // GROUP == g)
-            return done + FOLD_STEPS[STEPS[done + 1][1]]
-
-        turn_2, turn_3 = TURN_AFTER[2], TURN_AFTER[3]
-        for a, s in TURN_AFTER.items():
-            place(tensor_after, s, pair_turn, a)
-            place(scalar_after, s, pair_out, a, 0, on_scalar)
-        place(ahead, turn_2, pair_out, 2, 1, on_vector)
-        place(scalar_after, turn_3, pair_out, 3, 1, on_scalar)
+        turn_2, turn_3 = at[rest_0[-1]], at[(2, 3, PAIR, PAIR)]
         for g in range(2):
-            place(between, turn_2 + 1 + g, x_quant, 4, g)
-            place(behind, turn_3, x_quant, 6, g)
-        vector_empties = [
-            s for s in range(turn_3, LAST + 1) if s <= turn_3 + 1 or STEPS[s][2] % GROUP == GROUP - 1 or s >= LAST - 1
-        ]
-        s = turn_3 + 1
-        for a, g in ((0, 0), (1, 0), (0, 1), (1, 1), (2, 0)):
-            s = max(s + 1, fold_arrives(a, g))
-            place(behind, s, h_weave, a, g, 0, PAIR, on_vector)
-            place(between, s + 1, h_quant, a, g, 0, PAIR)
-        for r in range(2):
-            place(scalar_after, s + 1 + r, h_weave, 3, 0, r * P, (r + 1) * P, on_scalar)
-            place(between, s + 3 + r, h_quant, 3, 0, r * P, (r + 1) * P)
+            place(tensor_after, turn_2, x_turn, [4, 5], g, SUM_BANKS + g)
+            place(tensor_after, turn_3, x_turn, [6, 7], g, SUM_BANKS + g)
         tiles = [(r, n) for r in range(M // P) for n in range(2)]
+        vector_empties = [(2, 3, BANK, BANK), (2, 7, BANK, PAIR)] + [(j, 7, first, P) for first in last_rows for j in (1, 2)]
+        order, pending = [], []
+
+        def then(n, job, *args):
+            order.append(max(order[-1:] + [n]))
+            place(vector_after, order[-1], job, *args)
+
+        def done(j, T, first):
+            return max(n for s, n in at.items() if s[:2] == (j, T) and s[2] <= first < s[2] + s[3])
+
+        def max_1(T, first, n):
+            then(done(1, T, first + n - 1), first_out_max if (1, T, first, n) in vector_empties else first_max, T, first, n)
+
+        def max_2(T, first, n):
+            then(done(2, T, first + n - 1), second_out_max if (2, T, first, n) in vector_empties else second_max, T, first, n)
+
+        def y_tile(n):
+            r, half = tiles.pop(0)
+            place(tensor_after, n, y_mul, r, half, SUM_BANKS + half)
+            pending.append((n, r, half))
+
+        def y_empty():
+            n, r, half = pending.pop(0)
+            then(n, y_out, r, half)
+
+        for i in (4, 5):
+            then(-1, x_sort, i, [0, 1])
+        for i in (2, 3):
+            then(-1, x_out, i, 1, 1)
+        for i in (2, 3):
+            then(-1, x_quant, i, 1)
+        for i in (6, 7):
+            then(-1, x_sort, i, [0, 1])
+        for g in range(2):
+            then(turn_2, x_out, 4, 2, g)
+        then(turn_2, x_quant, 4, 0)
+        max_1(0, 0, BANK)
+        then(turn_2, x_quant, 4, 1)
+        for T in range(1, GROUP):
+            max_1(T, 0, BANK)
+            max_2(T - 1, 0, BANK)
+        then(turn_3, x_out, 6, 2, 0)
+        max_2(GROUP - 1, 0, BANK)
+        then(turn_3, x_out, 6, 2, 1)
+        then(turn_3, x_quant, 6, 0)
+        max_1(4, 0, BANK)
+        then(turn_3, x_quant, 6, 1)
+        max_2(4, 0, BANK)
+        A, B, C, D = 0, PAIR, BANK, 3 * PAIR
+        steps = [(T, 0, BANK) for T in range(GROUP + 1, TILES)] + [(T, BANK, BANK) for T in range(GROUP)]
+        steps += [(T, first, PAIR) for first in (C, D) for T in range(GROUP, TILES)][:-1]
+        mid = {1: [(A, PAIR, 0)], 2: [(A, 0)], 3: [(B, PAIR, 0)], 4: [(B, 0)], 5: [(A, 1)], 6: [(B, 1)], 11: [(C, 0), (C + P, 0)], 12: [(D, 0), (D + P, 0)], 13: ["y"]}
+        post = {4: [(A, PAIR, 1)], 5: [(B, PAIR, 1)], 9: ["y"], 10: ["y", (C, P, 0)], 11: ["y", (D, P, 0)], 12: ["y"]}
+        on_s = {10: [(1, (C + P, P, 0))], 11: [(2, (D + P, P, 0))]}
+        y_at = {9: [2], 10: [2], 11: [2], 12: [2], 13: [1]}
+
+        def do(jobs):
+            for job in jobs:
+                if job == "y":
+                    y_empty()
+                elif len(job) == 2:
+                    then(-1, h_quant, *job)
+                else:
+                    then(-1, h_weave, *job, on_vector)
+
+        for k, (T, first, n) in enumerate(steps):
+            for j in y_at.get(k, []):
+                y_tile(done(j, T, first))
+            for j, job in on_s.get(k, []):
+                place(scalar_after, done(j, T, first), h_weave, *job, on_scalar)
+            max_1(T, first, n)
+            do(mid.get(k, []))
+            if k == len(steps) - 1:
+                for row in last_rows:
+                    max_1(7, row, P)
+            max_2(T, first, n)
+            do(post.get(k, []))
+        for first in last_rows:
+            max_2(7, first, P)
+        held = tiles[:-4]
+        x_turn([2, 3], 1, 7)
+        run(vector_after, -1)
+        for n, todo in enumerate(slots):
+            z_bank((4 + n) % SUM_BANKS, *todo)
+            run(tensor_after, n)
+            for s in todo:
+                if s not in vector_empties:
+                    piece_out(*s)
+            run(scalar_after, n)
+            run(vector_after, n)
+
         final = tiles[-4:]
-        held = tiles[-4 - HELD : -4]
-        free_steps = [s for s in range(fold_arrives(0, 1) + 1, LAST) if s not in behind]
-        for s, (r, n) in zip(free_steps, tiles[: -4 - HELD]):
-            place(tensor_after, s, y_mul, r, n, SUM_BANKS + n)
-            place(behind, s, y_out, r, n)
-
-        lagging = [s for s in range(LAST) if STEPS[s][1] == 1 and max_width(s) and s not in between and s not in vector_empties]
-
-        def vector_steps(s):
-            if s < turn_2 or s == LAST:
-                return []
-            return range(GROUP, s + 1) if s == turn_2 else [s]
-
-        for s in range(LAST + 1):
-            z_step(s)
-            run(tensor_after, s)
-            pieces_out(s, 2 if s in vector_empties else PIECES)
-            run(scalar_after, s)
-            run(ahead, s)
-            for r in vector_steps(s):
-                first_max(r, 0, max_width(r))
-                if r - 1 in lagging:
-                    second_max(r - 1, 0, max_width(r - 1))
-                run(between, r)
-                if r not in lagging:
-                    second_max(r, 0, max_width(r))
-                run(behind, r)
-
-        row_tiles = ((0, P), (P, PAIR))
-        free_banks = [2, 6, 7, 3, 4, 5, 0, 1]
-        for lo, hi in row_tiles:
-            first_max(LAST, lo, hi)
-        for lo, hi in row_tiles:
-            second_max(LAST, lo, hi)
-        for i in range(2):
-            y_mul(*held[i], free_banks[i])
-        for lo, hi in row_tiles:
-            h_weave(2, 1, lo, hi, on_scalar)
-        h_quant(2, 1, 0, P)
-        y_out(*held[0])
-        h_quant(2, 1, P, PAIR)
-        for i in range(2, len(held)):
-            y_mul(*held[i], free_banks[i])
-        for tile in held[1:3]:
-            y_out(*tile)
-        for i, tile in enumerate(final):
-            y_open(*tile, free_banks[(len(held) + i) % 8])
-        for tile in held[3:5]:
-            y_out(*tile)
-        for lo, hi in row_tiles:
-            h_weave(3, 1, lo, hi, on_scalar)
-        h_quant(3, 1, 0, P)
-        y_out(*held[5], nc.scalar)
-        h_quant(3, 1, P, PAIR)
+        last = len(slots) - 1
+        free_banks = [SUM_BANKS + held[0][1], (4 + last + 1) % 6, SUM_BANKS + 1 - held[0][1]] + [(4 + last + i) % 6 for i in (2, 3, 5, 4, 6)]
+        free_banks = free_banks + free_banks
+        opened = final[: 0]
+        for first in (C, C + P):
+            h_weave(first, P, 1, on_scalar)
+        quant_after = {0: [C], 1: [C + P], 4: [D], 5: [D + P]}
+        for i, tile in enumerate(held):
+            y_mul(*tile, free_banks.pop(0))
+            if i == len(held) - 1:
+                for t in opened:
+                    y_open(*t, free_banks.pop(0))
+            y_out(*tile, nc.scalar if i == len(held) - 1 else nc.sync)
+            if i == 2:
+                for first in last_rows:
+                    h_weave(first, P, 1, on_scalar)
+            for first in quant_after.get(i, []):
+                h_quant(first, 1)
         for tile in final:
-            y_pass(*tile, 1)
-        for r, n in final:
+            if tile in opened:
+                y_pass(*tile, 1)
+            else:
+                y_mul(*tile, free_banks.pop(0))
+        for r, n in final[:-1]:
             y_out(r, n, (nc.sync, nc.scalar)[n])
+        y_out(*final[-1], nc.scalar, 0, PAIR)
+        y_out(*final[-1], nc.sync, PAIR, BANK)

@@ -23,10 +23,13 @@ BANK = 512
 PAIR = 2 * P
 TILES = F // P
 GROUP = 4
-SUM_BANKS = 6
 EARLY = 10
 FIRST = 4
-LATE = 20
+NARROW = 14
+TURN_AFTER = 6
+WIDE = 4
+OWN = 8
+A, B, C, D = 0, PAIR, 2 * PAIR, 3 * PAIR
 
 
 def tile_maxout_then_linear_f7_kernel(tc, x_bytes, x_scale, w_words, w_scales, b, v_words, v_scales, c, out):
@@ -41,7 +44,7 @@ def tile_maxout_then_linear_f7_kernel(tc, x_bytes, x_scale, w_words, w_scales, b
             t = psum.tile([P, BANK], F32, name="bank%d" % i)
             return t
 
-        parts = ((0, EARLY), (EARLY, LATE), (LATE, PIECES * TILES))
+        parts = ((0, EARLY), (EARLY, 2 * TILES), (2 * TILES, PIECES * TILES))
         scale_cols = keep.tile([P, 2, 4], F32, name="scale_cols")
         w_w = [keep.tile([P, 2, (hi - lo) * 2 * P], U8, name="w_w%d" % lo, align_bytes=256) for lo, hi in parts]
         w_sc = [keep.tile([P, 2, (hi - lo) * P], U8, name="w_sc%d" % lo, align_bytes=256) for lo, hi in parts]
@@ -52,22 +55,16 @@ def tile_maxout_then_linear_f7_kernel(tc, x_bytes, x_scale, w_words, w_scales, b
         one = keep.tile([P, 1], F32, name="one")
         b_rows = keep.tile([P, PIECES, P], BF16, name="b_rows")
         bias = keep.tile([P, PIECES * TILES], F32, name="bias")
-        x_start = [keep.tile([P, PASS], U8, name="x_start%d" % i, align_bytes=64) for i in range(2)]
-        x_next = keep.tile([P, 2, PASS], U8, name="x_next", align_bytes=64)
-        x_pair = [keep.tile([P, 2, K], U8, name="x_pair%d" % a, align_bytes=64) for a in range(1, 4)]
+        x_tile = [keep.tile([P, K], U8, name="x_tile%d" % i, align_bytes=64) for i in range(4)]
+        x_pair = [keep.tile([P, 2, K], U8, name="x_pair%d" % a, align_bytes=64) for a in (2, 3)]
         c_all = keep.tile([P, N], BF16, name="c_all")
         zeros = keep.tile([P, BANK], BF16, name="zeros")
 
-        nc.scalar.dma_start(out=scale_cols[:], in_=x_scale.rearrange("o (g p t) -> p (o g) t", g=2, t=4))
-        nc.vector.memset(b_rows[:], 0.0)
-        nc.vector.memset(zeros[:], 0.0)
-        for tile in (w_sc[0], w_sc[1], w_sc[2], v_sc):
+        def clear(tile):
             nc.vector.memset(tile[:].rearrange("p g n -> p (g n)").bitcast(U32), 0)
-        nc.vector.memset(one[:], 1.0)
-        make_identity(nc, ident[:])
 
         def load_pair(a):
-            nc.sync.dma_start(out=x_pair[a - 1][:], in_=x_bytes[a * PAIR : (a + 1) * PAIR, :].rearrange("(r p) k -> p r k", p=P))
+            nc.sync.dma_start(out=x_pair[a - 2][:], in_=x_bytes[a * PAIR : (a + 1) * PAIR, :].rearrange("(r p) k -> p r k", p=P))
 
         def load_w(part, g, lo=None, hi=None):
             base = parts[part][0]
@@ -85,56 +82,58 @@ def tile_maxout_then_linear_f7_kernel(tc, x_bytes, x_scale, w_words, w_scales, b
         def load_w_scales(part):
             load_scales(w_sc[part], w_scales, parts[part][0] * P, parts[part][1] * P)
 
-        for i in range(2):
-            nc.sync.dma_start(out=x_start[i][:], in_=x_bytes[i * P : (i + 1) * P, 0:PASS])
-        nc.sync.dma_start(out=x_next[:], in_=x_bytes[0:PAIR, PASS:K].rearrange("(r p) k -> p r k", p=P))
-        load_pair(1)
-        nc.scalar.dma_start(out=b_rows[0:TILES], in_=b.rearrange("j (t p) -> t j p", p=P))
+        nc.scalar.dma_start(out=scale_cols[:], in_=x_scale.rearrange("o (g p t) -> p (o g) t", g=2, t=4))
+        make_identity(nc, ident[:])
+        nc.vector.memset(zeros[:], 0.0)
+        clear(w_sc[0])
+        nc.vector.memset(one[:], 1.0)
+        nc.vector.memset(b_rows[:], 0.0)
+        for tile in w_sc[1:]:
+            clear(tile)
         nc.scalar.activation(out=pick[:], in_=ident[:, 0:TILES], func=ACT.Identity)
+        for i in range(4):
+            nc.sync.dma_start(out=x_tile[i][:], in_=x_bytes[i * P : (i + 1) * P, :])
         load_w_scales(0)
         load_w(0, 0, 0, FIRST)
         load_w(0, 0, FIRST, EARLY)
+        nc.sync.dma_start(out=b_rows[0:TILES], in_=b.rearrange("j (t p) -> t j p", p=P))
         load_w(0, 1)
-        load_pair(2)
         load_w_scales(1)
         load_w(1, 0)
         load_w(1, 1)
+        load_pair(2)
         load_pair(3)
         load_w_scales(2)
         load_w(2, 0)
         load_w(2, 1)
-        load_scales(v_sc, v_scales, 0, N)
-        for g in range(2):
-            nc.sync.dma_start(out=v_w[:, g].bitcast(I32), in_=v_words[g].rearrange("p n t -> p (n t)").bitcast(I32))
-        nc.sync.dma_start(out=c_all[:], in_=c.partition_broadcast(P))
+
+        def load_v():
+            clear(v_sc)
+            load_scales(v_sc, v_scales, 0, N)
+            for g in range(2):
+                nc.sync.dma_start(out=v_w[:, g].bitcast(I32), in_=v_words[g].rearrange("p n t -> p (n t)").bitcast(I32))
+            nc.sync.dma_start(out=c_all[:], in_=c.partition_broadcast(P))
 
         x_codes = [keep.tile([P, 2, BANK], U32, name="x_codes%d" % i, align_bytes=256) for i in range(2)]
         x_sc = [keep.tile([P, 2, BANK], U8, name="x_sc%d" % i, align_bytes=256) for i in range(2)]
         h_codes = [keep.tile([P, 2, PAIR], U32, name="h_codes%d" % i, align_bytes=256) for i in range(4)]
         h_sc = [keep.tile([P, 2, PAIR], U8, name="h_sc%d" % i, align_bytes=256) for i in range(4)]
 
-        plain, words, turned, grouped = {}, {}, {}, {}
+        words, turned, grouped = {}, {}, {}
 
         def x_row(i, passes):
-            if i >= 2:
-                return x_pair[i // 2 - 1][:, i % 2, passes[0] * PASS : (passes[-1] + 1) * PASS].bitcast(E4M3)
-            return (x_start[i][:] if passes[0] == 0 else x_next[:, i]).bitcast(E4M3)
+            if i >= 4:
+                return x_pair[i // 2 - 2][:, i % 2, passes[0] * PASS : (passes[-1] + 1) * PASS].bitcast(E4M3)
+            return x_tile[i][:, passes[0] * PASS : (passes[-1] + 1) * PASS].bitcast(E4M3)
 
         def x_cast(i, g):
-            t = stage.tile([P, PASS], BF16, name="plain", align_bytes=64, bufs=5)
-            plain[(i, g)] = t
+            t = keep.tile([P, PASS], BF16, name="plain%d_%d" % (i, g), align_bytes=64)
             nc.scalar.copy(out=t[:], in_=x_row(i, [g]))
             for u in range(2):
                 words[(i, g, u)] = t[:].bitcast(F32)[:, u:PAIR:2]
 
-        def x_resort(i, g):
-            t = stage.tile([P, 2, P], F32, name="resorted", align_bytes=64)
-            nc.scalar.copy(out=t[:], in_=plain[(i, g)][:].bitcast(F32).rearrange("m (w u) -> m u w", u=2))
-            for u in range(2):
-                words[(i, g, u)] = t[:, u]
-
         def x_sort(i, passes):
-            t = stage.tile([P, 2, len(passes) * P, 2], BF16, name="sorted", align_bytes=64)
+            t = keep.tile([P, 2, len(passes) * P, 2], BF16, name="sorted%d_%d" % (i, passes[0]), align_bytes=64)
             nc.vector.tensor_scalar(
                 out=t[:].rearrange("m u w e -> m w u e"),
                 in0=x_row(i, passes).rearrange("m (w u e) -> m w u e", u=2, e=2),
@@ -146,13 +145,14 @@ def tile_maxout_then_linear_f7_kernel(tc, x_bytes, x_scale, w_words, w_scales, b
                 for u in range(2):
                     words[(i, g, u)] = t[:].rearrange("m u w e -> m u (w e)").bitcast(F32)[:, u, n * P : (n + 1) * P]
 
-        def x_turn(rows, g, where):
-            t = bank(where)
-            for i in rows:
-                turned[(i, g)] = t
-                for u in range(2):
-                    at = u * PAIR + (i % 2) * P
-                    nc.tensor.transpose(t[:, at : at + P], words[(i, g, u)], ident[:])
+        def x_turn(i, g, where):
+            if (where, g, i // 2) not in turned:
+                turned[(where, g, i // 2)] = bank(where)
+            t = turned[(where, g, i // 2)]
+            turned[(i, g)] = t
+            for u in range(2):
+                at = u * PAIR + (i % 2) * P
+                nc.tensor.transpose(t[:, at : at + P], words[(i, g, u)], ident[:])
 
         def x_out(i, rows, g):
             t = stage.tile([P, rows * P, 4], BF16, name="grouped", align_bytes=64)
@@ -174,13 +174,14 @@ def tile_maxout_then_linear_f7_kernel(tc, x_bytes, x_scale, w_words, w_scales, b
 
         sums, pieces, upper, folds, woven = {}, {}, {}, {}, {}
 
-        def z_pass(dst, j, T, first, n, g, start, stop):
+        def z_pass(s, g, start, stop):
+            j, T, first, n = s
             col = TILES * j + T
             part = [lo <= col < hi for lo, hi in parts].index(True)
             col -= parts[part][0]
             half, cols = first // BANK, slice(first % BANK, first % BANK + n)
             nc.tensor.matmul_mx(
-                out=dst,
+                out=sums[s],
                 lhsT=w_w[part][:, g, col * 2 * P : (col + 1) * 2 * P].bitcast(FP4X4),
                 lhsT_scale=w_sc[part][:, g, col * P : (col + 1) * P],
                 rhs=x_codes[half][:, g, cols].bitcast(FP8X4),
@@ -189,66 +190,100 @@ def tile_maxout_then_linear_f7_kernel(tc, x_bytes, x_scale, w_words, w_scales, b
                 stop=stop,
             )
 
-        def z_bank(where, *todo):
+        def z_open(where, todo):
             t = bank(where)
             for n, s in enumerate(todo):
                 sums[s] = t[:, n * PAIR : n * PAIR + s[3]]
+
+        def z_bank(where, todo):
+            z_open(where, todo)
+            for s in todo:
                 for g in range(2):
-                    z_pass(sums[s], *s, g, g == 0, g == 1)
+                    z_pass(s, g, g == 0, g == 1)
+
+        def z_first(where, todo):
+            z_open(where, todo)
+            for n, s in enumerate(todo):
+                z_pass(s, 0, n == 0, False)
+
+        def z_second(todo):
+            for n, s in enumerate(todo):
+                z_pass(s, 1, False, n == len(todo) - 1)
+
+        def b_turn(where):
+            t = bank(where)
+            turned["b"] = t
+            for j in range(PIECES):
+                nc.tensor.matmul(t[:, j * TILES : (j + 1) * TILES], lhsT=b_rows[:, j], rhs=pick[:], start=True, stop=True)
+
+        def b_out():
+            nc.scalar.copy(out=bias[:], in_=turned["b"][:, 0 : PIECES * TILES])
+
+        def of_half(store, name, T, first, n):
+            half, lo = first // BANK, first % BANK
+            if (name, T, half) not in store:
+                t = keep.tile([P, BANK], BF16, name="%s_%d_%d" % (name, T, half), align_bytes=64)
+                store[(name, T, half)] = t
+            return store[(name, T, half)][:, lo : lo + n]
+
+        def piece(j, T, first, n):
+            return of_half(pieces, "piece%d" % j, T, first, n)
 
         def piece_out(j, T, first, n):
-            half, lo = first // BANK, first % BANK
-            if (j, T, half) not in pieces:
-                t = keep.tile([P, BANK], BF16, name="piece%d_%d_%d" % (j, T, half), align_bytes=64)
-                pieces[(j, T, half)] = t
             col = TILES * j + T
-            nc.scalar.activation(
-                out=pieces[(j, T, half)][:, lo : lo + n],
-                in_=sums[(j, T, first, n)],
-                func=ACT.Identity,
-                bias=bias[:, col : col + 1],
-            )
+            nc.scalar.activation(out=piece(j, T, first, n), in_=sums[(j, T, first, n)], func=ACT.Identity, bias=bias[:, col : col + 1])
 
         def first_max(T, first, n):
-            half, lo = first // BANK, first % BANK
-            t = stage.tile([P, n], BF16, name="upper", align_bytes=64)
-            upper[(T, first)] = t
-            nc.vector.tensor_tensor(out=t[:], in0=pieces[(0, T, half)][:, lo : lo + n], in1=pieces[(1, T, half)][:, lo : lo + n], op=ALU.max)
+            nc.vector.tensor_tensor(out=of_half(upper, "upper", T, first, n), in0=piece(0, T, first, n), in1=piece(1, T, first, n), op=ALU.max)
+
+        def fold_key(first, g):
+            return (first // PAIR, g) if first >= BANK and g == 1 else (first // BANK * 2, g)
 
         def fold(h, T, first, n):
             g, q = T // GROUP, T % GROUP
-            wide = first < BANK or g == 0
-            key = (first // BANK * 2 if wide else first // PAIR, g)
-            if key not in folds:
-                t = keep.tile([P, 4, BANK if wide else PAIR], BF16, name="fold%d_%d" % key, align_bytes=64)
-                folds[key] = t
-            lo = first - key[0] * PAIR
-            nc.sync.dma_start(out=folds[key][32 * q : 32 * q + 32, :, lo : lo + n], in_=h[:])
+            width = PAIR if first >= BANK and g == 1 else BANK
+            for lo in range(first, first + n, width):
+                key = fold_key(lo, g)
+                if key not in folds:
+                    t = keep.tile([P, 4, width], BF16, name="fold%d_%d" % key, align_bytes=64)
+                    folds[key] = t
+                m = min(n, width)
+                at = lo - key[0] * PAIR
+                nc.sync.dma_start(out=folds[key][32 * q : 32 * q + 32, :, at : at + m], in_=h[:, lo - first : lo - first + m])
 
         def second_max(T, first, n):
-            half, lo = first // BANK, first % BANK
             h = stage.tile([P, n], BF16, name="h", align_bytes=64, bufs=8)
-            nc.vector.tensor_tensor(out=h[:], in0=pieces[(2, T, half)][:, lo : lo + n], in1=upper[(T, first)][:], op=ALU.max)
+            nc.vector.tensor_tensor(out=h[:], in0=piece(2, T, first, n), in1=of_half(upper, "upper", T, first, n), op=ALU.max)
             fold(h, T, first, n)
 
-        def out_max(dst, j, T, first, n, other):
+        def first_out_max(s):
+            j, T, first, n = s
             col = TILES * j + T
             nc.vector.scalar_tensor_tensor(
-                out=dst, in0=sums[(j, T, first, n)], scalar=bias[:, col : col + 1], in1=other, op0=ALU.add, op1=ALU.max
+                out=of_half(upper, "upper", T, first, n),
+                in0=sums[s],
+                scalar=bias[:, col : col + 1],
+                in1=piece(0, T, first, n),
+                op0=ALU.add,
+                op1=ALU.max,
             )
 
-        def first_out_max(T, first, n):
-            t = stage.tile([P, n], BF16, name="upper", align_bytes=64)
-            upper[(T, first)] = t
-            out_max(t[:], 1, T, first, n, pieces[(0, T, first // BANK)][:, first % BANK : first % BANK + n])
-
-        def second_out_max(T, first, n):
+        def last_max(s, first, n):
+            T = s[1]
+            col = TILES * 2 + T
             h = stage.tile([P, n], BF16, name="h", align_bytes=64, bufs=8)
-            out_max(h[:], 2, T, first, n, upper[(T, first)][:])
+            nc.vector.scalar_tensor_tensor(
+                out=h[:],
+                in0=sums[s][:, first - s[2] : first - s[2] + n],
+                scalar=bias[:, col : col + 1],
+                in1=of_half(upper, "upper", T, first, n),
+                op0=ALU.add,
+                op1=ALU.max,
+            )
             fold(h, T, first, n)
 
         def h_weave(first, n, g, copy):
-            key = (first // PAIR, g) if (first // PAIR, g) in folds else (first // BANK * 2, g)
+            key = fold_key(first, g)
             lo = first - key[0] * PAIR
             t = stage.tile([P, n, 4], BF16, name="woven", align_bytes=64)
             woven[(first, g)] = t
@@ -261,238 +296,271 @@ def tile_maxout_then_linear_f7_kernel(tc, x_bytes, x_scale, w_words, w_scales, b
                 out=h_codes[a][:, g, cols].bitcast(FP8X4), scales=h_sc[a][:, g, cols], in_=t[:].rearrange("p m t -> p (m t)")
             )
 
-        y_sums, y_rows = {}, {}
-
-        def y_pass(r, n, g):
-            rows = slice((r % 2) * P, (r % 2 + 1) * P)
-            nc.tensor.matmul_mx(
-                out=y_sums[(r, n)][:],
-                lhsT=h_codes[r // 2][:, g, rows].bitcast(FP8X4),
-                lhsT_scale=h_sc[r // 2][:, g, rows],
-                rhs=v_w[:, g, 4 * n * BANK : 4 * (n + 1) * BANK].bitcast(FP8X4),
-                rhs_scale=v_sc[:, g, n * BANK : (n + 1) * BANK],
-                start=(g == 0),
-                stop=(g == 1),
-            )
-
-        def y_open(r, n, where):
-            y_sums[(r, n)] = bank(where)
-            y_pass(r, n, 0)
+        y_sums = {}
 
         def y_mul(r, n, where):
-            y_open(r, n, where)
-            y_pass(r, n, 1)
+            y_sums[(r, n)] = bank(where)
+            rows = slice((r % 2) * P, (r % 2 + 1) * P)
+            for g in range(2):
+                nc.tensor.matmul_mx(
+                    out=y_sums[(r, n)][:],
+                    lhsT=h_codes[r // 2][:, g, rows].bitcast(FP8X4),
+                    lhsT_scale=h_sc[r // 2][:, g, rows],
+                    rhs=v_w[:, g, 4 * n * BANK : 4 * (n + 1) * BANK].bitcast(FP8X4),
+                    rhs_scale=v_sc[:, g, n * BANK : (n + 1) * BANK],
+                    start=(g == 0),
+                    stop=(g == 1),
+                )
 
-        def y_out(r, n, queue=nc.sync, lo=0, hi=BANK):
+        def y_out(r, n, queue, lo, hi):
             o = stage.tile([P, hi - lo], F32, name="y", bufs=8)
             cols = slice(n * BANK + lo, n * BANK + hi)
             nc.vector.tensor_tensor(out=o[:], in0=y_sums[(r, n)][:, lo:hi], in1=c_all[:, cols], op=ALU.add)
             queue.dma_start(out=out[r * P : (r + 1) * P, cols], in_=o[:])
 
-        def y_row_out(r, n, queue=nc.sync):
-            if n == 0:
-                o = stage.tile([P, N], F32, name="y_row", bufs=4)
-                y_rows[r] = o
-            cols = slice(n * BANK, (n + 1) * BANK)
-            nc.vector.tensor_tensor(out=y_rows[r][:, cols], in0=y_sums[(r, n)][:], in1=c_all[:, cols], op=ALU.add)
-            if n == 1:
-                queue.dma_start(out=out[r * P : (r + 1) * P, :], in_=y_rows[r][:])
-
-        idle_bank = bank(0)
-
         def warm_up(times):
+            t = bank(0)
             for i in range(times):
-                nc.tensor.matmul(idle_bank[:], lhsT=zeros[:, 0:P], rhs=zeros[:], start=True, stop=True)
+                nc.tensor.matmul(t[:], lhsT=zeros[:, 0:P], rhs=zeros[:], start=True, stop=True)
 
-        on_vector, on_scalar = nc.vector.tensor_copy, nc.scalar.copy
-        warm_up(3)
-        for i, g in ((0, 0), (1, 0), (0, 1)):
-            x_sort(i, [g])
-        for i, g in ((1, 1), (2, 0), (3, 0)):
-            x_cast(i, g)
-        x_turn([0], 0, 6)
-        x_turn([1], 0, 7)
-        x_turn([0, 1], 1, 4)
-        b_turned = bank(3)
-        for j in range(PIECES):
-            nc.tensor.matmul(b_turned[:, j * TILES : (j + 1) * TILES], lhsT=b_rows[:, j], rhs=pick[:], start=True, stop=True)
-        nc.scalar.copy(out=bias[:], in_=b_turned[:, 0 : PIECES * TILES])
-        for job in (x_cast, x_resort):
-            for i in (2, 3):
-                job(i, 1)
-        warm_up(2)
-        x_turn([2, 3], 0, 5)
-        for job in (x_out, x_quant):
-            for i in (0, 1):
-                job(*((i, 1, 0) if job is x_out else (i, 0)))
-        early = [(col // TILES, col % TILES, 0, PAIR) for col in range(EARLY)]
-        early_banks = [bank(i) for i in (6, 0, 1, 2, 3)]
-        for n, s in enumerate(early):
-            sums[s] = early_banks[n // 2][:, (n % 2) * PAIR : (n % 2 + 1) * PAIR]
-            z_pass(sums[s], *s, 0, n % 2 == 0, False)
-        for i in (0, 1):
-            x_out(i, 1, 1)
-        for i in (0, 1):
-            x_quant(i, 1)
-        for n, s in enumerate(early):
-            z_pass(sums[s], *s, 1, False, n % 2 == 1)
-        for s in early:
-            piece_out(*s)
-        for i in (2, 3):
-            x_out(i, 1, 0)
-        for i in (2, 3):
-            x_quant(i, 0)
+        tensor_jobs, scalar_jobs, vector_jobs = [], [], []
+        emptied_by = {}
 
-        low = [(j, T) for T in range(GROUP) for j in range(PIECES)]
-        high = [(j, T) for T in range(GROUP, TILES) for j in range(PIECES)]
-        rest_0 = [(j, T, 0, PAIR) for j, T in sorted(low) if (j, T, 0, PAIR) not in early]
-        pair_1 = [(j, T, PAIR, PAIR) for j, T in low + high if j == 0 or T < GROUP]
+        def rows_of(first, n):
+            return range(first // P, (first + n) // P)
 
-        last_rows = (3 * PAIR, 3 * PAIR + P)
+        def named(name, first, n, *more):
+            return [(name, r) + more for r in rows_of(first, n)]
+
+        def on_tensor(job, args, needs, gives, where=None, readers=None):
+            if readers is not None:
+                needs = needs + emptied_by.get(where, [])
+                emptied_by[where] = readers
+            tensor_jobs.append((job, args, needs, gives))
+
+        def x_needs(todo, passes):
+            return [key for s in todo for g in passes for key in named("codes", s[2], s[3], g)]
+
+        def sum_keys(name, todo):
+            return [key for s in todo for key in named(name, s[2], s[3], s[0], s[1])]
+
+        def turn(i, g, where, opens):
+            readers = [("grouped", r, g) for r in opens] if opens else None
+            on_tensor(x_turn, (i, g, where), [("words", i, g)], [("turned", i, g)], where, readers)
+
+        def slot(todo, by_vector=False):
+            where = ring.pop(0)
+            ring.append(where)
+            on_tensor(z_bank, (where, todo), x_needs(todo, (0, 1)), sum_keys("sum", todo), where, sum_keys("piece", todo))
+            if not by_vector:
+                empty(todo)
+
+        def empty(todo):
+            for s in todo:
+                scalar_jobs.append((piece_out, s, sum_keys("sum", [s]) + ["bias"], sum_keys("piece", [s])))
+
+        def y_slot():
+            r, n = tiles.pop(0)
+            where = ring.pop(0)
+            ring.append(where)
+            on_tensor(y_mul, (r, n, where), [("h", r, 0), ("h", r, 1)], [("y", r, n)], where, [("stored", r, n)])
+            pending.append((r, n))
+
+        def cast(i, g):
+            scalar_jobs.append((x_cast, (i, g), [], [("words", i, g)]))
+
+        def sort(i, passes):
+            vector_jobs.append((x_sort, (i, passes), [], [("words", i, g) for g in passes]))
+
+        def scale(i, rows, g):
+            vector_jobs.append((x_out, (i, rows, g), named("turned", i * P, rows * P, g), named("grouped", i * P, rows * P, g)))
+
+        def quant(i, rows, g):
+            vector_jobs.append((x_quant, (i, g), [], named("codes", i * P, rows * P, g)))
+
+        def max_1(T, first, n):
+            vector_jobs.append((first_max, (T, first, n), named("piece", first, n, 0, T) + named("piece", first, n, 1, T), []))
+
+        def max_2(T, first, n):
+            vector_jobs.append((second_max, (T, first, n), named("piece", first, n, 2, T), named("fold", first, n, T)))
+
+        def max_out(s, first, n):
+            vector_jobs.append((last_max, (s, first, n), named("sum", first, n, 2, s[1]), named("piece", first, n, 2, s[1]) + named("fold", first, n, s[1])))
+
+        def max_1_out(s):
+            vector_jobs.append((first_out_max, (s,), sum_keys("sum", [s]) + named("piece", s[2], s[3], 0, s[1]), sum_keys("piece", [s])))
+
+        def weave(first, n, g, jobs):
+            needs = [key for T in range(GROUP * g, GROUP * (g + 1)) for key in named("fold", first, n, T)]
+            copy = nc.vector.tensor_copy if jobs is vector_jobs else nc.scalar.copy
+            jobs.append((h_weave, (first, n, g, copy), needs, named("woven", first, n, g)))
+
+        def h_q(first, n, g):
+            vector_jobs.append((h_quant, (first, g), named("woven", first, n, g), named("h", first, n, g)))
+
+        def store(queue=nc.sync, halves=False):
+            r, n = pending.pop(0)
+            if halves:
+                vector_jobs.append((y_out, (r, n, nc.scalar, 0, PAIR), [("y", r, n)], []))
+                vector_jobs.append((y_out, (r, n, nc.sync, PAIR, BANK), [("y", r, n)], [("stored", r, n)]))
+            else:
+                vector_jobs.append((y_out, (r, n, queue, 0, BANK), [("y", r, n)], [("stored", r, n)]))
 
         def by_two(todo):
             return [todo[i : i + 2] for i in range(0, len(todo), 2)]
 
-        slots = (
-            by_two(rest_0)
-            + by_two(pair_1)
-            + [[(j, T, 0, BANK)] for j, T in high if j > 0]
-            + [[(j, T, BANK, BANK)] for j, T in low]
-            + by_two([(j, T, BANK, PAIR) for j, T in high])
-            + by_two([(j, T, 3 * PAIR, PAIR) for j, T in high[:-4] + [high[-3], high[-4]]])
-            + [[(j, TILES - 1, first, P)] for first in last_rows for j in (1, 2)]
-        )
-        at = {s: n for n, todo in enumerate(slots) for s in todo}
-        tensor_after, scalar_after, vector_after = {}, {}, {}
-
-        def place(table, n, job, *args):
-            table.setdefault(n, []).append((job, args))
-
-        def run(table, n):
-            for job, args in table.get(n, []):
-                job(*args)
-
-        turn_2, turn_3 = at[rest_0[-1]], at[(2, 3, PAIR, PAIR)]
-        for g in range(2):
-            place(tensor_after, turn_2, x_turn, [4, 5], g, SUM_BANKS + g)
-            place(tensor_after, turn_3, x_turn, [6, 7], g, SUM_BANKS + g)
         tiles = [(r, n) for r in range(M // P) for n in range(2)]
-        vector_empties = [(2, 3, BANK, BANK), (2, 7, BANK, PAIR)] + [(j, 7, first, P) for first in last_rows for j in (1, 2)]
-        order, pending = [], []
+        pending = []
+        columns = [(col // TILES, col % TILES) for col in range(PIECES * TILES)]
 
-        def then(n, job, *args):
-            order.append(max(order[-1:] + [n]))
-            place(vector_after, order[-1], job, *args)
+        on_tensor(warm_up, (3,), [], [])
+        for i, g in ((0, 0), (1, 0), (1, 1), (3, 1)):
+            sort(i, [g])
+        for i, g in ((0, 1), (2, 0), (2, 1), (3, 0)):
+            cast(i, g)
+        turn(0, 0, 6, [0])
+        turn(1, 0, 7, [1])
+        on_tensor(warm_up, (2,), [], [])
+        turn(0, 1, 4, [0, 1])
+        turn(1, 1, 4, [])
+        turn(2, 0, 5, [2, 3])
+        turn(3, 1, 3, [2, 3])
+        turn(2, 1, 3, [])
+        turn(3, 0, 5, [])
+        for a, g in ((0, 0), (0, 1), (1, 0), (1, 1)):
+            for i in (2 * a, 2 * a + 1):
+                scale(i, 1, g)
+            for i in (2 * a, 2 * a + 1):
+                quant(i, 1, g)
+        early = by_two([(j, T, A, PAIR) for j, T in columns[:EARLY]])
+        for where, todo in zip((6, 7, 0, 1, 2), early):
+            on_tensor(z_first, (where, todo), x_needs(todo, (0,)), [], where, sum_keys("piece", todo))
+        on_tensor(b_turn, (4,), [], ["b turned"], 4, ["bias"])
+        scalar_jobs.append((b_out, (), ["b turned"], ["bias"]))
+        for todo in early:
+            on_tensor(z_second, (todo,), x_needs(todo, (1,)), sum_keys("sum", todo))
+            empty(todo)
+        ring = [4, 5, 6, 7, 0, 3, 1, 2]
 
-        def done(j, T, first):
-            return max(n for s, n in at.items() if s[:2] == (j, T) and s[2] <= first < s[2] + s[3])
+        first_half = (
+            by_two([(j, T, A, PAIR) for j, T in columns[EARLY:NARROW]])
+            + by_two([(j, T, B, PAIR) for j, T in columns[:NARROW]])
+            + [[(j, T, A, BANK)] for j, T in columns[NARROW:]]
+        )
+        lent = []
+        for n, todo in enumerate(first_half):
+            if n == TURN_AFTER:
+                lent = [ring.pop(0) for i in range(4)]
+                for where, (a, g) in zip(lent, ((2, 0), (2, 1), (3, 0), (3, 1))):
+                    turn(2 * a, g, where, [2 * a, 2 * a + 1])
+                    turn(2 * a + 1, g, where, [])
+            slot(todo, todo[0][0] == 2 and todo[0][1] >= OWN)
+            if lent and (n - TURN_AFTER) % 2 == 0:
+                ring.append(lent.pop(0))
+        for i in range(4, 8):
+            sort(i, [0, 1])
+        split = NARROW - TILES
+        for T in range(split):
+            max_1(T, A, PAIR)
+        vector_jobs.append((load_v, (), [], []))
+        scale(4, 2, 0)
+        scale(4, 2, 1)
+        quant(4, 2, 0)
+        scale(6, 2, 0)
+        quant(4, 2, 1)
+        scale(6, 2, 1)
+        quant(6, 2, 0)
+        max_1(0, B, PAIR)
+        quant(6, 2, 1)
+        for T in range(1, OWN + 1):
+            if T < TILES:
+                max_1(T, *((B, PAIR) if T < split else (A, BANK)))
+            max_2(T - 1, A, BANK)
+        for T in range(OWN + 1, TILES):
+            max_1(T, *((B, PAIR) if T < split else (A, BANK)))
+        for T in range(OWN, TILES):
+            max_out((2, T, A, BANK), A, BANK)
 
-        def max_1(T, first, n):
-            then(done(1, T, first + n - 1), first_out_max if (1, T, first, n) in vector_empties else first_max, T, first, n)
-
-        def max_2(T, first, n):
-            then(done(2, T, first + n - 1), second_out_max if (2, T, first, n) in vector_empties else second_max, T, first, n)
-
-        def y_tile(n):
-            r, half = tiles.pop(0)
-            place(tensor_after, n, y_mul, r, half, SUM_BANKS + half)
-            pending.append((n, r, half))
-
-        def y_empty():
-            n, r, half = pending.pop(0)
-            then(n, y_out, r, half)
-
-        for i in (4, 5):
-            then(-1, x_sort, i, [0, 1])
-        for i in (2, 3):
-            then(-1, x_out, i, 1, 1)
-        for i in (2, 3):
-            then(-1, x_quant, i, 1)
-        for i in (6, 7):
-            then(-1, x_sort, i, [0, 1])
-        for g in range(2):
-            then(turn_2, x_out, 4, 2, g)
-        then(turn_2, x_quant, 4, 0)
-        max_1(0, 0, BANK)
-        then(turn_2, x_quant, 4, 1)
-        for T in range(1, GROUP):
-            max_1(T, 0, BANK)
-            max_2(T - 1, 0, BANK)
-        then(turn_3, x_out, 6, 2, 0)
-        max_2(GROUP - 1, 0, BANK)
-        then(turn_3, x_out, 6, 2, 1)
-        then(turn_3, x_quant, 6, 0)
-        max_1(4, 0, BANK)
-        then(turn_3, x_quant, 6, 1)
-        max_2(4, 0, BANK)
-        A, B, C, D = 0, PAIR, BANK, 3 * PAIR
-        steps = [(T, 0, BANK) for T in range(GROUP + 1, TILES)] + [(T, BANK, BANK) for T in range(GROUP)]
-        steps += [(T, first, PAIR) for first in (C, D) for T in range(GROUP, TILES)][:-1]
-        mid = {1: [(A, PAIR, 0)], 2: [(A, 0)], 3: [(B, PAIR, 0)], 4: [(B, 0)], 5: [(A, 1)], 6: [(B, 1)], 11: [(C, 0), (C + P, 0)], 12: [(D, 0), (D + P, 0)], 13: ["y"]}
-        post = {4: [(A, PAIR, 1)], 5: [(B, PAIR, 1)], 9: ["y"], 10: ["y", (C, P, 0)], 11: ["y", (D, P, 0)], 12: ["y"]}
-        on_s = {10: [(1, (C + P, P, 0))], 11: [(2, (D + P, P, 0))]}
-        y_at = {9: [2], 10: [2], 11: [2], 12: [2], 13: [1]}
-
-        def do(jobs):
-            for job in jobs:
-                if job == "y":
-                    y_empty()
-                elif len(job) == 2:
-                    then(-1, h_quant, *job)
-                else:
-                    then(-1, h_weave, *job, on_vector)
-
-        for k, (T, first, n) in enumerate(steps):
-            for j in y_at.get(k, []):
-                y_tile(done(j, T, first))
-            for j, job in on_s.get(k, []):
-                place(scalar_after, done(j, T, first), h_weave, *job, on_scalar)
-            max_1(T, first, n)
-            do(mid.get(k, []))
-            if k == len(steps) - 1:
-                for row in last_rows:
-                    max_1(7, row, P)
-            max_2(T, first, n)
-            do(post.get(k, []))
-        for first in last_rows:
-            max_2(7, first, P)
-        held = tiles[:-4]
-        x_turn([2, 3], 1, 7)
-        run(vector_after, -1)
-        for n, todo in enumerate(slots):
-            z_bank((4 + n) % SUM_BANKS, *todo)
-            run(tensor_after, n)
-            for s in todo:
-                if s not in vector_empties:
-                    piece_out(*s)
-            run(scalar_after, n)
-            run(vector_after, n)
-
-        final = tiles[-4:]
-        last = len(slots) - 1
-        free_banks = [SUM_BANKS + held[0][1], (4 + last + 1) % 6, SUM_BANKS + 1 - held[0][1]] + [(4 + last + i) % 6 for i in (2, 3, 5, 4, 6)]
-        free_banks = free_banks + free_banks
-        opened = final[: 0]
-        for first in (C, C + P):
-            h_weave(first, P, 1, on_scalar)
-        quant_after = {0: [C], 1: [C + P], 4: [D], 5: [D + P]}
-        for i, tile in enumerate(held):
-            y_mul(*tile, free_banks.pop(0))
-            if i == len(held) - 1:
-                for t in opened:
-                    y_open(*t, free_banks.pop(0))
-            y_out(*tile, nc.scalar if i == len(held) - 1 else nc.sync)
-            if i == 2:
-                for first in last_rows:
-                    h_weave(first, P, 1, on_scalar)
-            for first in quant_after.get(i, []):
-                h_quant(first, 1)
-        for tile in final:
-            if tile in opened:
-                y_pass(*tile, 1)
+        for T in range(WIDE):
+            for j in range(PIECES):
+                slot([(j, T, C, BANK)], j == 2 and T in ())
+            if T < 4:
+                weave((A, B)[T % 2], PAIR, T // 2, vector_jobs)
+            max_1(T, C, BANK)
+            if T < 4:
+                h_q((A, B)[T % 2], PAIR, T // 2)
+            if T in ():
+                max_out((2, T, C, BANK), C, BANK)
             else:
-                y_mul(*tile, free_banks.pop(0))
-        for r, n in final[:-1]:
-            y_out(r, n, (nc.sync, nc.scalar)[n])
-        y_out(*final[-1], nc.scalar, 0, PAIR)
-        y_out(*final[-1], nc.sync, PAIR, BANK)
+                max_2(T, C, BANK)
+        high = [(j, T) for T in range(WIDE, TILES) for j in range(PIECES)]
+        third = by_two([(j, T, C, PAIR) for j, T in high])
+        for n, todo in enumerate(third):
+            slot(todo)
+            if n in (1, 3, 5):
+                y_slot()
+            if n in {}:
+                weave({}[n], P, 0, scalar_jobs)
+        fourth = [(j, T, D, PAIR) for j, T in ((0, 4), (1, 4), (2, 4), (0, 5), (1, 5), (2, 5), (0, 6), (0, 7))]
+        for n, todo in enumerate(by_two(fourth)):
+            slot(todo)
+            if n in (0, 1, 2):
+                y_slot()
+            if n in {2: C, 3: C + P}:
+                weave({2: C, 3: C + P}[n], P, 1, scalar_jobs)
+        for j in (1, 2):
+            for T in (6, 7):
+                slot([(j, T, D, PAIR)], by_vector=True)
+        max_1(4, C, PAIR)
+        store()
+        max_2(4, C, PAIR)
+        max_1(5, C, PAIR)
+        store()
+        max_2(5, C, PAIR)
+        weave(C, PAIR, 0, vector_jobs)
+        max_1(6, C, PAIR)
+        h_q(C, PAIR, 0)
+        max_2(6, C, PAIR)
+        max_1(7, C, PAIR)
+        weave(D, PAIR, 0, vector_jobs)
+        max_2(7, C, PAIR)
+        store()
+        h_q(D, PAIR, 0)
+        store()
+        max_1(4, D, PAIR)
+        store()
+        max_2(4, D, PAIR)
+        max_1(5, D, PAIR)
+        store()
+        max_2(5, D, PAIR)
+        h_q(C, P, 1)
+        max_1_out((1, 6, D, PAIR))
+        max_1_out((1, 7, D, PAIR))
+        max_out((2, 6, D, PAIR), D, PAIR)
+        max_out((2, 7, D, PAIR), D, P)
+        max_out((2, 7, D, PAIR), D + P, P)
+        h_q(C + P, P, 1)
+        for first in (D, D + P):
+            weave(first, P, 1, scalar_jobs)
+        left = len(tiles)
+        for n in range(left):
+            y_slot()
+            if n == left - 6:
+                h_q(D, P, 1)
+            if n == left - 5:
+                h_q(D + P, P, 1)
+            store((nc.sync, nc.scalar)[n % 2] if n >= left - 5 else nc.sync, halves=(n == left - 1))
+
+
+        given = set()
+        queues = (tensor_jobs, scalar_jobs, vector_jobs)
+        while any(queues):
+            moved = False
+            for jobs in queues:
+                while jobs and all(key in given for key in jobs[0][2]):
+                    job, args, needs, gives = jobs.pop(0)
+                    job(*args)
+                    for key in gives:
+                        given.add(key)
+                    moved = True
+            assert moved

@@ -26,9 +26,9 @@ GROUP = 4
 EARLY = 10
 FIRST = 4
 NARROW = 14
-TURN_AFTER = 6
+TURN_AFTER = 5
 WIDE = 4
-OWN = 8
+OWN = 6
 A, B, C, D = 0, PAIR, 2 * PAIR, 3 * PAIR
 
 
@@ -94,18 +94,17 @@ def tile_maxout_then_linear_f7_kernel(tc, x_bytes, x_scale, w_words, w_scales, b
         for i in range(4):
             nc.sync.dma_start(out=x_tile[i][:], in_=x_bytes[i * P : (i + 1) * P, :])
         load_w_scales(0)
-        load_w(0, 0, 0, FIRST)
-        load_w(0, 0, FIRST, EARLY)
+        for g in range(2):
+            load_w(0, g)
         nc.sync.dma_start(out=b_rows[0:TILES], in_=b.rearrange("j (t p) -> t j p", p=P))
-        load_w(0, 1)
-        load_w_scales(1)
-        load_w(1, 0)
-        load_w(1, 1)
         load_pair(2)
+        load_w_scales(1)
+        for g in range(2):
+            load_w(1, g)
         load_pair(3)
         load_w_scales(2)
-        load_w(2, 0)
-        load_w(2, 1)
+        for g in range(2):
+            load_w(2, g)
 
         def load_v():
             clear(v_sc)
@@ -119,7 +118,10 @@ def tile_maxout_then_linear_f7_kernel(tc, x_bytes, x_scale, w_words, w_scales, b
         h_codes = [keep.tile([P, 2, PAIR], U32, name="h_codes%d" % i, align_bytes=256) for i in range(4)]
         h_sc = [keep.tile([P, 2, PAIR], U8, name="h_sc%d" % i, align_bytes=256) for i in range(4)]
 
-        words, turned, grouped = {}, {}, {}
+        words, turned, planes, grouped = {}, {}, {}, {}
+
+        def interleave(copy, dst, src):
+            copy(out=dst.rearrange("p (c i) t -> p c t i", i=4), in_=src.rearrange("p t (c i) -> p c t i", i=4))
 
         def x_row(i, passes):
             if i >= 4:
@@ -164,6 +166,18 @@ def tile_maxout_then_linear_f7_kernel(tc, x_bytes, x_scale, w_words, w_scales, b
                 in1=scale_cols[:, g].rearrange("p (u e) -> p u e", u=2).unsqueeze(1).to_broadcast([P, rows * P, 2, 2]),
                 op=ALU.mult,
             )
+
+        def x_planes(a, g):
+            t = keep.tile([P, 4, PAIR], BF16, name="planes%d_%d" % (a, g), align_bytes=64)
+            planes[(a, g)] = t
+            source = turned[(2 * a, g)][:].bitcast(BF16).rearrange("p (u m e) -> p u e m", u=2, e=2)
+            for k in range(4):
+                nc.scalar.activation(out=t[:, k], in_=source[:, k // 2, k % 2], func=ACT.Copy, scale=scale_cols[:, g, k : k + 1])
+
+        def x_weave(a, g):
+            t = stage.tile([P, PAIR, 4], BF16, name="grouped", align_bytes=64)
+            grouped[(2 * a, g)] = t
+            interleave(nc.vector.tensor_copy, t[:], planes[(a, g)][:])
 
         def x_quant(i, g):
             t = grouped[(i, g)]
@@ -287,7 +301,7 @@ def tile_maxout_then_linear_f7_kernel(tc, x_bytes, x_scale, w_words, w_scales, b
             lo = first - key[0] * PAIR
             t = stage.tile([P, n, 4], BF16, name="woven", align_bytes=64)
             woven[(first, g)] = t
-            copy(out=t[:].rearrange("p (c i) t -> p c t i", i=4), in_=folds[key][:, :, lo : lo + n].rearrange("p t (c i) -> p c t i", i=4))
+            interleave(copy, t[:], folds[key][:, :, lo : lo + n])
 
         def h_quant(first, g):
             t = woven[(first, g)]
@@ -375,6 +389,12 @@ def tile_maxout_then_linear_f7_kernel(tc, x_bytes, x_scale, w_words, w_scales, b
         def scale(i, rows, g):
             vector_jobs.append((x_out, (i, rows, g), named("turned", i * P, rows * P, g), named("grouped", i * P, rows * P, g)))
 
+        def scale_by_planes(a, g):
+            scalar_jobs.append((x_planes, (a, g), named("turned", a * PAIR, PAIR, g), named("grouped", a * PAIR, PAIR, g)))
+
+        def regroup(a, g):
+            vector_jobs.append((x_weave, (a, g), named("grouped", a * PAIR, PAIR, g), []))
+
         def quant(i, rows, g):
             vector_jobs.append((x_quant, (i, g), [], named("codes", i * P, rows * P, g)))
 
@@ -416,22 +436,31 @@ def tile_maxout_then_linear_f7_kernel(tc, x_bytes, x_scale, w_words, w_scales, b
         on_tensor(warm_up, (3,), [], [])
         for i, g in ((0, 0), (1, 0), (1, 1), (3, 1)):
             sort(i, [g])
-        for i, g in ((0, 1), (2, 0), (2, 1), (3, 0)):
+        for i, g in ((0, 1), (2, 1), (2, 0), (3, 0)):
             cast(i, g)
         turn(0, 0, 6, [0])
         turn(1, 0, 7, [1])
-        on_tensor(warm_up, (2,), [], [])
+        on_tensor(warm_up, (1,), [], [])
         turn(0, 1, 4, [0, 1])
         turn(1, 1, 4, [])
-        turn(2, 0, 5, [2, 3])
         turn(3, 1, 3, [2, 3])
         turn(2, 1, 3, [])
+        on_tensor(warm_up, (1,), [], [])
+        turn(2, 0, 5, [2, 3])
         turn(3, 0, 5, [])
-        for a, g in ((0, 0), (0, 1), (1, 0), (1, 1)):
-            for i in (2 * a, 2 * a + 1):
+        for g in range(2):
+            for i in (0, 1):
                 scale(i, 1, g)
-            for i in (2 * a, 2 * a + 1):
+            for i in (0, 1):
                 quant(i, 1, g)
+        for g in (1, 0):
+            scale_by_planes(1, g)
+        regroup(1, 1)
+        sort(4, [0, 1])
+        quant(2, 2, 1)
+        regroup(1, 0)
+        sort(5, [0, 1])
+        quant(2, 2, 0)
         early = by_two([(j, T, A, PAIR) for j, T in columns[:EARLY]])
         for where, todo in zip((6, 7, 0, 1, 2), early):
             on_tensor(z_first, (where, todo), x_needs(todo, (0,)), [], where, sum_keys("piece", todo))
@@ -440,7 +469,7 @@ def tile_maxout_then_linear_f7_kernel(tc, x_bytes, x_scale, w_words, w_scales, b
         for todo in early:
             on_tensor(z_second, (todo,), x_needs(todo, (1,)), sum_keys("sum", todo))
             empty(todo)
-        ring = [4, 5, 6, 7, 0, 3, 1, 2]
+        ring = [3, 4, 5, 6, 7, 0, 1, 2]
 
         first_half = (
             by_two([(j, T, A, PAIR) for j, T in columns[EARLY:NARROW]])
@@ -457,11 +486,8 @@ def tile_maxout_then_linear_f7_kernel(tc, x_bytes, x_scale, w_words, w_scales, b
             slot(todo, todo[0][0] == 2 and todo[0][1] >= OWN)
             if lent and (n - TURN_AFTER) % 2 == 0:
                 ring.append(lent.pop(0))
-        for i in range(4, 8):
+        for i in range(6, 8):
             sort(i, [0, 1])
-        split = NARROW - TILES
-        for T in range(split):
-            max_1(T, A, PAIR)
         vector_jobs.append((load_v, (), [], []))
         scale(4, 2, 0)
         scale(4, 2, 1)
@@ -470,14 +496,14 @@ def tile_maxout_then_linear_f7_kernel(tc, x_bytes, x_scale, w_words, w_scales, b
         quant(4, 2, 1)
         scale(6, 2, 1)
         quant(6, 2, 0)
-        max_1(0, B, PAIR)
+        max_1(0, A, BANK)
         quant(6, 2, 1)
         for T in range(1, OWN + 1):
             if T < TILES:
-                max_1(T, *((B, PAIR) if T < split else (A, BANK)))
+                max_1(T, A, BANK)
             max_2(T - 1, A, BANK)
         for T in range(OWN + 1, TILES):
-            max_1(T, *((B, PAIR) if T < split else (A, BANK)))
+            max_1(T, A, BANK)
         for T in range(OWN, TILES):
             max_out((2, T, A, BANK), A, BANK)
 
@@ -497,17 +523,19 @@ def tile_maxout_then_linear_f7_kernel(tc, x_bytes, x_scale, w_words, w_scales, b
         third = by_two([(j, T, C, PAIR) for j, T in high])
         for n, todo in enumerate(third):
             slot(todo)
-            if n in (1, 3, 5):
+            if n in (1, 3):
                 y_slot()
             if n in {}:
-                weave({}[n], P, 0, scalar_jobs)
+                weave(*{}[n], scalar_jobs)
         fourth = [(j, T, D, PAIR) for j, T in ((0, 4), (1, 4), (2, 4), (0, 5), (1, 5), (2, 5), (0, 6), (0, 7))]
         for n, todo in enumerate(by_two(fourth)):
             slot(todo)
             if n in (0, 1, 2):
                 y_slot()
-            if n in {2: C, 3: C + P}:
-                weave({2: C, 3: C + P}[n], P, 1, scalar_jobs)
+            if n in {}:
+                weave(*{}[n], scalar_jobs)
+        for first in (C, C + P):
+            weave(first, P, 1, scalar_jobs)
         for j in (1, 2):
             for T in (6, 7):
                 slot([(j, T, D, PAIR)], by_vector=True)
@@ -517,34 +545,33 @@ def tile_maxout_then_linear_f7_kernel(tc, x_bytes, x_scale, w_words, w_scales, b
         max_1(5, C, PAIR)
         store()
         max_2(5, C, PAIR)
-        weave(C, PAIR, 0, vector_jobs)
         max_1(6, C, PAIR)
-        h_q(C, PAIR, 0)
+        weave(C, PAIR, 0, vector_jobs)
         max_2(6, C, PAIR)
         max_1(7, C, PAIR)
-        weave(D, PAIR, 0, vector_jobs)
+        h_q(C, PAIR, 0)
         max_2(7, C, PAIR)
-        store()
-        h_q(D, PAIR, 0)
+        weave(D, PAIR, 0, vector_jobs)
         store()
         max_1(4, D, PAIR)
-        store()
+        h_q(D, PAIR, 0)
         max_2(4, D, PAIR)
+        store()
         max_1(5, D, PAIR)
         store()
         max_2(5, D, PAIR)
-        h_q(C, P, 1)
         max_1_out((1, 6, D, PAIR))
         max_1_out((1, 7, D, PAIR))
         max_out((2, 6, D, PAIR), D, PAIR)
         max_out((2, 7, D, PAIR), D, P)
         max_out((2, 7, D, PAIR), D + P, P)
-        h_q(C + P, P, 1)
         for first in (D, D + P):
             weave(first, P, 1, scalar_jobs)
         left = len(tiles)
         for n in range(left):
             y_slot()
+            if n in (0, 0 + 1):
+                h_q(C + (n - 0) * P, P, 1)
             if n == left - 6:
                 h_q(D, P, 1)
             if n == left - 5:

@@ -26,9 +26,9 @@ GROUP = 4
 EARLY = 10
 FIRST = 4
 NARROW = 14
-TURN_AFTER = 5
+TURN_AFTER = 3
 WIDE = 4
-OWN = 6
+OWN = (0, 2, 7)
 A, B, C, D = 0, PAIR, 2 * PAIR, 3 * PAIR
 
 
@@ -82,7 +82,7 @@ def tile_maxout_then_linear_f7_kernel(tc, x_bytes, x_scale, w_words, w_scales, b
         def load_w_scales(part):
             load_scales(w_sc[part], w_scales, parts[part][0] * P, parts[part][1] * P)
 
-        nc.scalar.dma_start(out=scale_cols[:], in_=x_scale.rearrange("o (g p t) -> p (o g) t", g=2, t=4))
+        nc.sync.dma_start(out=scale_cols[:], in_=x_scale.rearrange("o (g p t) -> p (o g) t", g=2, t=4))
         make_identity(nc, ident[:])
         nc.vector.memset(zeros[:], 0.0)
         clear(w_sc[0])
@@ -105,13 +105,13 @@ def tile_maxout_then_linear_f7_kernel(tc, x_bytes, x_scale, w_words, w_scales, b
         load_w_scales(2)
         for g in range(2):
             load_w(2, g)
+        nc.sync.dma_start(out=c_all[:], in_=c.partition_broadcast(P))
 
         def load_v():
             clear(v_sc)
             load_scales(v_sc, v_scales, 0, N)
             for g in range(2):
                 nc.sync.dma_start(out=v_w[:, g].bitcast(I32), in_=v_words[g].rearrange("p n t -> p (n t)").bitcast(I32))
-            nc.sync.dma_start(out=c_all[:], in_=c.partition_broadcast(P))
 
         x_codes = [keep.tile([P, 2, BANK], U32, name="x_codes%d" % i, align_bytes=256) for i in range(2)]
         x_sc = [keep.tile([P, 2, BANK], U8, name="x_sc%d" % i, align_bytes=256) for i in range(2)]
@@ -337,6 +337,10 @@ def tile_maxout_then_linear_f7_kernel(tc, x_bytes, x_scale, w_words, w_scales, b
             for i in range(times):
                 nc.tensor.matmul(t[:], lhsT=zeros[:, 0:P], rhs=zeros[:], start=True, stop=True)
 
+        def warm_up_on_landing():
+            t = bank(0)
+            nc.tensor.matmul(t[:, 0:P], lhsT=scale_cols[:, 0, 0:1].to_broadcast([P, P]), rhs=ident[:], start=True, stop=True)
+
         tensor_jobs, scalar_jobs, vector_jobs = [], [], []
         emptied_by = {}
 
@@ -433,12 +437,14 @@ def tile_maxout_then_linear_f7_kernel(tc, x_bytes, x_scale, w_words, w_scales, b
         pending = []
         columns = [(col // TILES, col % TILES) for col in range(PIECES * TILES)]
 
-        on_tensor(warm_up, (3,), [], [])
+        on_tensor(warm_up, (2,), [], [])
+        on_tensor(warm_up_on_landing, (), [], [])
         for i, g in ((0, 0), (1, 0), (1, 1), (3, 1)):
             sort(i, [g])
         for i, g in ((0, 1), (2, 1), (2, 0), (3, 0)):
             cast(i, g)
         turn(0, 0, 6, [0])
+        on_tensor(warm_up, (1,), [], [])
         turn(1, 0, 7, [1])
         on_tensor(warm_up, (1,), [], [])
         turn(0, 1, 4, [0, 1])
@@ -478,12 +484,13 @@ def tile_maxout_then_linear_f7_kernel(tc, x_bytes, x_scale, w_words, w_scales, b
         )
         lent = []
         for n, todo in enumerate(first_half):
-            if n == TURN_AFTER:
-                lent = [ring.pop(0) for i in range(4)]
-                for where, (a, g) in zip(lent, ((2, 0), (2, 1), (3, 0), (3, 1))):
-                    turn(2 * a, g, where, [2 * a, 2 * a + 1])
-                    turn(2 * a + 1, g, where, [])
-            slot(todo, todo[0][0] == 2 and todo[0][1] >= OWN)
+            if n in (TURN_AFTER, TURN_AFTER + 3):
+                a = 2 if n == TURN_AFTER else 3
+                for g in range(2):
+                    lent.append(ring.pop(0))
+                    turn(2 * a, g, lent[-1], [2 * a, 2 * a + 1])
+                    turn(2 * a + 1, g, lent[-1], [])
+            slot(todo, todo[0][0] == 2 and todo[0][1] in OWN)
             if lent and (n - TURN_AFTER) % 2 == 0:
                 ring.append(lent.pop(0))
         for i in range(6, 8):
@@ -498,14 +505,13 @@ def tile_maxout_then_linear_f7_kernel(tc, x_bytes, x_scale, w_words, w_scales, b
         quant(6, 2, 0)
         max_1(0, A, BANK)
         quant(6, 2, 1)
-        for T in range(1, OWN + 1):
-            if T < TILES:
-                max_1(T, A, BANK)
-            max_2(T - 1, A, BANK)
-        for T in range(OWN + 1, TILES):
-            max_1(T, A, BANK)
-        for T in range(OWN, TILES):
-            max_out((2, T, A, BANK), A, BANK)
+        for T in range(TILES):
+            if T + 1 < TILES:
+                max_1(T + 1, A, BANK)
+            if T in OWN:
+                max_out((2, T, A, BANK), A, BANK)
+            else:
+                max_2(T, A, BANK)
 
         for T in range(WIDE):
             for j in range(PIECES):

from contextlib import ExitStack

import concourse.mybir as mybir
from concourse.masks import make_identity

M, K, F, PIECES, N = 1024, 1024, 1024, 3, 1024
FLOPS = 2 * M * K * PIECES * F + 2 * M * F * N

F32 = mybir.dt.float32
BF16 = mybir.dt.bfloat16
I32 = mybir.dt.int32
U32 = mybir.dt.uint32
U8 = mybir.dt.uint8
E4M3 = mybir.dt.float8_e4m3fn
FP8X4 = mybir.dt.float8_e4m3fn_x4
FP4X4 = mybir.dt.float4_e2m1fn_x4
ALU = mybir.AluOpType
ACT = mybir.ActivationFunctionType

P = 128
PASS = 512
BANK = 512
PAIR = 2 * P
TILES = F // P
GROUP = 4
EARLY = 10
FIRST = 4
NARROW = 14
TURN_AFTER = 3
WIDE = 4
OWN = (0, 2, 7)
A, B, C, D = 0, PAIR, 2 * PAIR, 3 * PAIR


def tile_maxout_then_linear_f7_kernel(tc, x_bytes, x_scale, w_words, w_scales, b, v_words, v_scales, c, out):
    nc = tc.nc
    with ExitStack() as ctx:
        keep = ctx.enter_context(tc.tile_pool(name="keep", bufs=1))
        stage = ctx.enter_context(tc.tile_pool(name="stage", bufs=4))
        psum = ctx.enter_context(tc.psum_pool(name="psum", bufs=1))
        ctx.enter_context(tc.manual_schedule())

        def bank(i):
            t = psum.tile([P, BANK], F32, name="bank%d" % i)
            return t

        parts = ((0, EARLY), (EARLY, 2 * TILES), (2 * TILES, PIECES * TILES))
        scale_cols = keep.tile([P, 2, 4], F32, name="scale_cols")
        w_w = [keep.tile([P, 2, (hi - lo) * 2 * P], U8, name="w_w%d" % lo, align_bytes=256) for lo, hi in parts]
        w_sc = [keep.tile([P, 2, (hi - lo) * P], U8, name="w_sc%d" % lo, align_bytes=256) for lo, hi in parts]
        v_w = keep.tile([P, 2, 4 * N], U8, name="v_w", align_bytes=256)
        v_sc = keep.tile([P, 2, N], U8, name="v_sc", align_bytes=256)
        ident = keep.tile([P, P], F32, name="ident")
        pick = keep.tile([P, TILES], BF16, name="pick")
        one = keep.tile([P, 1], F32, name="one")
        b_rows = keep.tile([P, PIECES, P], BF16, name="b_rows")
        bias = keep.tile([P, PIECES * TILES], F32, name="bias")
        x_tile = [keep.tile([P, K], U8, name="x_tile%d" % i, align_bytes=64) for i in range(4)]
        x_pair = [keep.tile([P, 2, K], U8, name="x_pair%d" % a, align_bytes=64) for a in (2, 3)]
        c_all = keep.tile([P, N], BF16, name="c_all")
        zeros = keep.tile([P, BANK], BF16, name="zeros")

        def clear(tile):
            nc.vector.memset(tile[:].rearrange("p g n -> p (g n)").bitcast(U32), 0)

        def load_pair(a):
            nc.sync.dma_start(out=x_pair[a - 2][:], in_=x_bytes[a * PAIR : (a + 1) * PAIR, :].rearrange("(r p) k -> p r k", p=P))

        def load_w(part, g, lo=None, hi=None):
            base = parts[part][0]
            if lo is None:
                lo, hi = parts[part]
            nc.sync.dma_start(
                out=w_w[part][:, g, (lo - base) * 2 * P : (hi - base) * 2 * P].bitcast(I32),
                in_=w_words[g][:, lo * 2 * P : hi * 2 * P].bitcast(I32),
            )

        def load_scales(tile, scales, lo, hi):
            for i in range(4):
                nc.sync.dma_start(out=tile[i:P:32].bitcast(I32), in_=scales[:, i:16:4, lo:hi].rearrange("g q n -> q g n").bitcast(I32))

        def load_w_scales(part):
            load_scales(w_sc[part], w_scales, parts[part][0] * P, parts[part][1] * P)

        nc.sync.dma_start(out=scale_cols[:], in_=x_scale.rearrange("o (g p t) -> p (o g) t", g=2, t=4))
        make_identity(nc, ident[:])
        nc.vector.memset(zeros[:], 0.0)
        clear(w_sc[0])
        nc.vector.memset(one[:], 1.0)
        nc.vector.memset(b_rows[:], 0.0)
        for tile in w_sc[1:]:
            clear(tile)
        nc.scalar.activation(out=pick[:], in_=ident[:, 0:TILES], func=ACT.Identity)
        for i in range(4):
            nc.sync.dma_start(out=x_tile[i][:], in_=x_bytes[i * P : (i + 1) * P, :])
        load_w_scales(0)
        for g in range(2):
            load_w(0, g)
        nc.sync.dma_start(out=b_rows[0:TILES], in_=b.rearrange("j (t p) -> t j p", p=P))
        load_pair(2)
        load_w_scales(1)
        for g in range(2):
            load_w(1, g)
        load_pair(3)
        load_w_scales(2)
        for g in range(2):
            load_w(2, g)
        nc.sync.dma_start(out=c_all[:], in_=c.partition_broadcast(P))

        def load_v():
            clear(v_sc)
            load_scales(v_sc, v_scales, 0, N)
            for g in range(2):
                nc.sync.dma_start(out=v_w[:, g].bitcast(I32), in_=v_words[g].rearrange("p n t -> p (n t)").bitcast(I32))

        x_codes = [keep.tile([P, 2, BANK], U32, name="x_codes%d" % i, align_bytes=256) for i in range(2)]
        x_sc = [keep.tile([P, 2, BANK], U8, name="x_sc%d" % i, align_bytes=256) for i in range(2)]
        h_codes = [keep.tile([P, 2, PAIR], U32, name="h_codes%d" % i, align_bytes=256) for i in range(4)]
        h_sc = [keep.tile([P, 2, PAIR], U8, name="h_sc%d" % i, align_bytes=256) for i in range(4)]

        words, turned, planes, grouped = {}, {}, {}, {}

        def interleave(copy, dst, src):
            copy(out=dst.rearrange("p (c i) t -> p c t i", i=4), in_=src.rearrange("p t (c i) -> p c t i", i=4))

        def x_row(i, passes):
            if i >= 4:
                return x_pair[i // 2 - 2][:, i % 2, passes[0] * PASS : (passes[-1] + 1) * PASS].bitcast(E4M3)
            return x_tile[i][:, passes[0] * PASS : (passes[-1] + 1) * PASS].bitcast(E4M3)

        def x_cast(i, g):
            t = keep.tile([P, PASS], BF16, name="plain%d_%d" % (i, g), align_bytes=64)
            nc.scalar.copy(out=t[:], in_=x_row(i, [g]))
            for u in range(2):
                words[(i, g, u)] = t[:].bitcast(F32)[:, u:PAIR:2]

        def x_sort(i, passes):
            t = keep.tile([P, 2, len(passes) * P, 2], BF16, name="sorted%d_%d" % (i, passes[0]), align_bytes=64)
            nc.vector.tensor_scalar(
                out=t[:].rearrange("m u w e -> m w u e"),
                in0=x_row(i, passes).rearrange("m (w u e) -> m w u e", u=2, e=2),
                scalar1=one[:],
                scalar2=None,
                op0=ALU.mult,
            )
            for n, g in enumerate(passes):
                for u in range(2):
                    words[(i, g, u)] = t[:].rearrange("m u w e -> m u (w e)").bitcast(F32)[:, u, n * P : (n + 1) * P]

        def x_turn(i, g, where):
            if (where, g, i // 2) not in turned:
                turned[(where, g, i // 2)] = bank(where)
            t = turned[(where, g, i // 2)]
            turned[(i, g)] = t
            for u in range(2):
                at = u * PAIR + (i % 2) * P
                nc.tensor.transpose(t[:, at : at + P], words[(i, g, u)], ident[:])

        def x_out(i, rows, g):
            t = stage.tile([P, rows * P, 4], BF16, name="grouped", align_bytes=64)
            grouped[(i, g)] = t
            lo = (i % 2) * P
            nc.vector.tensor_tensor(
                out=t[:].rearrange("p m (u e) -> p m u e", u=2),
                in0=turned[(i, g)][:].bitcast(BF16).rearrange("p (u m e) -> p m u e", u=2, e=2)[:, lo : lo + rows * P],
                in1=scale_cols[:, g].rearrange("p (u e) -> p u e", u=2).unsqueeze(1).to_broadcast([P, rows * P, 2, 2]),
                op=ALU.mult,
            )

        def x_planes(a, g):
            t = keep.tile([P, 4, PAIR], BF16, name="planes%d_%d" % (a, g), align_bytes=64)
            planes[(a, g)] = t
            source = turned[(2 * a, g)][:].bitcast(BF16).rearrange("p (u m e) -> p u e m", u=2, e=2)
            for k in range(4):
                nc.scalar.activation(out=t[:, k], in_=source[:, k // 2, k % 2], func=ACT.Copy, scale=scale_cols[:, g, k : k + 1])

        def x_weave(a, g):
            t = stage.tile([P, PAIR, 4], BF16, name="grouped", align_bytes=64)
            grouped[(2 * a, g)] = t
            interleave(nc.vector.tensor_copy, t[:], planes[(a, g)][:])

        def x_quant(i, g):
            t = grouped[(i, g)]
            cols = slice((i % 4) * P, (i % 4) * P + t.shape[1])
            nc.vector.quantize_mx(
                out=x_codes[i // 4][:, g, cols].bitcast(FP8X4), scales=x_sc[i // 4][:, g, cols], in_=t[:].rearrange("p m t -> p (m t)")
            )

        sums, pieces, upper, folds, woven = {}, {}, {}, {}, {}

        def z_pass(s, g, start, stop):
            j, T, first, n = s
            col = TILES * j + T
            part = [lo <= col < hi for lo, hi in parts].index(True)
            col -= parts[part][0]
            half, cols = first // BANK, slice(first % BANK, first % BANK + n)
            nc.tensor.matmul_mx(
                out=sums[s],
                lhsT=w_w[part][:, g, col * 2 * P : (col + 1) * 2 * P].bitcast(FP4X4),
                lhsT_scale=w_sc[part][:, g, col * P : (col + 1) * P],
                rhs=x_codes[half][:, g, cols].bitcast(FP8X4),
                rhs_scale=x_sc[half][:, g, cols],
                start=start,
                stop=stop,
            )

        def z_open(where, todo):
            t = bank(where)
            for n, s in enumerate(todo):
                sums[s] = t[:, n * PAIR : n * PAIR + s[3]]

        def z_bank(where, todo):
            z_open(where, todo)
            for s in todo:
                for g in range(2):
                    z_pass(s, g, g == 0, g == 1)

        def z_first(where, todo):
            z_open(where, todo)
            for n, s in enumerate(todo):
                z_pass(s, 0, n == 0, False)

        def z_second(todo):
            for n, s in enumerate(todo):
                z_pass(s, 1, False, n == len(todo) - 1)

        def b_turn(where):
            t = bank(where)
            turned["b"] = t
            for j in range(PIECES):
                nc.tensor.matmul(t[:, j * TILES : (j + 1) * TILES], lhsT=b_rows[:, j], rhs=pick[:], start=True, stop=True)

        def b_out():
            nc.scalar.copy(out=bias[:], in_=turned["b"][:, 0 : PIECES * TILES])

        def of_half(store, name, T, first, n):
            half, lo = first // BANK, first % BANK
            if (name, T, half) not in store:
                t = keep.tile([P, BANK], BF16, name="%s_%d_%d" % (name, T, half), align_bytes=64)
                store[(name, T, half)] = t
            return store[(name, T, half)][:, lo : lo + n]

        def piece(j, T, first, n):
            return of_half(pieces, "piece%d" % j, T, first, n)

        def piece_out(j, T, first, n):
            col = TILES * j + T
            nc.scalar.activation(out=piece(j, T, first, n), in_=sums[(j, T, first, n)], func=ACT.Identity, bias=bias[:, col : col + 1])

        def first_max(T, first, n):
            nc.vector.tensor_tensor(out=of_half(upper, "upper", T, first, n), in0=piece(0, T, first, n), in1=piece(1, T, first, n), op=ALU.max)

        def fold_key(first, g):
            return (first // PAIR, g) if first >= BANK and g == 1 else (first // BANK * 2, g)

        def fold(h, T, first, n):
            g, q = T // GROUP, T % GROUP
            width = PAIR if first >= BANK and g == 1 else BANK
            for lo in range(first, first + n, width):
                key = fold_key(lo, g)
                if key not in folds:
                    t = keep.tile([P, 4, width], BF16, name="fold%d_%d" % key, align_bytes=64)
                    folds[key] = t
                m = min(n, width)
                at = lo - key[0] * PAIR
                nc.sync.dma_start(out=folds[key][32 * q : 32 * q + 32, :, at : at + m], in_=h[:, lo - first : lo - first + m])

        def second_max(T, first, n):
            h = stage.tile([P, n], BF16, name="h", align_bytes=64, bufs=8)
            nc.vector.tensor_tensor(out=h[:], in0=piece(2, T, first, n), in1=of_half(upper, "upper", T, first, n), op=ALU.max)
            fold(h, T, first, n)

        def first_out_max(s):
            j, T, first, n = s
            col = TILES * j + T
            nc.vector.scalar_tensor_tensor(
                out=of_half(upper, "upper", T, first, n),
                in0=sums[s],
                scalar=bias[:, col : col + 1],
                in1=piece(0, T, first, n),
                op0=ALU.add,
                op1=ALU.max,
            )

        def last_max(s, first, n):
            T = s[1]
            col = TILES * 2 + T
            h = stage.tile([P, n], BF16, name="h", align_bytes=64, bufs=8)
            nc.vector.scalar_tensor_tensor(
                out=h[:],
                in0=sums[s][:, first - s[2] : first - s[2] + n],
                scalar=bias[:, col : col + 1],
                in1=of_half(upper, "upper", T, first, n),
                op0=ALU.add,
                op1=ALU.max,
            )
            fold(h, T, first, n)

        def h_weave(first, n, g, copy):
            key = fold_key(first, g)
            lo = first - key[0] * PAIR
            t = stage.tile([P, n, 4], BF16, name="woven", align_bytes=64)
            woven[(first, g)] = t
            interleave(copy, t[:], folds[key][:, :, lo : lo + n])

        def h_quant(first, g):
            t = woven[(first, g)]
            a, cols = first // PAIR, slice(first % PAIR, first % PAIR + t.shape[1])
            nc.vector.quantize_mx(
                out=h_codes[a][:, g, cols].bitcast(FP8X4), scales=h_sc[a][:, g, cols], in_=t[:].rearrange("p m t -> p (m t)")
            )

        y_sums = {}

        def y_mul(r, n, where):
            y_sums[(r, n)] = bank(where)
            rows = slice((r % 2) * P, (r % 2 + 1) * P)
            for g in range(2):
                nc.tensor.matmul_mx(
                    out=y_sums[(r, n)][:],
                    lhsT=h_codes[r // 2][:, g, rows].bitcast(FP8X4),
                    lhsT_scale=h_sc[r // 2][:, g, rows],
                    rhs=v_w[:, g, 4 * n * BANK : 4 * (n + 1) * BANK].bitcast(FP8X4),
                    rhs_scale=v_sc[:, g, n * BANK : (n + 1) * BANK],
                    start=(g == 0),
                    stop=(g == 1),
                )

        def y_out(r, n, queue, lo, hi):
            o = stage.tile([P, hi - lo], F32, name="y", bufs=8)
            cols = slice(n * BANK + lo, n * BANK + hi)
            nc.vector.tensor_tensor(out=o[:], in0=y_sums[(r, n)][:, lo:hi], in1=c_all[:, cols], op=ALU.add)
            queue.dma_start(out=out[r * P : (r + 1) * P, cols], in_=o[:])

        def warm_up(times):
            t = bank(0)
            for i in range(times):
                nc.tensor.matmul(t[:], lhsT=zeros[:, 0:P], rhs=zeros[:], start=True, stop=True)

        def warm_up_on_landing():
            t = bank(0)
            nc.tensor.matmul(t[:, 0:P], lhsT=scale_cols[:, 0, 0:1].to_broadcast([P, P]), rhs=ident[:], start=True, stop=True)

        tensor_jobs, scalar_jobs, vector_jobs = [], [], []
        emptied_by = {}

        def rows_of(first, n):
            return range(first // P, (first + n) // P)

        def named(name, first, n, *more):
            return [(name, r) + more for r in rows_of(first, n)]

        def on_tensor(job, args, needs, gives, where=None, readers=None):
            if readers is not None:
                needs = needs + emptied_by.get(where, [])
                emptied_by[where] = readers
            tensor_jobs.append((job, args, needs, gives))

        def x_needs(todo, passes):
            return [key for s in todo for g in passes for key in named("codes", s[2], s[3], g)]

        def sum_keys(name, todo):
            return [key for s in todo for key in named(name, s[2], s[3], s[0], s[1])]

        def turn(i, g, where, opens):
            readers = [("grouped", r, g) for r in opens] if opens else None
            on_tensor(x_turn, (i, g, where), [("words", i, g)], [("turned", i, g)], where, readers)

        def slot(todo, by_vector=False):
            where = ring.pop(0)
            ring.append(where)
            on_tensor(z_bank, (where, todo), x_needs(todo, (0, 1)), sum_keys("sum", todo), where, sum_keys("piece", todo))
            if not by_vector:
                empty(todo)

        def empty(todo):
            for s in todo:
                scalar_jobs.append((piece_out, s, sum_keys("sum", [s]) + ["bias"], sum_keys("piece", [s])))

        def y_slot():
            r, n = tiles.pop(0)
            where = ring.pop(0)
            ring.append(where)
            on_tensor(y_mul, (r, n, where), [("h", r, 0), ("h", r, 1)], [("y", r, n)], where, [("stored", r, n)])
            pending.append((r, n))

        def cast(i, g):
            scalar_jobs.append((x_cast, (i, g), [], [("words", i, g)]))

        def sort(i, passes):
            vector_jobs.append((x_sort, (i, passes), [], [("words", i, g) for g in passes]))

        def scale(i, rows, g):
            vector_jobs.append((x_out, (i, rows, g), named("turned", i * P, rows * P, g), named("grouped", i * P, rows * P, g)))

        def scale_by_planes(a, g):
            scalar_jobs.append((x_planes, (a, g), named("turned", a * PAIR, PAIR, g), named("grouped", a * PAIR, PAIR, g)))

        def regroup(a, g):
            vector_jobs.append((x_weave, (a, g), named("grouped", a * PAIR, PAIR, g), []))

        def quant(i, rows, g):
            vector_jobs.append((x_quant, (i, g), [], named("codes", i * P, rows * P, g)))

        def max_1(T, first, n):
            vector_jobs.append((first_max, (T, first, n), named("piece", first, n, 0, T) + named("piece", first, n, 1, T), []))

        def max_2(T, first, n):
            vector_jobs.append((second_max, (T, first, n), named("piece", first, n, 2, T), named("fold", first, n, T)))

        def max_out(s, first, n):
            vector_jobs.append((last_max, (s, first, n), named("sum", first, n, 2, s[1]), named("piece", first, n, 2, s[1]) + named("fold", first, n, s[1])))

        def max_1_out(s):
            vector_jobs.append((first_out_max, (s,), sum_keys("sum", [s]) + named("piece", s[2], s[3], 0, s[1]), sum_keys("piece", [s])))

        def weave(first, n, g, jobs):
            needs = [key for T in range(GROUP * g, GROUP * (g + 1)) for key in named("fold", first, n, T)]
            copy = nc.vector.tensor_copy if jobs is vector_jobs else nc.scalar.copy
            jobs.append((h_weave, (first, n, g, copy), needs, named("woven", first, n, g)))

        def h_q(first, n, g):
            vector_jobs.append((h_quant, (first, g), named("woven", first, n, g), named("h", first, n, g)))

        def store(queue=nc.sync, halves=False):
            r, n = pending.pop(0)
            if halves:
                vector_jobs.append((y_out, (r, n, nc.scalar, 0, PAIR), [("y", r, n)], []))
                vector_jobs.append((y_out, (r, n, nc.sync, PAIR, BANK), [("y", r, n)], [("stored", r, n)]))
            else:
                vector_jobs.append((y_out, (r, n, queue, 0, BANK), [("y", r, n)], [("stored", r, n)]))

        def by_two(todo):
            return [todo[i : i + 2] for i in range(0, len(todo), 2)]

        tiles = [(r, n) for r in range(M // P) for n in range(2)]
        pending = []
        columns = [(col // TILES, col % TILES) for col in range(PIECES * TILES)]

        on_tensor(warm_up, (2,), [], [])
        on_tensor(warm_up_on_landing, (), [], [])
        for i, g in ((0, 0), (1, 0), (1, 1), (3, 1)):
            sort(i, [g])
        for i, g in ((0, 1), (2, 1), (2, 0), (3, 0)):
            cast(i, g)
        turn(0, 0, 6, [0])
        on_tensor(warm_up, (1,), [], [])
        turn(1, 0, 7, [1])
        on_tensor(warm_up, (1,), [], [])
        turn(0, 1, 4, [0, 1])
        turn(1, 1, 4, [])
        turn(3, 1, 3, [2, 3])
        turn(2, 1, 3, [])
        on_tensor(warm_up, (1,), [], [])
        turn(2, 0, 5, [2, 3])
        turn(3, 0, 5, [])
        for g in range(2):
            for i in (0, 1):
                scale(i, 1, g)
            for i in (0, 1):
                quant(i, 1, g)
        for g in (1, 0):
            scale_by_planes(1, g)
        regroup(1, 1)
        sort(4, [0, 1])
        quant(2, 2, 1)
        regroup(1, 0)
        sort(5, [0, 1])
        quant(2, 2, 0)
        early = by_two([(j, T, A, PAIR) for j, T in columns[:EARLY]])
        for where, todo in zip((6, 7, 0, 1, 2), early):
            on_tensor(z_first, (where, todo), x_needs(todo, (0,)), [], where, sum_keys("piece", todo))
        on_tensor(b_turn, (4,), [], ["b turned"], 4, ["bias"])
        scalar_jobs.append((b_out, (), ["b turned"], ["bias"]))
        for todo in early:
            on_tensor(z_second, (todo,), x_needs(todo, (1,)), sum_keys("sum", todo))
            empty(todo)
        ring = [3, 4, 5, 6, 7, 0, 1, 2]

        first_half = (
            by_two([(j, T, A, PAIR) for j, T in columns[EARLY:NARROW]])
            + by_two([(j, T, B, PAIR) for j, T in columns[:NARROW]])
            + [[(j, T, A, BANK)] for j, T in columns[NARROW:]]
        )
        lent = []
        for n, todo in enumerate(first_half):
            if n in (TURN_AFTER, TURN_AFTER + 3):
                a = 2 if n == TURN_AFTER else 3
                for g in range(2):
                    lent.append(ring.pop(0))
                    turn(2 * a, g, lent[-1], [2 * a, 2 * a + 1])
                    turn(2 * a + 1, g, lent[-1], [])
            slot(todo, todo[0][0] == 2 and todo[0][1] in OWN)
            if lent and (n - TURN_AFTER) % 2 == 0:
                ring.append(lent.pop(0))
        for i in range(6, 8):
            sort(i, [0, 1])
        vector_jobs.append((load_v, (), [], []))
        scale(4, 2, 0)
        scale(4, 2, 1)
        quant(4, 2, 0)
        scale(6, 2, 0)
        quant(4, 2, 1)
        scale(6, 2, 1)
        quant(6, 2, 0)
        max_1(0, A, BANK)
        quant(6, 2, 1)
        for T in range(TILES):
            if T + 1 < TILES:
                max_1(T + 1, A, BANK)
            if T in OWN:
                max_out((2, T, A, BANK), A, BANK)
            else:
                max_2(T, A, BANK)

        for T in range(WIDE):
            for j in range(PIECES):
                slot([(j, T, C, BANK)], j == 2 and T in ())
            if T < 4:
                weave((A, B)[T % 2], PAIR, T // 2, vector_jobs)
            max_1(T, C, BANK)
            if T < 4:
                h_q((A, B)[T % 2], PAIR, T // 2)
            if T in ():
                max_out((2, T, C, BANK), C, BANK)
            else:
                max_2(T, C, BANK)
        high = [(j, T) for T in range(WIDE, TILES) for j in range(PIECES)]
        third = by_two([(j, T, C, PAIR) for j, T in high])
        for n, todo in enumerate(third):
            slot(todo)
            if n in (1, 3):
                y_slot()
            if n in {}:
                weave(*{}[n], scalar_jobs)
        fourth = [(j, T, D, PAIR) for j, T in ((0, 4), (1, 4), (2, 4), (0, 5), (1, 5), (2, 5), (0, 6), (0, 7))]
        for n, todo in enumerate(by_two(fourth)):
            slot(todo)
            if n in (0, 1, 2):
                y_slot()
            if n in {}:
                weave(*{}[n], scalar_jobs)
        for first in (C, C + P):
            weave(first, P, 1, scalar_jobs)
        for j in (1, 2):
            for T in (6, 7):
                slot([(j, T, D, PAIR)], by_vector=True)
        max_1(4, C, PAIR)
        store()
        max_2(4, C, PAIR)
        max_1(5, C, PAIR)
        store()
        max_2(5, C, PAIR)
        max_1(6, C, PAIR)
        weave(C, PAIR, 0, vector_jobs)
        max_2(6, C, PAIR)
        max_1(7, C, PAIR)
        h_q(C, PAIR, 0)
        max_2(7, C, PAIR)
        weave(D, PAIR, 0, vector_jobs)
        store()
        max_1(4, D, PAIR)
        h_q(D, PAIR, 0)
        max_2(4, D, PAIR)
        store()
        max_1(5, D, PAIR)
        store()
        max_2(5, D, PAIR)
        max_1_out((1, 6, D, PAIR))
        max_1_out((1, 7, D, PAIR))
        max_out((2, 6, D, PAIR), D, PAIR)
        max_out((2, 7, D, PAIR), D, P)
        max_out((2, 7, D, PAIR), D + P, P)
        for first in (D, D + P):
            weave(first, P, 1, scalar_jobs)
        left = len(tiles)
        for n in range(left):
            y_slot()
            if n in (0, 0 + 1):
                h_q(C + (n - 0) * P, P, 1)
            if n == left - 6:
                h_q(D, P, 1)
            if n == left - 5:
                h_q(D + P, P, 1)
            store((nc.sync, nc.scalar)[n % 2] if n >= left - 5 else nc.sync, halves=(n == left - 1))


        given = set()
        queues = (tensor_jobs, scalar_jobs, vector_jobs)
        while any(queues):
            moved = False
            for jobs in queues:
                while jobs and all(key in given for key in jobs[0][2]):
                    job, args, needs, gives = jobs.pop(0)
                    job(*args)
                    for key in gives:
                        given.add(key)
                    moved = True
            assert moved
